import numpy as np
import ml_dtypes


def mxq(x, axis, fmt="e4m3"):
    dtype, down = {"e4m3": (ml_dtypes.float8_e4m3fn, 7), "e5m2": (ml_dtypes.float8_e5m2, 14)}[fmt]
    v = np.moveaxis(np.asarray(x, np.float32).astype(ml_dtypes.bfloat16).astype(np.float64), axis, -1)
    blocks = v.reshape(v.shape[:-1] + (-1, 32))
    amax = np.abs(blocks).max(-1, keepdims=True)
    byte = np.maximum(np.where(amax > 0, np.frexp(amax)[1] - 1 + 127, 0) - down, 1)
    scale = np.exp2(byte - 127.0)
    codes = (blocks / scale).astype(np.float32).astype(dtype).astype(np.float64)
    return np.moveaxis((codes * scale).reshape(v.shape), -1, axis)


WIDE = False


def mx_kscale(k):
    if not WIDE:
        return np.ones(k)
    levels = np.array([10, -10, 5, -5, 0])
    if k % 512:
        return np.exp2(np.random.permutation(np.resize(levels, k // 32))).repeat(32)
    a = np.empty((k // 512, 16))
    for p in range(k // 512):
        a[p, :8] = np.random.permutation(np.resize(levels, 8))
        for g in range(8):
            far = levels[np.abs(levels - a[p, g]) >= 10]
            a[p, g + 8] = far[np.random.randint(len(far))]
    return np.exp2(a.ravel()).repeat(32)


def f64(x):
    return np.asarray(x).astype(np.float64)


def striped(idx):
    return np.tile(idx.reshape(-1, 16).T, (8, 1)).astype(np.uint16)


def unstriped(offs):
    return offs[:16].T.reshape(-1).astype(np.int64)


E2M1 = np.array([0.0, 0.5, 1.0, 1.5, 2.0, 3.0, 4.0, 6.0, -0.0, -0.5, -1.0, -1.5, -2.0, -3.0, -4.0, -6.0])


def pack_weight(w, fmt):
    k, n = w.shape
    w = f64(np.asarray(w, np.float32).astype(ml_dtypes.bfloat16)).reshape(k // 32, 32, n)
    amax = np.abs(w).max(1)
    if fmt == "e4m3":
        byte = np.frexp(amax)[1] - 1 + 127 - 7
    else:
        mant, ex = np.frexp(amax / 6.0)
        byte = np.where(mant > 0.5, ex, ex - 1) + 127
    byte = np.clip(np.where(amax > 0, byte, 1), 1, 254)
    scaled = (w * np.exp2(127.0 - byte)[:, None, :]).reshape(k, n).astype(np.float32)
    by_word = np.ascontiguousarray(scaled.reshape(k // 512, 128, 4, n).transpose(0, 1, 3, 2))
    if fmt == "e4m3":
        words = by_word.astype(ml_dtypes.float8_e4m3fn).view(np.uint8)
    else:
        c = by_word.astype(ml_dtypes.float4_e2m1fn).view(np.uint8) & 0xF
        words = (c[..., 0::2] | (c[..., 1::2] << 4)).reshape(k // 512, 128, 2 * n)
    return np.ascontiguousarray(words), np.ascontiguousarray(byte.astype(np.uint8).reshape(k // 512, 16, n))


def unpack_weight(words, scales, fmt):
    g, _, n = scales.shape
    words = np.ascontiguousarray(words).reshape(g, 128, n, -1)
    if fmt == "e4m3":
        vals = words.view(ml_dtypes.float8_e4m3fn).astype(np.float64)
    else:
        nib = np.empty((g, 128, n, 4), np.uint8)
        nib[..., 0::2] = words & 0xF
        nib[..., 1::2] = words >> 4
        vals = E2M1[nib]
    vals = vals * np.repeat(np.exp2(scales.astype(np.float64) - 127.0), 8, axis=1)[..., None]
    return vals.transpose(0, 1, 3, 2).reshape(g * 512, n)


def gelu(v):
    return 0.5 * v * (1.0 + np.tanh(np.sqrt(2.0 / np.pi) * (v + 0.044715 * v**3)))


def striped8(idx):
    return np.concatenate([v.reshape(-1, 16).T for v in idx]).astype(np.uint16)


def unstriped8(offs):
    return np.stack([offs[16 * g:16 * g + 16].T.reshape(-1) for g in range(8)]).astype(np.int64)


def put_heads(h, wgs, idx8, t2):
    r = np.arange(h.shape[0])
    page = np.zeros((h.shape[0], t2))
    page[r[:, None], idx8[r % 512 // 64]] = wgs[r // 4 % 128] * h
    return page


K, T, S, H, T2, N = 1024, 2048, 512, 1024, 1024, 768

def setup_inputs():
    n = np.random.standard_normal
    s = mx_kscale(K)[:, None]
    u = mx_kscale(H)[:, None]
    tab_words, tab_scales = pack_weight(n((K, T)) * s, "e4m3")
    wa_words, wa_scales = pack_weight(n((H, N)) / np.sqrt(H) / u, "e2m1")
    places = np.stack([np.random.permutation(T2)[:S] for _ in range(8)])
    return {
        "tab_words": tab_words, "tab_scales": tab_scales,
        "offs": striped(np.random.permutation(T)[:S]),
        "w1": (n((K, H)) / np.sqrt(K) / s * u.T).astype(np.float32),
        "wgs": np.repeat(np.random.uniform(0.5, 2.0, (8, S)), 16, axis=0).astype(np.float32),
        "offs2": striped8(places),
        "prior": (n((H, T2)) * u).astype(np.float32),
        "wa_words": wa_words, "wa_scales": wa_scales,
        "wb": (0.8 * n((H, N)) / np.sqrt(H) / u).astype(np.float32),
    }

def reference(tab_words, tab_scales, offs, w1, wgs, offs2, prior, wa_words, wa_scales, wb):
    v = unpack_weight(tab_words, tab_scales, "e4m3")[:, unstriped(offs)]
    h = mxq(f64(w1), 0, "e4m3").T @ v
    page = put_heads(h, f64(wgs), unstriped8(offs2), T2)
    z = mxq(page + f64(prior), 0, "e4m3")
    spend = unpack_weight(wa_words, wa_scales, "e2m1").T @ z
    load = mxq(f64(wb), 0, "e4m3").T @ z
    return spend / (1.0 + load * load)

@@ -1,0 +1,327 @@
+from contextlib import ExitStack
+
+import concourse.mybir as mybir
+from concourse.masks import make_identity
+
+K, T, S, H, T2, N = 1024, 2048, 512, 1024, 1024, 768
+FLOPS = 2 * K * H * S + 2 * 2 * H * N * T2
+
+F32 = mybir.dt.float32
+BF16 = mybir.dt.bfloat16
+I32 = mybir.dt.int32
+U32 = mybir.dt.uint32
+U16 = mybir.dt.uint16
+U8 = mybir.dt.uint8
+FP8X4 = mybir.dt.float8_e4m3fn_x4
+FP4X4 = mybir.dt.float4_e2m1fn_x4
+MULT = mybir.AluOpType.mult
+ACT = mybir.ActivationFunctionType
+
+P = 128
+PACK = 4
+KP = P * PACK
+BANK = 512
+WB_PIECE = 256
+PAGES = 3
+
+
+def tile_list_listing_budget_pacer_kernel(
+    tc, tab_words, tab_scales, offs, w1, wgs, offs2, prior, wa_words, wa_scales, wb, out
+):
+    nc = tc.nc
+    with ExitStack() as ctx:
+        held = ctx.enter_context(tc.tile_pool(name="held", bufs=1))
+        ring = ctx.enter_context(tc.tile_pool(name="ring", bufs=4))
+        psum = ctx.enter_context(tc.psum_pool(name="psum", bufs=1))
+
+        def keep(name, shape, dtype, after=None):
+            return held.tile(shape, dtype, name=name, tag=after or name, align_bytes=64)
+
+        def bank(i):
+            return psum.tile([P, BANK], F32, name="bank%d" % i)
+
+        idx = held.tile([P, S // 16], U16, name="idx")
+        idx2 = held.tile([P, S // 16], U16, name="idx2")
+        ident = keep("ident", [P, P], F32)
+        tab_w = [keep("tab_w%d" % a, [P, T], I32) for a in range(2)]
+        tab_s = keep("tab_s", [P, T // 4], I32)
+        wa_s = keep("wa_s", [P, 2, N // 4], I32)
+        wa_w = [keep("wa_w%d" % a, [P, 2 * N // 4], I32) for a in range(2)]
+        wgs_sb = keep("wgs_sb", [P, S], F32)
+        pages = [keep("page%d" % e, [P, T2], F32) for e in range(PAGES)]
+        prior_sb = [keep("prior%d" % s, [P, T2], F32) for s in range(8)]
+        wb_raw = [keep("wb_raw%d" % a, [P, PACK, N], F32) for a in range(2)]
+
+        nc.gpsimd.memset(tab_s[:], 0)
+        for q in range(4):
+            nc.gpsimd.dma_start(
+                tab_s[32 * q : 32 * q + 8, :], tab_scales[:, 4 * q : 4 * q + 4, :].bitcast(I32)
+            )
+        nc.vector.memset(wa_s[:], 0)
+        for q in range(4):
+            nc.gpsimd.dma_start(
+                wa_s[32 * q : 32 * q + 4, :, :],
+                wa_scales[:, 4 * q : 4 * q + 4, :].bitcast(I32).rearrange("a r c -> r a c"),
+            )
+        make_identity(nc, ident[:])
+        for page in pages:
+            nc.vector.memset(page[:], 0.0)
+        warm = keep("warm", [P, 1], F32)
+        nc.scalar.activation(warm[:], pages[0][:, 0:1], ACT.Abs_reciprocal_sqrt, bias=1.0)
+
+        w1_raw = {}
+
+        def load_w1(a, b):
+            raw = ring.tile([P, PACK, KP], F32, name="wide")
+            rows = w1[KP * a : KP * (a + 1), KP * b : KP * (b + 1)]
+            nc.sync.dma_start(raw[:], rows.rearrange("(p j) c -> p j c", j=PACK))
+            w1_raw[a, b] = raw
+
+        def load_prior(s):
+            b, i = divmod(s, PACK)
+            rows = prior[KP * b : KP * (b + 1), :].rearrange("(p i) m -> p i m", i=PACK)
+            nc.sync.dma_start(prior_sb[s][:], rows[:, i, :])
+
+        def load_wb(a):
+            rows = wb[KP * a : KP * (a + 1), :]
+            nc.sync.dma_start(wb_raw[a][:], rows.rearrange("(p j) c -> p j c", j=PACK))
+
+        load_w1(0, 0)
+        nc.sync.dma_start(idx[:], offs)
+        load_w1(1, 0)
+        for a in range(2):
+            nc.sync.dma_start(tab_w[a][:], tab_words[a].rearrange("p t i -> p (t i)").bitcast(I32))
+        nc.sync.dma_start(wgs_sb[:], wgs)
+        nc.sync.dma_start(idx2[:], offs2)
+        load_w1(0, 1)
+        load_w1(1, 1)
+        load_wb(0)
+        for s in range(4):
+            load_prior(s)
+        load_wb(1)
+        for s in range(4, 6):
+            load_prior(s)
+        for a in range(2):
+            nc.sync.dma_start(wa_w[a][:], wa_words[a].bitcast(I32))
+        for s in range(6, 8):
+            load_prior(s)
+
+        w1_c, w1_s = {}, {}
+
+        def quantise_w1(a, b, after=None):
+            stage = keep("w1_stage%d%d" % (a, b), [P, PACK * KP], BF16, after=after)
+            nc.scalar.copy(
+                stage[:].rearrange("p (t m j) -> p m j t", t=PACK, j=PACK),
+                w1_raw[a, b][:].rearrange("p j (m t) -> p m j t", t=PACK),
+            )
+            w1_c[a, b] = keep("w1_c%d%d" % (a, b), [P, KP], U32)
+            w1_s[a, b] = keep("w1_s%d%d" % (a, b), [P, KP], U8)
+            nc.vector.quantize_mx(w1_c[a, b][:].bitcast(FP8X4), w1_s[a, b][:], stage[:])
+
+        wb_c = [keep("wb_c%d" % a, [P, N], U32) for a in range(2)]
+        wb_s = {}
+        wb_stage = {}
+
+        def round_wb(a, piece, after):
+            c0 = piece * WB_PIECE
+            stage = keep("wb_stage%d_%d" % (a, c0), [P, PACK * WB_PIECE], BF16, after=after)
+            wb_stage[a, c0] = stage
+            nc.scalar.copy(
+                stage[:].rearrange("p (c i j) -> p c j i", i=4, j=PACK),
+                wb_raw[a][:, :, c0 : c0 + WB_PIECE].rearrange("p j (c i) -> p c j i", i=4),
+            )
+
+        def quantise_wb(a, after):
+            wb_s[a] = keep("wb_s%d" % a, [P, N], U8, after=after)
+            for c0 in range(0, N, WB_PIECE):
+                cols = slice(c0, c0 + WB_PIECE)
+                nc.vector.quantize_mx(wb_c[a][:, cols].bitcast(FP8X4), wb_s[a][:, cols], wb_stage[a, c0][:])
+
+        v_w = {}
+
+        h_banks = (0, 1, 6, 7)
+        h_sb = {}
+        h_ps = {}
+
+        def make_h(s, which, entries):
+            b, i = divmod(s, PACK)
+            cols = slice(P * i, P * (i + 1))
+            acc = bank(which)
+            for a in range(2):
+                nc.tensor.matmul_mx(
+                    acc[:, entries],
+                    lhsT=w1_c[a, b][:, cols].bitcast(FP8X4),
+                    lhsT_scale=w1_s[a, b][:, cols],
+                    rhs=v_w[a][:, entries].bitcast(FP8X4),
+                    rhs_scale=v_s[4 * a : P, entries],
+                    start=(a == 0),
+                    stop=(a == 1),
+                )
+            h_ps[s, entries.start] = acc
+
+        def fetch_h(s, entries, after=None):
+            if entries.start == 0:
+                h_sb[s] = keep("h%d" % s, [P, S], F32, after=after)
+            nc.scalar.copy(h_sb[s][:, entries], h_ps[s, entries.start][:, entries])
+
+        sums = {}
+        z_t = {}
+
+        def turn(acc, l, e, src, mb, start, stop):
+            region = slice(P * (2 * l + e), P * (2 * l + e + 1))
+            nc.tensor.matmul(
+                acc[:, region],
+                lhsT=src[:, P * mb : P * (mb + 1)],
+                rhs=ident[:],
+                is_transpose=True,
+                start=start,
+                stop=stop,
+            )
+
+        def place(s, entries):
+            offsets = idx2[:, entries.start // 16 : entries.stop // 16]
+            nc.vector.tensor_tensor(
+                pages[s % PAGES][:].indirect(offsets), h_sb[s][:, entries], wgs_sb[:, entries], MULT
+            )
+
+        def add_prior(s):
+            b, i = divmod(s, PACK)
+            u, e = divmod(i, 2)
+            if e == 0:
+                for k in range(4):
+                    sums[k] = bank(2 + k)
+            page = pages[s % PAGES]
+            order = (page, prior_sb[s]) if e == 0 else (prior_sb[s], page)
+            for k in range(4):
+                for l in range(2):
+                    turn(sums[k], l, e, order[0], 2 * k + l, e == 0 and l == 0, False)
+            for k in range(4):
+                for l in range(2):
+                    turn(sums[k], l, e, order[1], 2 * k + l, False, e == 1 and l == 1)
+                if e == 1:
+                    z_t[u, k] = keep("z_t%d%d%d" % (b, u, k), [P, BANK], BF16)
+                    copy = nc.vector.tensor_copy if s == 7 and k == 1 else nc.scalar.copy
+                    copy(
+                        z_t[u, k][:].rearrange("m (l p e) -> m l p e", l=2, e=2),
+                        sums[k][:].rearrange("m (l e p) -> m l p e", l=2, e=2),
+                    )
+
+        z_c = {(b, hf): keep("z_c%d%d" % (b, hf), [P, BANK], U32) for b in range(2) for hf in range(2)}
+        z_s = {}
+        z_in = {}
+
+        def turn_back(b):
+            for k in range(4):
+                back = bank(2 + k)
+                for u in range(2):
+                    words = z_t[u, k][:].bitcast(F32)
+                    for l in range(2):
+                        nc.tensor.transpose(
+                            back[:, P * (2 * u + l) : P * (2 * u + l + 1)],
+                            words[:, P * l : P * (l + 1)],
+                            ident[:],
+                        )
+                z_in[k] = ring.tile([P, 2 * BANK], BF16, name="z_in", align_bytes=64)
+                copy = nc.vector.tensor_copy if b == 1 and k in (0, 3) else nc.scalar.copy
+                copy(
+                    z_in[k][:].bitcast(F32).rearrange("p (m u) -> p m u", u=2),
+                    back[:].rearrange("p (u m) -> p m u", u=2),
+                )
+
+        def quantise_z(b, after=None):
+            z_s[b] = keep("z_s%d" % b, [P, T2], U8, after=after)
+            for k in range(4):
+                hf, part = divmod(k, 2)
+                cols = slice(256 * part, 256 * (part + 1))
+                nc.vector.quantize_mx(
+                    z_c[b, hf][:, cols].bitcast(FP8X4), z_s[b][:, 256 * k : 256 * (k + 1)], z_in[k][:]
+                )
+
+        unit_banks = ((0, 1), (6, 7), (2, 3), (4, 5))
+
+        def finish(unit):
+            hf, nt = divmod(unit, N // P)
+            cols = slice(P * nt, P * (nt + 1))
+            spend = bank(unit_banks[unit % 4][0])
+            load = bank(unit_banks[unit % 4][1])
+            for b in range(2):
+                nc.tensor.matmul_mx(
+                    load[:],
+                    lhsT=wb_c[b][:, cols].bitcast(FP8X4),
+                    lhsT_scale=wb_s[b][:, cols],
+                    rhs=z_c[b, hf][:].bitcast(FP8X4),
+                    rhs_scale=z_s[b][:, BANK * hf : BANK * (hf + 1)],
+                    start=(b == 0),
+                    stop=(b == 1),
+                )
+                nc.tensor.matmul_mx(
+                    spend[:],
+                    lhsT=wa_w[b][:].bitcast(U8)[:, 2 * P * nt : 2 * P * (nt + 1)].bitcast(FP4X4),
+                    lhsT_scale=wa_s[:, b, :].bitcast(U8)[:, cols],
+                    rhs=z_c[b, hf][:].bitcast(FP8X4),
+                    rhs_scale=z_s[b][:, BANK * hf : BANK * (hf + 1)],
+                    start=(b == 0),
+                    stop=(b == 1),
+                )
+            work = ring.tile([P, 3, BANK], F32, name="wide")
+            nc.scalar.activation(work[:, 0, :], load[:], ACT.Square)
+            nc.scalar.activation(work[:, 1, :], work[:, 0, :], ACT.Abs_reciprocal_sqrt, bias=1.0)
+            nc.vector.tensor_tensor(work[:, 2, :], spend[:], work[:, 1, :], MULT)
+            res = keep("res%d" % unit, [P, BANK], F32, after="prior%d" % (unit % 8))
+            nc.vector.tensor_tensor(res[:], work[:, 2, :], work[:, 1, :], MULT)
+            nc.sync.dma_start(out[cols, BANK * hf : BANK * (hf + 1)], res[:])
+
+        quantise_w1(0, 0)
+        quantise_w1(1, 0)
+        v_s = keep("v_s", [P, S], U8, after="w1_stage00")
+        nc.vector.tensor_copy(v_s[:], tab_s[:].bitcast(U8).indirect(idx[:]))
+        whole = slice(0, S)
+        halves = (slice(0, S // 2), slice(S // 2, S))
+        v_w[0] = keep("v_w0", [P, S], U32, after="tab_s")
+        nc.vector.tensor_copy(v_w[0][:], tab_w[0][:].bitcast(U32).indirect(idx[:]))
+        v_w[1] = keep("v_w1", [P, S], U32, after="w1_stage10")
+        for half in halves:
+            offsets = idx[:, half.start // 16 : half.stop // 16]
+            nc.vector.tensor_copy(v_w[1][:, half], tab_w[1][:].bitcast(U32).indirect(offsets))
+        for half, which in zip(halves, (0, 2)):
+            make_h(0, which, half)
+            fetch_h(0, half)
+            place(0, half)
+        for s in (1, 2, 3):
+            make_h(s, h_banks[s], whole)
+        fetch_h(1, whole)
+        add_prior(0)
+        place(1, whole)
+        quantise_w1(0, 1, after="w1_c00")
+        quantise_w1(1, 1, after="w1_c10")
+        round_wb(0, 0, "w1_s00")
+        fetch_h(2, whole, after="w1_c00")
+        fetch_h(3, whole, after="w1_c10")
+        add_prior(1)
+        for s in range(4, 8):
+            make_h(s, h_banks[s % PACK], whole)
+            fetch_h(s, whole)
+        place(2, whole)
+        add_prior(2)
+        round_wb(0, 1, "w1_c01")
+        round_wb(0, 2, "w1_c11")
+        place(3, whole)
+        add_prior(3)
+        turn_back(0)
+        place(4, whole)
+        add_prior(4)
+        quantise_wb(0, after="h4")
+        for piece, tag in enumerate(("z_t013", "z_t003", "z_t012")):
+            round_wb(1, piece, tag)
+        place(5, whole)
+        add_prior(5)
+        place(6, whole)
+        add_prior(6)
+        quantise_z(0, after="h5")
+        quantise_wb(1, after="h6")
+        place(7, whole)
+        add_prior(7)
+        turn_back(1)
+        quantise_z(1)
+        for unit in range(2 * N // P):
+            finish(unit)

@@ -15,6 +15,7 @@ U8 = mybir.dt.uint8
 FP8X4 = mybir.dt.float8_e4m3fn_x4
 FP4X4 = mybir.dt.float4_e2m1fn_x4
 MULT = mybir.AluOpType.mult
+ADD = mybir.AluOpType.add
 ACT = mybir.ActivationFunctionType
 
 P = 128
@@ -23,6 +24,10 @@ KP = P * PACK
 BANK = 512
 WB_PIECE = 256
 PAGES = 3
+WORK_TAGS = ("w1_raw00", "w1_raw10", "w1_raw01", "w1_raw11", "wb_raw0", "wb_raw1", "spare0", "spare1")
+QUARTER = T2 // 4
+UNITS = 2 * N // P
+SQUARED_ON_SCALAR = 2
 
 
 def tile_list_listing_budget_pacer_kernel(
@@ -31,7 +36,6 @@ def tile_list_listing_budget_pacer_kernel(
     nc = tc.nc
     with ExitStack() as ctx:
         held = ctx.enter_context(tc.tile_pool(name="held", bufs=1))
-        ring = ctx.enter_context(tc.tile_pool(name="ring", bufs=4))
         psum = ctx.enter_context(tc.psum_pool(name="psum", bufs=1))
 
         def keep(name, shape, dtype, after=None):
@@ -52,27 +56,22 @@ def tile_list_listing_budget_pacer_kernel(
         prior_sb = [keep("prior%d" % s, [P, T2], F32) for s in range(8)]
         wb_raw = [keep("wb_raw%d" % a, [P, PACK, N], F32) for a in range(2)]
 
-        nc.gpsimd.memset(tab_s[:], 0)
+        nc.vector.memset(tab_s[:], 0)
+        nc.vector.memset(wa_s[:], 0)
         for q in range(4):
             nc.gpsimd.dma_start(
                 tab_s[32 * q : 32 * q + 8, :], tab_scales[:, 4 * q : 4 * q + 4, :].bitcast(I32)
             )
-        nc.vector.memset(wa_s[:], 0)
-        for q in range(4):
-            nc.gpsimd.dma_start(
-                wa_s[32 * q : 32 * q + 4, :, :],
-                wa_scales[:, 4 * q : 4 * q + 4, :].bitcast(I32).rearrange("a r c -> r a c"),
-            )
-        make_identity(nc, ident[:])
         for page in pages:
-            nc.vector.memset(page[:], 0.0)
+            nc.gpsimd.memset(page[:], 0.0)
+        make_identity(nc, ident[:])
         warm = keep("warm", [P, 1], F32)
         nc.scalar.activation(warm[:], pages[0][:, 0:1], ACT.Abs_reciprocal_sqrt, bias=1.0)
 
         w1_raw = {}
 
         def load_w1(a, b):
-            raw = ring.tile([P, PACK, KP], F32, name="wide")
+            raw = keep("w1_raw%d%d" % (a, b), [P, PACK, KP], F32)
             rows = w1[KP * a : KP * (a + 1), KP * b : KP * (b + 1)]
             nc.sync.dma_start(raw[:], rows.rearrange("(p j) c -> p j c", j=PACK))
             w1_raw[a, b] = raw
@@ -95,27 +94,33 @@ def tile_list_listing_budget_pacer_kernel(
         nc.sync.dma_start(idx2[:], offs2)
         load_w1(0, 1)
         load_w1(1, 1)
+        load_prior(0)
+        load_prior(1)
         load_wb(0)
-        for s in range(4):
-            load_prior(s)
+        load_prior(2)
+        load_prior(3)
         load_wb(1)
-        for s in range(4, 6):
+        for s in range(4, 7):
             load_prior(s)
+        for q in range(4):
+            nc.sync.dma_start(
+                wa_s[32 * q : 32 * q + 4, :, :],
+                wa_scales[:, 4 * q : 4 * q + 4, :].bitcast(I32).rearrange("a r c -> r a c"),
+            )
         for a in range(2):
             nc.sync.dma_start(wa_w[a][:], wa_words[a].bitcast(I32))
-        for s in range(6, 8):
-            load_prior(s)
+        load_prior(7)
 
         w1_c, w1_s = {}, {}
 
-        def quantise_w1(a, b, after=None):
+        def quantise_w1(a, b, after=None, scales_after=None):
             stage = keep("w1_stage%d%d" % (a, b), [P, PACK * KP], BF16, after=after)
             nc.scalar.copy(
                 stage[:].rearrange("p (t m j) -> p m j t", t=PACK, j=PACK),
                 w1_raw[a, b][:].rearrange("p j (m t) -> p m j t", t=PACK),
             )
             w1_c[a, b] = keep("w1_c%d%d" % (a, b), [P, KP], U32)
-            w1_s[a, b] = keep("w1_s%d%d" % (a, b), [P, KP], U8)
+            w1_s[a, b] = keep("w1_s%d%d" % (a, b), [P, KP], U8, after=scales_after)
             nc.vector.quantize_mx(w1_c[a, b][:].bitcast(FP8X4), w1_s[a, b][:], stage[:])
 
         wb_c = [keep("wb_c%d" % a, [P, N], U32) for a in range(2)]
@@ -143,19 +148,19 @@ def tile_list_listing_budget_pacer_kernel(
         h_sb = {}
         h_ps = {}
 
-        def make_h(s, which, entries):
+        def make_h(s, which, entries, passes):
             b, i = divmod(s, PACK)
             cols = slice(P * i, P * (i + 1))
             acc = bank(which)
-            for a in range(2):
+            for a in passes:
                 nc.tensor.matmul_mx(
                     acc[:, entries],
                     lhsT=w1_c[a, b][:, cols].bitcast(FP8X4),
                     lhsT_scale=w1_s[a, b][:, cols],
                     rhs=v_w[a][:, entries].bitcast(FP8X4),
                     rhs_scale=v_s[4 * a : P, entries],
-                    start=(a == 0),
-                    stop=(a == 1),
+                    start=(a == passes[0]),
+                    stop=(a == passes[1]),
                 )
             h_ps[s, entries.start] = acc
 
@@ -184,25 +189,21 @@ def tile_list_listing_budget_pacer_kernel(
                 pages[s % PAGES][:].indirect(offsets), h_sb[s][:, entries], wgs_sb[:, entries], MULT
             )
 
-        def add_prior(s):
+        def open_sums():
+            for k in range(4):
+                sums[k] = bank(2 + k)
+
+        def add_rows(s, src, first=False, last=False, after=None):
             b, i = divmod(s, PACK)
-            u, e = divmod(i, 2)
-            if e == 0:
-                for k in range(4):
-                    sums[k] = bank(2 + k)
-            page = pages[s % PAGES]
-            order = (page, prior_sb[s]) if e == 0 else (prior_sb[s], page)
+            u = i // 2
+            if last:
+                z_t[u] = keep("z_t%d%d" % (b, u), [P, 4 * BANK], BF16, after=after)
             for k in range(4):
                 for l in range(2):
-                    turn(sums[k], l, e, order[0], 2 * k + l, e == 0 and l == 0, False)
-            for k in range(4):
-                for l in range(2):
-                    turn(sums[k], l, e, order[1], 2 * k + l, False, e == 1 and l == 1)
-                if e == 1:
-                    z_t[u, k] = keep("z_t%d%d%d" % (b, u, k), [P, BANK], BF16)
-                    copy = nc.vector.tensor_copy if s == 7 and k == 1 else nc.scalar.copy
-                    copy(
-                        z_t[u, k][:].rearrange("m (l p e) -> m l p e", l=2, e=2),
+                    turn(sums[k], l, s % 2, src, 2 * k + l, first and l == 0, last and l == 1)
+                if last:
+                    nc.scalar.copy(
+                        z_t[u][:, BANK * k : BANK * (k + 1)].rearrange("m (l p e) -> m l p e", l=2, e=2),
                         sums[k][:].rearrange("m (l e p) -> m l p e", l=2, e=2),
                     )
 
@@ -210,40 +211,67 @@ def tile_list_listing_budget_pacer_kernel(
         z_s = {}
         z_in = {}
 
-        def turn_back(b):
+        def turn_back_first():
             for k in range(4):
                 back = bank(2 + k)
                 for u in range(2):
-                    words = z_t[u, k][:].bitcast(F32)
+                    words = z_t[u][:].bitcast(F32)
                     for l in range(2):
                         nc.tensor.transpose(
                             back[:, P * (2 * u + l) : P * (2 * u + l + 1)],
-                            words[:, P * l : P * (l + 1)],
+                            words[:, P * (2 * k + l) : P * (2 * k + l + 1)],
                             ident[:],
                         )
-                z_in[k] = ring.tile([P, 2 * BANK], BF16, name="z_in", align_bytes=64)
-                copy = nc.vector.tensor_copy if b == 1 and k in (0, 3) else nc.scalar.copy
-                copy(
+                z_in[k] = keep("z_in%d" % k, [P, PACK * QUARTER], BF16)
+                nc.scalar.copy(
                     z_in[k][:].bitcast(F32).rearrange("p (m u) -> p m u", u=2),
                     back[:].rearrange("p (u m) -> p m u", u=2),
                 )
 
-        def quantise_z(b, after=None):
-            z_s[b] = keep("z_s%d" % b, [P, T2], U8, after=after)
-            for k in range(4):
-                hf, part = divmod(k, 2)
-                cols = slice(256 * part, 256 * (part + 1))
-                nc.vector.quantize_mx(
-                    z_c[b, hf][:, cols].bitcast(FP8X4), z_s[b][:, 256 * k : 256 * (k + 1)], z_in[k][:]
+        def quantise_z(b, k):
+            hf, part = divmod(k, 2)
+            cols = slice(QUARTER * part, QUARTER * (part + 1))
+            nc.vector.quantize_mx(
+                z_c[b, hf][:, cols].bitcast(FP8X4), z_s[b][:, QUARTER * k : QUARTER * (k + 1)], z_in[k][:]
+            )
+
+        rows = {}
+
+        def turn_back_second():
+            for hf in range(2):
+                back = bank(2 + 2 * hf)
+                for mb in range(4):
+                    words = z_t[0][:].bitcast(F32)[:, P * (4 * hf + mb) : P * (4 * hf + mb + 1)]
+                    nc.tensor.transpose(back[:, P * mb : P * (mb + 1)], words, ident[:])
+                nc.scalar.copy(
+                    rows[hf][:, :, 0:2, :], back[:].bitcast(BF16).rearrange("p (q m e) -> p q e m", q=2, e=2)
                 )
 
-        unit_banks = ((0, 1), (6, 7), (2, 3), (4, 5))
+        def add_direct(s, hf, parts):
+            cols = slice(BANK * hf + QUARTER * parts.start, BANK * hf + QUARTER * parts.stop)
+            nc.vector.tensor_tensor(
+                rows[hf][:, parts, s % PACK, :],
+                pages[s % PAGES][:, cols].rearrange("p (q m) -> p q m", m=QUARTER),
+                prior_sb[s][:, cols].rearrange("p (q m) -> p q m", m=QUARTER),
+                ADD,
+            )
 
-        def finish(unit):
+        def weave(k):
+            hf, part = divmod(k, 2)
+            z_in[k] = keep("woven%d" % k, [P, PACK * QUARTER], BF16, after="z_in%d" % (1 if k == 2 else k))
+            copy = nc.scalar.copy if part else nc.vector.tensor_copy
+            copy(
+                z_in[k][:].rearrange("p (m t) -> p m t", t=PACK),
+                rows[hf][:, part, :, :].rearrange("p t m -> p m t"),
+            )
+
+        unit_banks = ((0, 1), (6, 7), (3, 5), (2, 4))
+        damp = {}
+
+        def contention(unit):
             hf, nt = divmod(unit, N // P)
             cols = slice(P * nt, P * (nt + 1))
-            spend = bank(unit_banks[unit % 4][0])
-            load = bank(unit_banks[unit % 4][1])
+            load = bank(unit_banks[unit % 4][0])
             for b in range(2):
                 nc.tensor.matmul_mx(
                     load[:],
@@ -254,6 +282,15 @@ def tile_list_listing_budget_pacer_kernel(
                     start=(b == 0),
                     stop=(b == 1),
                 )
+            work = keep("work%d" % unit, [P, 3, BANK], F32, after=WORK_TAGS[unit % len(WORK_TAGS)])
+            nc.scalar.activation(work[:, 0, :], load[:], ACT.Square)
+            damp[unit] = work
+
+        def finish(unit):
+            hf, nt = divmod(unit, N // P)
+            cols = slice(P * nt, P * (nt + 1))
+            spend = bank(unit_banks[unit % 4][1])
+            for b in range(2):
                 nc.tensor.matmul_mx(
                     spend[:],
                     lhsT=wa_w[b][:].bitcast(U8)[:, 2 * P * nt : 2 * P * (nt + 1)].bitcast(FP4X4),
@@ -263,65 +300,91 @@ def tile_list_listing_budget_pacer_kernel(
                     start=(b == 0),
                     stop=(b == 1),
                 )
-            work = ring.tile([P, 3, BANK], F32, name="wide")
-            nc.scalar.activation(work[:, 0, :], load[:], ACT.Square)
+            work = damp[unit]
             nc.scalar.activation(work[:, 1, :], work[:, 0, :], ACT.Abs_reciprocal_sqrt, bias=1.0)
-            nc.vector.tensor_tensor(work[:, 2, :], spend[:], work[:, 1, :], MULT)
             res = keep("res%d" % unit, [P, BANK], F32, after="prior%d" % (unit % 8))
-            nc.vector.tensor_tensor(res[:], work[:, 2, :], work[:, 1, :], MULT)
+            if unit < UNITS - SQUARED_ON_SCALAR:
+                nc.vector.tensor_tensor(work[:, 2, :], spend[:], work[:, 1, :], MULT)
+                nc.vector.tensor_tensor(res[:], work[:, 2, :], work[:, 1, :], MULT)
+            else:
+                nc.scalar.activation(work[:, 2, :], work[:, 1, :], ACT.Square)
+                nc.vector.tensor_tensor(res[:], spend[:], work[:, 2, :], MULT)
             nc.sync.dma_start(out[cols, BANK * hf : BANK * (hf + 1)], res[:])
 
-        quantise_w1(0, 0)
-        quantise_w1(1, 0)
-        v_s = keep("v_s", [P, S], U8, after="w1_stage00")
-        nc.vector.tensor_copy(v_s[:], tab_s[:].bitcast(U8).indirect(idx[:]))
         whole = slice(0, S)
         halves = (slice(0, S // 2), slice(S // 2, S))
-        v_w[0] = keep("v_w0", [P, S], U32, after="tab_s")
+        v_s = keep("v_s", [P, S], U8)
+        nc.vector.tensor_copy(v_s[:], tab_s[:].bitcast(U8).indirect(idx[:]))
+        quantise_w1(0, 0)
+        v_w[0] = keep("v_w0", [P, S], U32, after="w1_stage00")
         nc.vector.tensor_copy(v_w[0][:], tab_w[0][:].bitcast(U32).indirect(idx[:]))
+        quantise_w1(1, 0, scales_after="tab_w0")
         v_w[1] = keep("v_w1", [P, S], U32, after="w1_stage10")
         for half in halves:
             offsets = idx[:, half.start // 16 : half.stop // 16]
             nc.vector.tensor_copy(v_w[1][:, half], tab_w[1][:].bitcast(U32).indirect(offsets))
         for half, which in zip(halves, (0, 2)):
-            make_h(0, which, half)
+            make_h(0, which, half, (0, 1))
             fetch_h(0, half)
             place(0, half)
         for s in (1, 2, 3):
-            make_h(s, h_banks[s], whole)
+            make_h(s, h_banks[s], whole, (1, 0))
         fetch_h(1, whole)
-        add_prior(0)
+        open_sums()
+        add_rows(0, pages[0], first=True)
+        add_rows(0, prior_sb[0])
         place(1, whole)
-        quantise_w1(0, 1, after="w1_c00")
+        quantise_w1(0, 1)
         quantise_w1(1, 1, after="w1_c10")
-        round_wb(0, 0, "w1_s00")
-        fetch_h(2, whole, after="w1_c00")
+        fetch_h(2, whole, after="w1_raw11")
         fetch_h(3, whole, after="w1_c10")
-        add_prior(1)
-        for s in range(4, 8):
-            make_h(s, h_banks[s % PACK], whole)
-            fetch_h(s, whole)
+        add_rows(1, prior_sb[1])
+        add_rows(1, pages[1], last=True)
         place(2, whole)
-        add_prior(2)
+        for s in range(4, 8):
+            make_h(s, h_banks[s % PACK], whole, (1, 0))
+            fetch_h(s, whole)
+        round_wb(0, 0, "w1_s00")
+        open_sums()
+        add_rows(2, pages[2], first=True)
+        add_rows(2, prior_sb[2])
         round_wb(0, 1, "w1_c01")
         round_wb(0, 2, "w1_c11")
         place(3, whole)
-        add_prior(3)
-        turn_back(0)
+        add_rows(3, prior_sb[3])
+        add_rows(3, pages[0], last=True)
+        turn_back_first()
         place(4, whole)
-        add_prior(4)
         quantise_wb(0, after="h4")
-        for piece, tag in enumerate(("z_t013", "z_t003", "z_t012")):
+        for piece, tag in enumerate(("z_t00", "z_t01", "wb_raw0")):
             round_wb(1, piece, tag)
         place(5, whole)
-        add_prior(5)
+        open_sums()
+        add_rows(4, prior_sb[4], first=True)
+        add_rows(5, prior_sb[5])
+        add_rows(5, pages[2])
+        add_rows(4, pages[1], last=True)
+        for hf in range(2):
+            rows[hf] = keep("rows%d" % hf, [P, 2, PACK, QUARTER], BF16, after="tab_w%d" % hf)
         place(6, whole)
-        add_prior(6)
-        quantise_z(0, after="h5")
+        z_s[0] = keep("z_s0", [P, T2], U8, after="h5")
+        for k in range(4):
+            quantise_z(0, k)
+        for hf in range(2):
+            add_direct(6, hf, slice(0, 2))
+        turn_back_second()
         quantise_wb(1, after="h6")
         place(7, whole)
-        add_prior(7)
-        turn_back(1)
-        quantise_z(1)
-        for unit in range(2 * N // P):
+        add_direct(7, 0, slice(0, 1))
+        add_direct(7, 0, slice(1, 2))
+        add_direct(7, 1, slice(0, 2))
+        z_s[1] = keep("z_s1", [P, T2], U8)
+        for hf in range(2):
+            for part in range(2):
+                weave(2 * hf + part)
+                quantise_z(1, 2 * hf + part)
+        contention(0)
+        for unit in range(UNITS):
+            if unit + 1 < UNITS:
+                contention(unit + 1)
             finish(unit)

@@ -23,7 +23,7 @@ PACK = 4
 KP = P * PACK
 BANK = 512
 WB_PIECE = 256
-PAGES = 3
+PAGES = 2
 WORK_TAGS = ("w1_raw00", "w1_raw10", "w1_raw01", "w1_raw11", "wb_raw0", "wb_raw1", "spare0", "spare1")
 QUARTER = T2 // 4
 UNITS = 2 * N // P
@@ -136,11 +136,12 @@ def tile_list_listing_budget_pacer_kernel(
                 wb_raw[a][:, :, c0 : c0 + WB_PIECE].rearrange("p j (c i) -> p c j i", i=4),
             )
 
-        def quantise_wb(a, after):
-            wb_s[a] = keep("wb_s%d" % a, [P, N], U8, after=after)
-            for c0 in range(0, N, WB_PIECE):
-                cols = slice(c0, c0 + WB_PIECE)
-                nc.vector.quantize_mx(wb_c[a][:, cols].bitcast(FP8X4), wb_s[a][:, cols], wb_stage[a, c0][:])
+        def quantise_wb(a, piece, after=None):
+            c0 = piece * WB_PIECE
+            wb_s[a, piece] = keep("wb_s%d_%d" % (a, piece), [P, WB_PIECE], U8, after=after)
+            nc.vector.quantize_mx(
+                wb_c[a][:, c0 : c0 + WB_PIECE].bitcast(FP8X4), wb_s[a, piece][:], wb_stage[a, c0][:]
+            )
 
         v_w = {}
 
@@ -222,9 +223,9 @@ def tile_list_listing_budget_pacer_kernel(
                             words[:, P * (2 * k + l) : P * (2 * k + l + 1)],
                             ident[:],
                         )
-                z_in[k] = keep("z_in%d" % k, [P, PACK * QUARTER], BF16)
+                z_in[0, k] = keep("z_in%d" % k, [P, PACK * QUARTER], BF16)
                 nc.scalar.copy(
-                    z_in[k][:].bitcast(F32).rearrange("p (m u) -> p m u", u=2),
+                    z_in[0, k][:].bitcast(F32).rearrange("p (m u) -> p m u", u=2),
                     back[:].rearrange("p (u m) -> p m u", u=2),
                 )
 
@@ -232,20 +233,34 @@ def tile_list_listing_budget_pacer_kernel(
             hf, part = divmod(k, 2)
             cols = slice(QUARTER * part, QUARTER * (part + 1))
             nc.vector.quantize_mx(
-                z_c[b, hf][:, cols].bitcast(FP8X4), z_s[b][:, QUARTER * k : QUARTER * (k + 1)], z_in[k][:]
+                z_c[b, hf][:, cols].bitcast(FP8X4), z_s[b, hf][:, cols], z_in[b, k][:]
             )
 
         rows = {}
 
         def turn_back_second():
             for hf in range(2):
-                back = bank(2 + 2 * hf)
+                back = bank(hf)
                 for mb in range(4):
                     words = z_t[0][:].bitcast(F32)[:, P * (4 * hf + mb) : P * (4 * hf + mb + 1)]
                     nc.tensor.transpose(back[:, P * mb : P * (mb + 1)], words, ident[:])
                 nc.scalar.copy(
                     rows[hf][:, :, 0:2, :], back[:].bitcast(BF16).rearrange("p (q m e) -> p q e m", q=2, e=2)
                 )
+
+        def add_alone(s):
+            for hf in range(2):
+                acc = bank(3 + 2 * hf)
+                for n, src in enumerate((prior_sb[s], pages[s % PAGES])):
+                    for mb in range(4):
+                        turn(acc, mb // 2, mb % 2, src, 4 * hf + mb, n == 0 and mb == 0, n == 1 and mb == 3)
+                turned = keep("turned%d" % hf, [P, BANK], F32)
+                nc.scalar.copy(turned[:], acc[:])
+                back = bank(3 + 2 * hf)
+                for mb in range(4):
+                    cols = slice(P * mb, P * (mb + 1))
+                    nc.tensor.transpose(back[:, cols], turned[:, cols], ident[:])
+                nc.scalar.copy(rows[hf][:, :, s % PACK, :], back[:].rearrange("p (q m) -> p q m", q=2))
 
         def add_direct(s, hf, parts):
             cols = slice(BANK * hf + QUARTER * parts.start, BANK * hf + QUARTER * parts.stop)
@@ -258,14 +273,14 @@ def tile_list_listing_budget_pacer_kernel(
 
         def weave(k):
             hf, part = divmod(k, 2)
-            z_in[k] = keep("woven%d" % k, [P, PACK * QUARTER], BF16, after="z_in%d" % (1 if k == 2 else k))
+            z_in[1, k] = keep("woven%d" % k, [P, PACK * QUARTER], BF16, after="woven1" if k == 2 else None)
             copy = nc.scalar.copy if part else nc.vector.tensor_copy
             copy(
-                z_in[k][:].rearrange("p (m t) -> p m t", t=PACK),
+                z_in[1, k][:].rearrange("p (m t) -> p m t", t=PACK),
                 rows[hf][:, part, :, :].rearrange("p t m -> p m t"),
             )
 
-        unit_banks = ((0, 1), (6, 7), (3, 5), (2, 4))
+        unit_banks = ((6, 7), (2, 4), (0, 1), (3, 5))
         damp = {}
 
         def contention(unit):
@@ -276,9 +291,9 @@ def tile_list_listing_budget_pacer_kernel(
                 nc.tensor.matmul_mx(
                     load[:],
                     lhsT=wb_c[b][:, cols].bitcast(FP8X4),
-                    lhsT_scale=wb_s[b][:, cols],
+                    lhsT_scale=wb_s[b, nt // 2][:, P * (nt % 2) : P * (nt % 2 + 1)],
                     rhs=z_c[b, hf][:].bitcast(FP8X4),
-                    rhs_scale=z_s[b][:, BANK * hf : BANK * (hf + 1)],
+                    rhs_scale=z_s[b, hf][:],
                     start=(b == 0),
                     stop=(b == 1),
                 )
@@ -296,7 +311,7 @@ def tile_list_listing_budget_pacer_kernel(
                     lhsT=wa_w[b][:].bitcast(U8)[:, 2 * P * nt : 2 * P * (nt + 1)].bitcast(FP4X4),
                     lhsT_scale=wa_s[:, b, :].bitcast(U8)[:, cols],
                     rhs=z_c[b, hf][:].bitcast(FP8X4),
-                    rhs_scale=z_s[b][:, BANK * hf : BANK * (hf + 1)],
+                    rhs_scale=z_s[b, hf][:],
                     start=(b == 0),
                     stop=(b == 1),
                 )
@@ -344,45 +359,56 @@ def tile_list_listing_budget_pacer_kernel(
         for s in range(4, 8):
             make_h(s, h_banks[s % PACK], whole, (1, 0))
             fetch_h(s, whole)
-        round_wb(0, 0, "w1_s00")
+        round_wb(0, 0, None)
         open_sums()
-        add_rows(2, pages[2], first=True)
+        add_rows(2, pages[0], first=True)
         add_rows(2, prior_sb[2])
         round_wb(0, 1, "w1_c01")
         round_wb(0, 2, "w1_c11")
         place(3, whole)
         add_rows(3, prior_sb[3])
-        add_rows(3, pages[0], last=True)
+        add_rows(3, pages[1], last=True)
         turn_back_first()
         place(4, whole)
-        quantise_wb(0, after="h4")
+        quantise_wb(0, 0)
         for piece, tag in enumerate(("z_t00", "z_t01", "wb_raw0")):
             round_wb(1, piece, tag)
         place(5, whole)
         open_sums()
-        add_rows(4, prior_sb[4], first=True)
+        add_rows(4, pages[0], first=True)
+        add_rows(4, prior_sb[4])
         add_rows(5, prior_sb[5])
-        add_rows(5, pages[2])
-        add_rows(4, pages[1], last=True)
+        add_rows(5, pages[1], last=True)
         for hf in range(2):
             rows[hf] = keep("rows%d" % hf, [P, 2, PACK, QUARTER], BF16, after="tab_w%d" % hf)
+        z_s[0, 0] = keep("z_s00", [P, BANK], U8, after="h4")
+        quantise_z(0, 0)
+        quantise_z(0, 1)
         place(6, whole)
-        z_s[0] = keep("z_s0", [P, T2], U8, after="h5")
-        for k in range(4):
-            quantise_z(0, k)
-        for hf in range(2):
-            add_direct(6, hf, slice(0, 2))
         turn_back_second()
-        quantise_wb(1, after="h6")
+        add_alone(6)
+        quantise_wb(0, 1)
+        quantise_wb(1, 0)
         place(7, whole)
-        add_direct(7, 0, slice(0, 1))
         add_direct(7, 0, slice(1, 2))
+        add_direct(7, 0, slice(0, 1))
         add_direct(7, 1, slice(0, 2))
-        z_s[1] = keep("z_s1", [P, T2], U8)
-        for hf in range(2):
-            for part in range(2):
-                weave(2 * hf + part)
-                quantise_z(1, 2 * hf + part)
+        z_s[1, 0] = keep("z_s10", [P, BANK], U8)
+        z_s[1, 1] = keep("z_s11", [P, BANK], U8)
+        for k in (1, 0):
+            weave(k)
+        for k in (1, 0):
+            quantise_z(1, k)
+        quantise_wb(1, 1, after="tab_w0")
+        for k in (3, 2):
+            weave(k)
+        for k in (3, 2):
+            quantise_z(1, k)
+        quantise_wb(0, 2, after="woven3")
+        quantise_wb(1, 2, after="woven1")
+        z_s[0, 1] = keep("z_s01", [P, BANK], U8, after="w1_c11")
+        quantise_z(0, 2)
+        quantise_z(0, 3)
         contention(0)
         for unit in range(UNITS):
             if unit + 1 < UNITS:

@@ -15,18 +15,20 @@ U8 = mybir.dt.uint8
 FP8X4 = mybir.dt.float8_e4m3fn_x4
 FP4X4 = mybir.dt.float4_e2m1fn_x4
 MULT = mybir.AluOpType.mult
-ADD = mybir.AluOpType.add
 ACT = mybir.ActivationFunctionType
 
 P = 128
 PACK = 4
 KP = P * PACK
 BANK = 512
-WB_PIECE = 256
-PAGES = 2
-WORK_TAGS = ("w1_raw00", "w1_raw10", "w1_raw01", "w1_raw11", "wb_raw0", "wb_raw1", "spare0", "spare1")
 QUARTER = T2 // 4
-UNITS = 2 * N // P
+WB_PIECE = 256
+LAST_SLICE = H // P - 1
+UNITS = (N // P) * (T2 // BANK)
+H_BANKS = (0, 1, 6, 7)
+SUM_BANK = 2
+UNIT_BANKS = ((0, 1), (6, 7), (2, 3), (4, 5))
+WORK_TAGS = ("w1_raw00", "w1_raw10", "w1_raw01", "w1_raw11", "work_a", "wb_raw1", "work_b", "work_c")
 SQUARED_ON_SCALAR = 2
 
 
@@ -41,8 +43,8 @@ def tile_list_listing_budget_pacer_kernel(
         def keep(name, shape, dtype, after=None):
             return held.tile(shape, dtype, name=name, tag=after or name, align_bytes=64)
 
-        def bank(i):
-            return psum.tile([P, BANK], F32, name="bank%d" % i)
+        def bank(number):
+            return psum.tile([P, BANK], F32, name="bank%d" % number)
 
         idx = held.tile([P, S // 16], U16, name="idx")
         idx2 = held.tile([P, S // 16], U16, name="idx2")
@@ -50,40 +52,39 @@ def tile_list_listing_budget_pacer_kernel(
         tab_w = [keep("tab_w%d" % a, [P, T], I32) for a in range(2)]
         tab_s = keep("tab_s", [P, T // 4], I32)
         wa_s = keep("wa_s", [P, 2, N // 4], I32)
-        wa_w = [keep("wa_w%d" % a, [P, 2 * N // 4], I32) for a in range(2)]
+        wa_w = [keep("wa_w%d" % b, [P, 2 * N // 4], I32) for b in range(2)]
         wgs_sb = keep("wgs_sb", [P, S], F32)
-        pages = [keep("page%d" % e, [P, T2], F32) for e in range(PAGES)]
-        prior_sb = [keep("prior%d" % s, [P, T2], F32) for s in range(8)]
-        wb_raw = [keep("wb_raw%d" % a, [P, PACK, N], F32) for a in range(2)]
+        pages = [keep("page%d" % e, [P, T2], F32) for e in range(2)]
+        prior_sb = [keep("prior%d" % s, [P, T2], F32) for s in range(H // P)]
+        wb_raw = [keep("wb_raw%d" % b, [P, PACK, N], F32) for b in range(2)]
 
         nc.vector.memset(tab_s[:], 0)
         nc.vector.memset(wa_s[:], 0)
-        for q in range(4):
+        for quad in range(4):
             nc.gpsimd.dma_start(
-                tab_s[32 * q : 32 * q + 8, :], tab_scales[:, 4 * q : 4 * q + 4, :].bitcast(I32)
+                tab_s[32 * quad : 32 * quad + 8, :], tab_scales[:, 4 * quad : 4 * quad + 4, :].bitcast(I32)
             )
         for page in pages:
             nc.gpsimd.memset(page[:], 0.0)
         make_identity(nc, ident[:])
-        warm = keep("warm", [P, 1], F32)
-        nc.scalar.activation(warm[:], pages[0][:, 0:1], ACT.Abs_reciprocal_sqrt, bias=1.0)
+        ones = keep("ones", [P, 1], F32)
+        nc.scalar.activation(ones[:], pages[0][:, 0:1], ACT.Abs_reciprocal_sqrt, bias=1.0)
 
         w1_raw = {}
 
         def load_w1(a, b):
-            raw = keep("w1_raw%d%d" % (a, b), [P, PACK, KP], F32)
-            rows = w1[KP * a : KP * (a + 1), KP * b : KP * (b + 1)]
-            nc.sync.dma_start(raw[:], rows.rearrange("(p j) c -> p j c", j=PACK))
-            w1_raw[a, b] = raw
+            w1_raw[a, b] = keep("w1_raw%d%d" % (a, b), [P, PACK, KP], F32)
+            part = w1[KP * a : KP * (a + 1), KP * b : KP * (b + 1)]
+            nc.sync.dma_start(w1_raw[a, b][:], part.rearrange("(p j) c -> p j c", j=PACK))
 
         def load_prior(s):
             b, i = divmod(s, PACK)
-            rows = prior[KP * b : KP * (b + 1), :].rearrange("(p i) m -> p i m", i=PACK)
-            nc.sync.dma_start(prior_sb[s][:], rows[:, i, :])
+            part = prior[KP * b : KP * (b + 1), :].rearrange("(p i) m -> p i m", i=PACK)
+            nc.sync.dma_start(prior_sb[s][:], part[:, i, :])
 
-        def load_wb(a):
-            rows = wb[KP * a : KP * (a + 1), :]
-            nc.sync.dma_start(wb_raw[a][:], rows.rearrange("(p j) c -> p j c", j=PACK))
+        def load_wb(b):
+            part = wb[KP * b : KP * (b + 1), :]
+            nc.sync.dma_start(wb_raw[b][:], part.rearrange("(p j) c -> p j c", j=PACK))
 
         load_w1(0, 0)
         nc.sync.dma_start(idx[:], offs)
@@ -100,62 +101,56 @@ def tile_list_listing_budget_pacer_kernel(
         load_prior(2)
         load_prior(3)
         load_wb(1)
-        for s in range(4, 7):
+        for s in range(4, LAST_SLICE):
             load_prior(s)
-        for q in range(4):
+        for quad in range(4):
             nc.sync.dma_start(
-                wa_s[32 * q : 32 * q + 4, :, :],
-                wa_scales[:, 4 * q : 4 * q + 4, :].bitcast(I32).rearrange("a r c -> r a c"),
+                wa_s[32 * quad : 32 * quad + 4, :, :],
+                wa_scales[:, 4 * quad : 4 * quad + 4, :].bitcast(I32).rearrange("b r c -> r b c"),
             )
-        for a in range(2):
-            nc.sync.dma_start(wa_w[a][:], wa_words[a].bitcast(I32))
-        load_prior(7)
+        for b in range(2):
+            nc.sync.dma_start(wa_w[b][:], wa_words[b].bitcast(I32))
+        load_prior(LAST_SLICE)
 
         w1_c, w1_s = {}, {}
 
         def quantise_w1(a, b, after=None, scales_after=None):
             stage = keep("w1_stage%d%d" % (a, b), [P, PACK * KP], BF16, after=after)
             nc.scalar.copy(
-                stage[:].rearrange("p (t m j) -> p m j t", t=PACK, j=PACK),
-                w1_raw[a, b][:].rearrange("p j (m t) -> p m j t", t=PACK),
+                stage[:].rearrange("p (i c j) -> p c j i", i=PACK, j=PACK),
+                w1_raw[a, b][:].rearrange("p j (c i) -> p c j i", i=PACK),
             )
             w1_c[a, b] = keep("w1_c%d%d" % (a, b), [P, KP], U32)
             w1_s[a, b] = keep("w1_s%d%d" % (a, b), [P, KP], U8, after=scales_after)
             nc.vector.quantize_mx(w1_c[a, b][:].bitcast(FP8X4), w1_s[a, b][:], stage[:])
 
-        wb_c = [keep("wb_c%d" % a, [P, N], U32) for a in range(2)]
-        wb_s = {}
-        wb_stage = {}
+        wb_c = [keep("wb_c%d" % b, [P, N], U32) for b in range(2)]
+        wb_s, wb_stage = {}, {}
 
-        def round_wb(a, piece, after):
-            c0 = piece * WB_PIECE
-            stage = keep("wb_stage%d_%d" % (a, c0), [P, PACK * WB_PIECE], BF16, after=after)
-            wb_stage[a, c0] = stage
+        def round_wb(b, piece, after=None):
+            wb_stage[b, piece] = keep("wb_stage%d%d" % (b, piece), [P, PACK * WB_PIECE], BF16, after=after)
             nc.scalar.copy(
-                stage[:].rearrange("p (c i j) -> p c j i", i=4, j=PACK),
-                wb_raw[a][:, :, c0 : c0 + WB_PIECE].rearrange("p j (c i) -> p c j i", i=4),
+                wb_stage[b, piece][:].rearrange("p (c n j) -> p c j n", n=4, j=PACK),
+                wb_raw[b][:, :, WB_PIECE * piece : WB_PIECE * (piece + 1)].rearrange("p j (c n) -> p c j n", n=4),
             )
 
-        def quantise_wb(a, piece, after=None):
-            c0 = piece * WB_PIECE
-            wb_s[a, piece] = keep("wb_s%d_%d" % (a, piece), [P, WB_PIECE], U8, after=after)
+        def quantise_wb(b, piece, after=None):
+            wb_s[b, piece] = keep("wb_s%d%d" % (b, piece), [P, WB_PIECE], U8, after=after)
             nc.vector.quantize_mx(
-                wb_c[a][:, c0 : c0 + WB_PIECE].bitcast(FP8X4), wb_s[a, piece][:], wb_stage[a, c0][:]
+                wb_c[b][:, WB_PIECE * piece : WB_PIECE * (piece + 1)].bitcast(FP8X4),
+                wb_s[b, piece][:],
+                wb_stage[b, piece][:],
             )
 
-        v_w = {}
+        v_w, h_ps, h_sb = {}, {}, {}
 
-        h_banks = (0, 1, 6, 7)
-        h_sb = {}
-        h_ps = {}
-
-        def make_h(s, which, entries, passes):
+        def make_h(s, number, entries, passes):
             b, i = divmod(s, PACK)
             cols = slice(P * i, P * (i + 1))
-            acc = bank(which)
+            h_ps[s, entries.start] = bank(number)
             for a in passes:
                 nc.tensor.matmul_mx(
-                    acc[:, entries],
+                    h_ps[s, entries.start][:, entries],
                     lhsT=w1_c[a, b][:, cols].bitcast(FP8X4),
                     lhsT_scale=w1_s[a, b][:, cols],
                     rhs=v_w[a][:, entries].bitcast(FP8X4),
@@ -163,171 +158,117 @@ def tile_list_listing_budget_pacer_kernel(
                     start=(a == passes[0]),
                     stop=(a == passes[1]),
                 )
-            h_ps[s, entries.start] = acc
 
         def fetch_h(s, entries, after=None):
             if entries.start == 0:
                 h_sb[s] = keep("h%d" % s, [P, S], F32, after=after)
             nc.scalar.copy(h_sb[s][:, entries], h_ps[s, entries.start][:, entries])
 
-        sums = {}
-        z_t = {}
-
-        def turn(acc, l, e, src, mb, start, stop):
-            region = slice(P * (2 * l + e), P * (2 * l + e + 1))
-            nc.tensor.matmul(
-                acc[:, region],
-                lhsT=src[:, P * mb : P * (mb + 1)],
-                rhs=ident[:],
-                is_transpose=True,
-                start=start,
-                stop=stop,
-            )
-
         def place(s, entries):
             offsets = idx2[:, entries.start // 16 : entries.stop // 16]
-            nc.vector.tensor_tensor(
-                pages[s % PAGES][:].indirect(offsets), h_sb[s][:, entries], wgs_sb[:, entries], MULT
-            )
+            nc.vector.tensor_tensor(pages[s % 2][:].indirect(offsets), h_sb[s][:, entries], wgs_sb[:, entries], MULT)
+
+        sums, z_t = {}, {}
 
         def open_sums():
-            for k in range(4):
-                sums[k] = bank(2 + k)
+            for quarter in range(4):
+                sums[quarter] = bank(SUM_BANK + quarter)
 
-        def add_rows(s, src, first=False, last=False, after=None):
+        def add_turned(s, src, first=False, last=False):
             b, i = divmod(s, PACK)
-            u = i // 2
+            pair, e = divmod(i, 2)
             if last:
-                z_t[u] = keep("z_t%d%d" % (b, u), [P, 4 * BANK], BF16, after=after)
-            for k in range(4):
+                z_t[pair] = keep("z_t%d%d" % (b, pair), [P, 4 * BANK], BF16)
+            for quarter in range(4):
                 for l in range(2):
-                    turn(sums[k], l, s % 2, src, 2 * k + l, first and l == 0, last and l == 1)
+                    nc.tensor.matmul(
+                        sums[quarter][:, P * (2 * l + e) : P * (2 * l + e + 1)],
+                        lhsT=src[:, P * (2 * quarter + l) : P * (2 * quarter + l + 1)],
+                        rhs=ident[:],
+                        is_transpose=True,
+                        start=first and l == 0,
+                        stop=last and l == 1,
+                    )
                 if last:
-                    nc.scalar.copy(
-                        z_t[u][:, BANK * k : BANK * (k + 1)].rearrange("m (l p e) -> m l p e", l=2, e=2),
-                        sums[k][:].rearrange("m (l e p) -> m l p e", l=2, e=2),
+                    copy = nc.vector.tensor_copy if s == LAST_SLICE and quarter == 1 else nc.scalar.copy
+                    copy(
+                        z_t[pair][:, BANK * quarter : BANK * (quarter + 1)].rearrange("m (l p e) -> m l p e", l=2, e=2),
+                        sums[quarter][:].rearrange("m (l e p) -> m l p e", l=2, e=2),
                     )
 
         z_c = {(b, hf): keep("z_c%d%d" % (b, hf), [P, BANK], U32) for b in range(2) for hf in range(2)}
-        z_s = {}
-        z_in = {}
+        z_s, z_in = {}, {}
 
-        def turn_back_first():
-            for k in range(4):
-                back = bank(2 + k)
-                for u in range(2):
-                    words = z_t[u][:].bitcast(F32)
+        def turn_back(b):
+            for quarter in range(4):
+                back = bank(SUM_BANK + quarter)
+                for pair in range(2):
+                    words = z_t[pair][:].bitcast(F32)
                     for l in range(2):
                         nc.tensor.transpose(
-                            back[:, P * (2 * u + l) : P * (2 * u + l + 1)],
-                            words[:, P * (2 * k + l) : P * (2 * k + l + 1)],
+                            back[:, P * (2 * pair + l) : P * (2 * pair + l + 1)],
+                            words[:, P * (2 * quarter + l) : P * (2 * quarter + l + 1)],
                             ident[:],
                         )
-                z_in[0, k] = keep("z_in%d" % k, [P, PACK * QUARTER], BF16)
-                nc.scalar.copy(
-                    z_in[0, k][:].bitcast(F32).rearrange("p (m u) -> p m u", u=2),
+                z_in[b, quarter] = keep("z_in%d%d" % (b, quarter), [P, PACK * QUARTER], BF16)
+                copy = nc.vector.tensor_copy if b == 1 and quarter == 0 else nc.scalar.copy
+                copy(
+                    z_in[b, quarter][:].bitcast(F32).rearrange("p (m u) -> p m u", u=2),
                     back[:].rearrange("p (u m) -> p m u", u=2),
                 )
 
-        def quantise_z(b, k):
-            hf, part = divmod(k, 2)
+        def quantise_z(b, quarter):
+            hf, part = divmod(quarter, 2)
             cols = slice(QUARTER * part, QUARTER * (part + 1))
-            nc.vector.quantize_mx(
-                z_c[b, hf][:, cols].bitcast(FP8X4), z_s[b, hf][:, cols], z_in[b, k][:]
-            )
+            nc.vector.quantize_mx(z_c[b, hf][:, cols].bitcast(FP8X4), z_s[b, hf][:, cols], z_in[b, quarter][:])
 
-        rows = {}
-
-        def turn_back_second():
-            for hf in range(2):
-                back = bank(hf)
-                for mb in range(4):
-                    words = z_t[0][:].bitcast(F32)[:, P * (4 * hf + mb) : P * (4 * hf + mb + 1)]
-                    nc.tensor.transpose(back[:, P * mb : P * (mb + 1)], words, ident[:])
-                nc.scalar.copy(
-                    rows[hf][:, :, 0:2, :], back[:].bitcast(BF16).rearrange("p (q m e) -> p q e m", q=2, e=2)
-                )
-
-        def add_alone(s):
-            for hf in range(2):
-                acc = bank(3 + 2 * hf)
-                for n, src in enumerate((prior_sb[s], pages[s % PAGES])):
-                    for mb in range(4):
-                        turn(acc, mb // 2, mb % 2, src, 4 * hf + mb, n == 0 and mb == 0, n == 1 and mb == 3)
-                turned = keep("turned%d" % hf, [P, BANK], F32)
-                nc.scalar.copy(turned[:], acc[:])
-                back = bank(3 + 2 * hf)
-                for mb in range(4):
-                    cols = slice(P * mb, P * (mb + 1))
-                    nc.tensor.transpose(back[:, cols], turned[:, cols], ident[:])
-                nc.scalar.copy(rows[hf][:, :, s % PACK, :], back[:].rearrange("p (q m) -> p q m", q=2))
-
-        def add_direct(s, hf, parts):
-            cols = slice(BANK * hf + QUARTER * parts.start, BANK * hf + QUARTER * parts.stop)
-            nc.vector.tensor_tensor(
-                rows[hf][:, parts, s % PACK, :],
-                pages[s % PAGES][:, cols].rearrange("p (q m) -> p q m", m=QUARTER),
-                prior_sb[s][:, cols].rearrange("p (q m) -> p q m", m=QUARTER),
-                ADD,
-            )
-
-        def weave(k):
-            hf, part = divmod(k, 2)
-            z_in[1, k] = keep("woven%d" % k, [P, PACK * QUARTER], BF16, after="woven1" if k == 2 else None)
-            copy = nc.scalar.copy if part else nc.vector.tensor_copy
-            copy(
-                z_in[1, k][:].rearrange("p (m t) -> p m t", t=PACK),
-                rows[hf][:, part, :, :].rearrange("p t m -> p m t"),
-            )
-
-        unit_banks = ((6, 7), (2, 4), (0, 1), (3, 5))
-        damp = {}
+        work = {}
 
         def contention(unit):
             hf, nt = divmod(unit, N // P)
-            cols = slice(P * nt, P * (nt + 1))
-            load = bank(unit_banks[unit % 4][0])
+            piece, part = divmod(nt, WB_PIECE // P)
+            load = bank(UNIT_BANKS[unit % 4][0])
             for b in range(2):
                 nc.tensor.matmul_mx(
                     load[:],
-                    lhsT=wb_c[b][:, cols].bitcast(FP8X4),
-                    lhsT_scale=wb_s[b, nt // 2][:, P * (nt % 2) : P * (nt % 2 + 1)],
+                    lhsT=wb_c[b][:, P * nt : P * (nt + 1)].bitcast(FP8X4),
+                    lhsT_scale=wb_s[b, piece][:, P * part : P * (part + 1)],
                     rhs=z_c[b, hf][:].bitcast(FP8X4),
                     rhs_scale=z_s[b, hf][:],
                     start=(b == 0),
                     stop=(b == 1),
                 )
-            work = keep("work%d" % unit, [P, 3, BANK], F32, after=WORK_TAGS[unit % len(WORK_TAGS)])
-            nc.scalar.activation(work[:, 0, :], load[:], ACT.Square)
-            damp[unit] = work
+            work[unit] = keep("work%d" % unit, [P, 3, BANK], F32, after=WORK_TAGS[unit % len(WORK_TAGS)])
+            nc.scalar.activation(work[unit][:, 0, :], load[:], ACT.Square)
 
         def finish(unit):
             hf, nt = divmod(unit, N // P)
-            cols = slice(P * nt, P * (nt + 1))
-            spend = bank(unit_banks[unit % 4][1])
+            rows = slice(P * nt, P * (nt + 1))
+            spend = bank(UNIT_BANKS[unit % 4][1])
             for b in range(2):
                 nc.tensor.matmul_mx(
                     spend[:],
                     lhsT=wa_w[b][:].bitcast(U8)[:, 2 * P * nt : 2 * P * (nt + 1)].bitcast(FP4X4),
-                    lhsT_scale=wa_s[:, b, :].bitcast(U8)[:, cols],
+                    lhsT_scale=wa_s[:, b, :].bitcast(U8)[:, rows],
                     rhs=z_c[b, hf][:].bitcast(FP8X4),
                     rhs_scale=z_s[b, hf][:],
                     start=(b == 0),
                     stop=(b == 1),
                 )
-            work = damp[unit]
-            nc.scalar.activation(work[:, 1, :], work[:, 0, :], ACT.Abs_reciprocal_sqrt, bias=1.0)
-            res = keep("res%d" % unit, [P, BANK], F32, after="prior%d" % (unit % 8))
+            square, root, between = [work[unit][:, n, :] for n in range(3)]
+            nc.scalar.activation(root, square, ACT.Abs_reciprocal_sqrt, bias=ones[:])
+            res = keep("res%d" % unit, [P, BANK], F32, after="prior%d" % (unit % len(prior_sb)))
             if unit < UNITS - SQUARED_ON_SCALAR:
-                nc.vector.tensor_tensor(work[:, 2, :], spend[:], work[:, 1, :], MULT)
-                nc.vector.tensor_tensor(res[:], work[:, 2, :], work[:, 1, :], MULT)
+                nc.vector.tensor_tensor(between, spend[:], root, MULT)
+                nc.vector.tensor_tensor(res[:], between, root, MULT)
             else:
-                nc.scalar.activation(work[:, 2, :], work[:, 1, :], ACT.Square)
-                nc.vector.tensor_tensor(res[:], spend[:], work[:, 2, :], MULT)
-            nc.sync.dma_start(out[cols, BANK * hf : BANK * (hf + 1)], res[:])
+                nc.scalar.activation(between, root, ACT.Square)
+                nc.vector.tensor_tensor(res[:], spend[:], between, MULT)
+            nc.sync.dma_start(out[rows, BANK * hf : BANK * (hf + 1)], res[:])
 
         whole = slice(0, S)
         halves = (slice(0, S // 2), slice(S // 2, S))
+
         v_s = keep("v_s", [P, S], U8)
         nc.vector.tensor_copy(v_s[:], tab_s[:].bitcast(U8).indirect(idx[:]))
         quantise_w1(0, 0)
@@ -338,77 +279,76 @@ def tile_list_listing_budget_pacer_kernel(
         for half in halves:
             offsets = idx[:, half.start // 16 : half.stop // 16]
             nc.vector.tensor_copy(v_w[1][:, half], tab_w[1][:].bitcast(U32).indirect(offsets))
-        for half, which in zip(halves, (0, 2)):
-            make_h(0, which, half, (0, 1))
+        for half, number in zip(halves, (H_BANKS[0], SUM_BANK)):
+            make_h(0, number, half, (0, 1))
             fetch_h(0, half)
             place(0, half)
-        for s in (1, 2, 3):
-            make_h(s, h_banks[s], whole, (1, 0))
+        for s in range(1, PACK):
+            make_h(s, H_BANKS[s], whole, (1, 0))
         fetch_h(1, whole)
+
         open_sums()
-        add_rows(0, pages[0], first=True)
-        add_rows(0, prior_sb[0])
+        add_turned(0, pages[0], first=True)
+        add_turned(0, prior_sb[0])
         place(1, whole)
         quantise_w1(0, 1)
         quantise_w1(1, 1, after="w1_c10")
         fetch_h(2, whole, after="w1_raw11")
         fetch_h(3, whole, after="w1_c10")
-        add_rows(1, prior_sb[1])
-        add_rows(1, pages[1], last=True)
+        add_turned(1, prior_sb[1])
+        add_turned(1, pages[1], last=True)
         place(2, whole)
-        for s in range(4, 8):
-            make_h(s, h_banks[s % PACK], whole, (1, 0))
+        for s in range(PACK, 2 * PACK):
+            make_h(s, H_BANKS[s % PACK], whole, (1, 0))
             fetch_h(s, whole)
-        round_wb(0, 0, None)
+        round_wb(0, 0)
         open_sums()
-        add_rows(2, pages[0], first=True)
-        add_rows(2, prior_sb[2])
-        round_wb(0, 1, "w1_c01")
-        round_wb(0, 2, "w1_c11")
+        add_turned(2, pages[0], first=True)
+        add_turned(2, prior_sb[2])
+        round_wb(0, 1, after="w1_c01")
+        round_wb(0, 2, after="w1_c11")
         place(3, whole)
-        add_rows(3, prior_sb[3])
-        add_rows(3, pages[1], last=True)
-        turn_back_first()
+        add_turned(3, prior_sb[3])
+        add_turned(3, pages[1], last=True)
+        turn_back(0)
+
         place(4, whole)
         quantise_wb(0, 0)
         for piece, tag in enumerate(("z_t00", "z_t01", "wb_raw0")):
-            round_wb(1, piece, tag)
+            round_wb(1, piece, after=tag)
         place(5, whole)
         open_sums()
-        add_rows(4, pages[0], first=True)
-        add_rows(4, prior_sb[4])
-        add_rows(5, prior_sb[5])
-        add_rows(5, pages[1], last=True)
-        for hf in range(2):
-            rows[hf] = keep("rows%d" % hf, [P, 2, PACK, QUARTER], BF16, after="tab_w%d" % hf)
+        add_turned(4, pages[0], first=True)
+        add_turned(4, prior_sb[4])
+        add_turned(5, prior_sb[5])
+        add_turned(5, pages[1], last=True)
         z_s[0, 0] = keep("z_s00", [P, BANK], U8, after="h4")
         quantise_z(0, 0)
         quantise_z(0, 1)
         place(6, whole)
-        turn_back_second()
-        add_alone(6)
-        quantise_wb(0, 1)
-        quantise_wb(1, 0)
+        open_sums()
+        add_turned(6, prior_sb[6], first=True)
+        add_turned(7, prior_sb[7])
+        add_turned(6, pages[0])
         place(7, whole)
-        add_direct(7, 0, slice(1, 2))
-        add_direct(7, 0, slice(0, 1))
-        add_direct(7, 1, slice(0, 2))
+        add_turned(7, pages[1], last=True)
+        turn_back(1)
+
         z_s[1, 0] = keep("z_s10", [P, BANK], U8)
         z_s[1, 1] = keep("z_s11", [P, BANK], U8)
-        for k in (1, 0):
-            weave(k)
-        for k in (1, 0):
-            quantise_z(1, k)
-        quantise_wb(1, 1, after="tab_w0")
-        for k in (3, 2):
-            weave(k)
-        for k in (3, 2):
-            quantise_z(1, k)
-        quantise_wb(0, 2, after="woven3")
-        quantise_wb(1, 2, after="woven1")
-        z_s[0, 1] = keep("z_s01", [P, BANK], U8, after="w1_c11")
+        quantise_wb(1, 0, after="h7")
+        quantise_wb(0, 1, after="wgs_sb")
+        quantise_z(1, 0)
+        quantise_z(1, 1)
+        quantise_wb(1, 1, after="z_t00")
+        quantise_z(1, 2)
+        quantise_z(1, 3)
+        quantise_wb(0, 2, after="z_in11")
+        quantise_wb(1, 2, after="w1_c11")
+        z_s[0, 1] = keep("z_s01", [P, BANK], U8, after="wb_raw0")
         quantise_z(0, 2)
         quantise_z(0, 3)
+
         contention(0)
         for unit in range(UNITS):
             if unit + 1 < UNITS:

@@ -15,6 +15,7 @@ U8 = mybir.dt.uint8
 FP8X4 = mybir.dt.float8_e4m3fn_x4
 FP4X4 = mybir.dt.float4_e2m1fn_x4
 MULT = mybir.AluOpType.mult
+ADD = mybir.AluOpType.add
 ACT = mybir.ActivationFunctionType
 
 P = 128
@@ -25,11 +26,14 @@ QUARTER = T2 // 4
 WB_PIECE = 256
 LAST_SLICE = H // P - 1
 UNITS = (N // P) * (T2 // BANK)
-H_BANKS = (0, 1, 6, 7)
-SUM_BANK = 2
-UNIT_BANKS = ((0, 1), (6, 7), (2, 3), (4, 5))
-WORK_TAGS = ("w1_raw00", "w1_raw10", "w1_raw01", "w1_raw11", "work_a", "wb_raw1", "work_b", "work_c")
-SQUARED_ON_SCALAR = 2
+PAGES = 3
+HALF = T2 // 2
+WORK_TAGS = ("w1_raw00", "w1_raw10", "w1_raw01", "w1_raw11", "tab_w0", "tab_w1")
+RES_TAGS = ["prior%d" % s for s in (0, 1, 2, 3, 4, 6, 5)] + ["h%d" % s for s in (0, 1, 4, 5, 7, 6)]
+LOAD_BANKS = (0, 1, 3, 6)
+SPEND_BANKS = (2, 7, 4, 5)
+UNIT_PLACES = [(hf, nt) for nts in (range(4), range(4, 6)) for hf in range(2) for nt in nts]
+ON_GPSIMD = ()
 
 
 def tile_list_listing_budget_pacer_kernel(
@@ -54,9 +58,10 @@ def tile_list_listing_budget_pacer_kernel(
         wa_s = keep("wa_s", [P, 2, N // 4], I32)
         wa_w = [keep("wa_w%d" % b, [P, 2 * N // 4], I32) for b in range(2)]
         wgs_sb = keep("wgs_sb", [P, S], F32)
-        pages = [keep("page%d" % e, [P, T2], F32) for e in range(2)]
-        prior_sb = [keep("prior%d" % s, [P, T2], F32) for s in range(H // P)]
-        wb_raw = [keep("wb_raw%d" % b, [P, PACK, N], F32) for b in range(2)]
+        pages = [keep("page%d" % e, [P, T2], F32) for e in range(PAGES)]
+        prior_sb = [keep("prior%d" % s, [P, T2], F32) for s in range(LAST_SLICE)]
+        prior_sb.append([keep("prior7" + hf, [P, HALF], F32) for hf in "ab"])
+        wb_raw = {}
 
         nc.vector.memset(tab_s[:], 0)
         nc.vector.memset(wa_s[:], 0)
@@ -80,11 +85,16 @@ def tile_list_listing_budget_pacer_kernel(
         def load_prior(s):
             b, i = divmod(s, PACK)
             part = prior[KP * b : KP * (b + 1), :].rearrange("(p i) m -> p i m", i=PACK)
-            nc.sync.dma_start(prior_sb[s][:], part[:, i, :])
+            if s < LAST_SLICE:
+                nc.sync.dma_start(prior_sb[s][:], part[:, i, :])
+            else:
+                for hf in range(2):
+                    nc.sync.dma_start(prior_sb[s][hf][:], part[:, i, HALF * hf : HALF * (hf + 1)])
 
-        def load_wb(b):
-            part = wb[KP * b : KP * (b + 1), :]
-            nc.sync.dma_start(wb_raw[b][:], part.rearrange("(p j) c -> p j c", j=PACK))
+        def load_wb(b, piece):
+            wb_raw[b, piece] = keep("wb_raw%d%d" % (b, piece), [P, PACK, WB_PIECE], F32)
+            part = wb[KP * b : KP * (b + 1), WB_PIECE * piece : WB_PIECE * (piece + 1)]
+            nc.sync.dma_start(wb_raw[b, piece][:], part.rearrange("(p j) c -> p j c", j=PACK))
 
         load_w1(0, 0)
         nc.sync.dma_start(idx[:], offs)
@@ -97,12 +107,15 @@ def tile_list_listing_budget_pacer_kernel(
         load_w1(1, 1)
         load_prior(0)
         load_prior(1)
-        load_wb(0)
         load_prior(2)
         load_prior(3)
-        load_wb(1)
-        for s in range(4, LAST_SLICE):
-            load_prior(s)
+        load_wb(0, 0)
+        load_wb(0, 1)
+        load_wb(1, 0)
+        load_prior(4)
+        load_prior(5)
+        load_wb(1, 1)
+        load_prior(6)
         for quad in range(4):
             nc.sync.dma_start(
                 wa_s[32 * quad : 32 * quad + 4, :, :],
@@ -111,6 +124,8 @@ def tile_list_listing_budget_pacer_kernel(
         for b in range(2):
             nc.sync.dma_start(wa_w[b][:], wa_words[b].bitcast(I32))
         load_prior(LAST_SLICE)
+        load_wb(0, 2)
+        load_wb(1, 2)
 
         w1_c, w1_s = {}, {}
 
@@ -127,18 +142,18 @@ def tile_list_listing_budget_pacer_kernel(
         wb_c = [keep("wb_c%d" % b, [P, N], U32) for b in range(2)]
         wb_s, wb_stage = {}, {}
 
-        def round_wb(b, piece, after=None):
+        def round_wb(b, piece, after=None, copy=nc.scalar.copy):
             wb_stage[b, piece] = keep("wb_stage%d%d" % (b, piece), [P, PACK * WB_PIECE], BF16, after=after)
-            nc.scalar.copy(
+            copy(
                 wb_stage[b, piece][:].rearrange("p (c n j) -> p c j n", n=4, j=PACK),
-                wb_raw[b][:, :, WB_PIECE * piece : WB_PIECE * (piece + 1)].rearrange("p j (c n) -> p c j n", n=4),
+                wb_raw[b, piece][:].rearrange("p j (c n) -> p c j n", n=4),
             )
 
-        def quantise_wb(b, piece, after=None):
-            wb_s[b, piece] = keep("wb_s%d%d" % (b, piece), [P, WB_PIECE], U8, after=after)
+        def quantise_wb(b, piece, scales):
+            wb_s[b, piece] = scales
             nc.vector.quantize_mx(
                 wb_c[b][:, WB_PIECE * piece : WB_PIECE * (piece + 1)].bitcast(FP8X4),
-                wb_s[b, piece][:],
+                scales,
                 wb_stage[b, piece][:],
             )
 
@@ -166,105 +181,149 @@ def tile_list_listing_budget_pacer_kernel(
 
         def place(s, entries):
             offsets = idx2[:, entries.start // 16 : entries.stop // 16]
-            nc.vector.tensor_tensor(pages[s % 2][:].indirect(offsets), h_sb[s][:, entries], wgs_sb[:, entries], MULT)
+            nc.vector.tensor_tensor(pages[s % PAGES][:].indirect(offsets), h_sb[s][:, entries], wgs_sb[:, entries], MULT)
 
-        sums, z_t = {}, {}
+        z_t = {}
 
-        def open_sums():
+        def new_z_t(pair, name, after=None):
+            both = keep(name, [P, 4 * BANK], BF16, after=after)
+            for hf in range(2):
+                z_t[pair, hf] = both[:, 2 * BANK * hf : 2 * BANK * (hf + 1)]
+
+        def add_turned(src, blocks, regions, first=False, last=False):
+            seen = [regions(block)[0] for block in blocks]
+            for n, block in enumerate(blocks):
+                sums, region = regions(block)
+                nc.tensor.matmul(
+                    sums[:, P * region : P * (region + 1)],
+                    lhsT=src[:, P * block : P * (block + 1)],
+                    rhs=ident[:],
+                    is_transpose=True,
+                    start=first and not any(sums is other for other in seen[:n]),
+                    stop=last and not any(sums is other for other in seen[n + 1 :]),
+                )
+
+        def pair_regions(banks, e):
+            return lambda block: (banks[block // 2], 2 * (block % 2) + e)
+
+        def round_pair(pair, quarter, sums, copy):
+            hf, part = divmod(quarter, 2)
+            copy(
+                z_t[pair, hf][:, BANK * part : BANK * (part + 1)].rearrange("m (l p e) -> m l p e", l=2, e=2),
+                sums[:].rearrange("m (l e p) -> m l p e", l=2, e=2),
+            )
+
+        def add_pair(s, numbers):
+            banks = [bank(number) for number in numbers]
+            add_turned(prior_sb[s], range(8), pair_regions(banks, 0), first=True)
+            add_turned(prior_sb[s + 1], range(8), pair_regions(banks, 1))
+            return banks
+
+        def close_pair(s, banks):
             for quarter in range(4):
-                sums[quarter] = bank(SUM_BANK + quarter)
-
-        def add_turned(s, src, first=False, last=False):
-            b, i = divmod(s, PACK)
-            pair, e = divmod(i, 2)
-            if last:
-                z_t[pair] = keep("z_t%d%d" % (b, pair), [P, 4 * BANK], BF16)
-            for quarter in range(4):
-                for l in range(2):
-                    nc.tensor.matmul(
-                        sums[quarter][:, P * (2 * l + e) : P * (2 * l + e + 1)],
-                        lhsT=src[:, P * (2 * quarter + l) : P * (2 * quarter + l + 1)],
-                        rhs=ident[:],
-                        is_transpose=True,
-                        start=first and l == 0,
-                        stop=last and l == 1,
-                    )
-                if last:
-                    copy = nc.vector.tensor_copy if s == LAST_SLICE and quarter == 1 else nc.scalar.copy
-                    copy(
-                        z_t[pair][:, BANK * quarter : BANK * (quarter + 1)].rearrange("m (l p e) -> m l p e", l=2, e=2),
-                        sums[quarter][:].rearrange("m (l e p) -> m l p e", l=2, e=2),
-                    )
+                add_turned(pages[(s + 1) % PAGES], (2 * quarter, 2 * quarter + 1), pair_regions(banks, 1), last=True)
+                round_pair(s % PACK // 2, quarter, banks[quarter], nc.scalar.copy)
 
         z_c = {(b, hf): keep("z_c%d%d" % (b, hf), [P, BANK], U32) for b in range(2) for hf in range(2)}
         z_s, z_in = {}, {}
 
-        def turn_back(b):
-            for quarter in range(4):
-                back = bank(SUM_BANK + quarter)
-                for pair in range(2):
-                    words = z_t[pair][:].bitcast(F32)
-                    for l in range(2):
-                        nc.tensor.transpose(
-                            back[:, P * (2 * pair + l) : P * (2 * pair + l + 1)],
-                            words[:, P * (2 * quarter + l) : P * (2 * quarter + l + 1)],
-                            ident[:],
-                        )
-                z_in[b, quarter] = keep("z_in%d%d" % (b, quarter), [P, PACK * QUARTER], BF16)
-                copy = nc.vector.tensor_copy if b == 1 and quarter == 0 else nc.scalar.copy
-                copy(
-                    z_in[b, quarter][:].bitcast(F32).rearrange("p (m u) -> p m u", u=2),
-                    back[:].rearrange("p (u m) -> p m u", u=2),
-                )
-
-        def quantise_z(b, quarter):
+        def turn_words(quarter, back, pairs):
             hf, part = divmod(quarter, 2)
-            cols = slice(QUARTER * part, QUARTER * (part + 1))
-            nc.vector.quantize_mx(z_c[b, hf][:, cols].bitcast(FP8X4), z_s[b, hf][:, cols], z_in[b, quarter][:])
+            for pair in pairs:
+                words = z_t[pair, hf].bitcast(F32)
+                for l in range(2):
+                    nc.tensor.transpose(
+                        back[:, P * (2 * pair + l) : P * (2 * pair + l + 1)],
+                        words[:, P * (2 * part + l) : P * (2 * part + l + 1)],
+                        ident[:],
+                    )
+            return back
 
-        work = {}
+        def fetch_words(b, quarter, back, after=None):
+            hf, part = divmod(quarter, 2)
+            if part == 0:
+                z_in[b, hf] = keep("z_in%d%d" % (b, hf), [P, PACK * HALF], BF16, after=after)
+            nc.scalar.copy(
+                z_in[b, hf][:].bitcast(F32)[:, BANK * part : BANK * (part + 1)].rearrange("p (m u) -> p m u", u=2),
+                back[:].rearrange("p (u m) -> p m u", u=2),
+            )
+
+        def quantise_z(b, hf):
+            nc.vector.quantize_mx(z_c[b, hf][:].bitcast(FP8X4), z_s[b, hf], z_in[b, hf][:])
+
+        work, loads, spends = {}, {}, {}
+
+        def load_pass(unit, b):
+            hf, nt = UNIT_PLACES[unit]
+            piece, part = divmod(nt, WB_PIECE // P)
+            if b == 0:
+                loads[unit] = bank(LOAD_BANKS[unit % 4])
+            nc.tensor.matmul_mx(
+                loads[unit][:],
+                lhsT=wb_c[b][:, P * nt : P * (nt + 1)].bitcast(FP8X4),
+                lhsT_scale=wb_s[b, piece][:, P * part : P * (part + 1)],
+                rhs=z_c[b, hf][:].bitcast(FP8X4),
+                rhs_scale=z_s[b, hf],
+                start=(b == 0),
+                stop=(b == 1),
+            )
+
+        def spend_pass(unit, b):
+            hf, nt = UNIT_PLACES[unit]
+            if b == 0:
+                spends[unit] = bank(SPEND_BANKS[unit % 4])
+            nc.tensor.matmul_mx(
+                spends[unit][:],
+                lhsT=wa_w[b][:].bitcast(U8)[:, 2 * P * nt : 2 * P * (nt + 1)].bitcast(FP4X4),
+                lhsT_scale=wa_s[:, b, :].bitcast(U8)[:, P * nt : P * (nt + 1)],
+                rhs=z_c[b, hf][:].bitcast(FP8X4),
+                rhs_scale=z_s[b, hf],
+                start=(b == 0),
+                stop=(b == 1),
+            )
 
         def contention(unit):
-            hf, nt = divmod(unit, N // P)
-            piece, part = divmod(nt, WB_PIECE // P)
-            load = bank(UNIT_BANKS[unit % 4][0])
             for b in range(2):
-                nc.tensor.matmul_mx(
-                    load[:],
-                    lhsT=wb_c[b][:, P * nt : P * (nt + 1)].bitcast(FP8X4),
-                    lhsT_scale=wb_s[b, piece][:, P * part : P * (part + 1)],
-                    rhs=z_c[b, hf][:].bitcast(FP8X4),
-                    rhs_scale=z_s[b, hf][:],
-                    start=(b == 0),
-                    stop=(b == 1),
-                )
-            work[unit] = keep("work%d" % unit, [P, 3, BANK], F32, after=WORK_TAGS[unit % len(WORK_TAGS)])
-            nc.scalar.activation(work[unit][:, 0, :], load[:], ACT.Square)
+                if b == 1 or unit not in loads:
+                    load_pass(unit, b)
+            if unit % 2 == 0:
+                work[unit // 2] = keep("work%d" % unit, [P, 2, 2 * BANK], F32, after=WORK_TAGS[unit // 2])
+            nc.scalar.activation(scratch(unit, 0), loads[unit][:], ACT.Square)
 
-        def finish(unit):
-            hf, nt = divmod(unit, N // P)
-            rows = slice(P * nt, P * (nt + 1))
-            spend = bank(UNIT_BANKS[unit % 4][1])
-            for b in range(2):
-                nc.tensor.matmul_mx(
-                    spend[:],
-                    lhsT=wa_w[b][:].bitcast(U8)[:, 2 * P * nt : 2 * P * (nt + 1)].bitcast(FP4X4),
-                    lhsT_scale=wa_s[:, b, :].bitcast(U8)[:, rows],
-                    rhs=z_c[b, hf][:].bitcast(FP8X4),
-                    rhs_scale=z_s[b, hf][:],
-                    start=(b == 0),
-                    stop=(b == 1),
-                )
-            square, root, between = [work[unit][:, n, :] for n in range(3)]
-            nc.scalar.activation(root, square, ACT.Abs_reciprocal_sqrt, bias=ones[:])
-            res = keep("res%d" % unit, [P, BANK], F32, after="prior%d" % (unit % len(prior_sb)))
-            if unit < UNITS - SQUARED_ON_SCALAR:
-                nc.vector.tensor_tensor(between, spend[:], root, MULT)
-                nc.vector.tensor_tensor(res[:], between, root, MULT)
+        def scratch(unit, row):
+            return work[unit // 2][:, row, BANK * (unit % 2) : BANK * (unit % 2 + 1)]
+
+        def damp(unit, apart):
+            if apart:
+                for one in (unit, unit + 1):
+                    nc.scalar.activation(scratch(one, 1), scratch(one, 0), ACT.Abs_reciprocal_sqrt, bias=ones[:])
             else:
-                nc.scalar.activation(between, root, ACT.Square)
-                nc.vector.tensor_tensor(res[:], spend[:], between, MULT)
-            nc.sync.dma_start(out[rows, BANK * hf : BANK * (hf + 1)], res[:])
+                both = work[unit // 2]
+                nc.scalar.activation(both[:, 1, :], both[:, 0, :], ACT.Abs_reciprocal_sqrt, bias=ones[:])
+
+        def first_product(unit):
+            for b in range(2):
+                if b == 1 or unit not in spends:
+                    spend_pass(unit, b)
+            nc.vector.tensor_tensor(scratch(unit, 0), spends[unit][:], scratch(unit, 1), MULT)
+
+        def second_product(unit, engine):
+            hf, nt = UNIT_PLACES[unit]
+            res = keep("res%d" % unit, [P, BANK], F32, after=RES_TAGS[unit])
+            engine.tensor_tensor(res[:], scratch(unit, 0), scratch(unit, 1), MULT)
+            nc.sync.dma_start(out[P * nt : P * (nt + 1), BANK * hf : BANK * (hf + 1)], res[:])
+
+        def one_product(unit, pieces):
+            hf, nt = UNIT_PLACES[unit]
+            for b in range(2):
+                spend_pass(unit, b)
+            for piece in range(pieces):
+                width = BANK // pieces
+                cols = slice(width * piece, width * (piece + 1))
+                res = keep("res%d_%d" % (unit, piece), [P, width], F32, after=RES_TAGS[unit + piece])
+                nc.scalar.activation(scratch(unit, 0)[:, cols], scratch(unit, 1)[:, cols], ACT.Square)
+                nc.vector.tensor_tensor(res[:], spends[unit][:, cols], scratch(unit, 0)[:, cols], MULT)
+                nc.sync.dma_start(out[P * nt : P * (nt + 1), BANK * hf : BANK * (hf + 1)][:, cols], res[:])
 
         whole = slice(0, S)
         halves = (slice(0, S // 2), slice(S // 2, S))
@@ -279,78 +338,117 @@ def tile_list_listing_budget_pacer_kernel(
         for half in halves:
             offsets = idx[:, half.start // 16 : half.stop // 16]
             nc.vector.tensor_copy(v_w[1][:, half], tab_w[1][:].bitcast(U32).indirect(offsets))
-        for half, number in zip(halves, (H_BANKS[0], SUM_BANK)):
+        for half, number in zip(halves, (0, 2)):
             make_h(0, number, half, (0, 1))
             fetch_h(0, half)
             place(0, half)
-        for s in range(1, PACK):
-            make_h(s, H_BANKS[s], whole, (1, 0))
+        for s, number in ((1, 1), (2, 6), (3, 7)):
+            make_h(s, number, whole, (1, 0))
         fetch_h(1, whole)
 
-        open_sums()
-        add_turned(0, pages[0], first=True)
-        add_turned(0, prior_sb[0])
+        banks = [bank(number) for number in (2, 3, 4, 5)]
+        add_turned(pages[0], range(8), pair_regions(banks, 0), first=True)
+        add_turned(prior_sb[0], range(8), pair_regions(banks, 0))
+        add_turned(prior_sb[1], range(8), pair_regions(banks, 1))
         place(1, whole)
         quantise_w1(0, 1)
         quantise_w1(1, 1, after="w1_c10")
         fetch_h(2, whole, after="w1_raw11")
         fetch_h(3, whole, after="w1_c10")
-        add_turned(1, prior_sb[1])
-        add_turned(1, pages[1], last=True)
+        new_z_t(0, "z_t00")
+        close_pair(0, banks)
         place(2, whole)
-        for s in range(PACK, 2 * PACK):
-            make_h(s, H_BANKS[s % PACK], whole, (1, 0))
+        for s, number in ((4, 0), (5, 1)):
+            make_h(s, number, whole, (1, 0))
             fetch_h(s, whole)
-        round_wb(0, 0)
-        open_sums()
-        add_turned(2, pages[0], first=True)
-        add_turned(2, prior_sb[2])
-        round_wb(0, 1, after="w1_c01")
-        round_wb(0, 2, after="w1_c11")
+        banks = add_pair(2, (2, 3, 4, 5))
+        add_turned(pages[2], range(8), pair_regions(banks, 0))
+        for piece in range(2):
+            round_wb(0, piece)
         place(3, whole)
-        add_turned(3, prior_sb[3])
-        add_turned(3, pages[1], last=True)
-        turn_back(0)
+        new_z_t(1, "z_t01", "wb_raw01")
+        close_pair(2, banks)
+        for s, number in ((6, 2), (7, 3)):
+            make_h(s, number, whole, (1, 0))
+            fetch_h(s, whole)
+        for quarter, number in enumerate((6, 7, 0, 1)):
+            fetch_words(0, quarter, turn_words(quarter, bank(number), (0, 1)))
 
         place(4, whole)
-        quantise_wb(0, 0)
-        for piece, tag in enumerate(("z_t00", "z_t01", "wb_raw0")):
-            round_wb(1, piece, after=tag)
+        banks = add_pair(4, (4, 5, 2, 7))
+        add_turned(pages[4 % PAGES], range(8), pair_regions(banks, 0))
         place(5, whole)
-        open_sums()
-        add_turned(4, pages[0], first=True)
-        add_turned(4, prior_sb[4])
-        add_turned(5, prior_sb[5])
-        add_turned(5, pages[1], last=True)
-        z_s[0, 0] = keep("z_s00", [P, BANK], U8, after="h4")
-        quantise_z(0, 0)
-        quantise_z(0, 1)
+        new_z_t(0, "z_t10")
+        close_pair(4, banks)
+        round_wb(1, 0, after="prior5")
+        backs = {}
         place(6, whole)
-        open_sums()
-        add_turned(6, prior_sb[6], first=True)
-        add_turned(7, prior_sb[7])
-        add_turned(6, pages[0])
-        place(7, whole)
-        add_turned(7, pages[1], last=True)
-        turn_back(1)
 
-        z_s[1, 0] = keep("z_s10", [P, BANK], U8)
-        z_s[1, 1] = keep("z_s11", [P, BANK], U8)
-        quantise_wb(1, 0, after="h7")
-        quantise_wb(0, 1, after="wgs_sb")
+        def slice_alone(hf, number, back_numbers):
+            blocks = range(4 * hf, 4 * hf + 4)
+            alone = bank(number)
+            add_turned(prior_sb[6], blocks, lambda block: (alone, block % 4), first=True)
+            add_turned(pages[6 % PAGES], blocks, lambda block: (alone, block % 4), last=True)
+            nc.scalar.copy(z_t[1, hf].rearrange("m (x e) -> m x e", e=2)[:, :, 0], alone[:])
+            for part in range(2):
+                backs[2 * hf + part] = turn_words(2 * hf + part, bank(back_numbers[part]), (0, 1))
+
+        early = keep("early_s", [P, 2 * BANK], U8, after="h6")
+        z_s[0, 0] = early[:, 0:BANK]
+        quantise_z(0, 0)
+        slice_alone(0, 2, (0, 1))
+        slice_alone(1, 7, (4, 5))
+        fetch_words(1, 0, backs[0])
+        fetch_words(1, 1, backs[1])
+        round_wb(1, 1, after="wb_raw01")
+        fetch_words(1, 2, backs[2], after="wb_raw11")
+        fetch_words(1, 3, backs[3])
+        quantise_wb(0, 0, early[:, BANK : BANK + WB_PIECE])
+        quantise_wb(1, 0, early[:, BANK + WB_PIECE : 2 * BANK])
+        spend_pass(0, 0)
+        spend_pass(1, 0)
+        load_pass(0, 0)
+        load_pass(1, 0)
+        spend_pass(2, 0)
+        spend_pass(3, 0)
+        place(7, whole)
+
+        def add_last(hf):
+            nc.vector.tensor_tensor(
+                z_in[1, hf][:].rearrange("p (m i) -> p m i", i=PACK)[:, :, PACK - 1],
+                pages[LAST_SLICE % PAGES][:, HALF * hf : HALF * (hf + 1)],
+                prior_sb[LAST_SLICE][hf][:],
+                ADD,
+            )
+
+        z_s[1, 0] = keep("z_s10", [P, BANK], U8)[:]
+        z_s[1, 1] = keep("z_s11", [P, BANK], U8)[:]
+        add_last(0)
         quantise_z(1, 0)
+        rest = keep("late_s", [P, 2 * BANK], U8, after="prior7a")
+        quantise_wb(0, 1, rest[:, 0:WB_PIECE])
+        quantise_wb(1, 1, rest[:, WB_PIECE : 2 * WB_PIECE])
+        add_last(1)
         quantise_z(1, 1)
-        quantise_wb(1, 1, after="z_t00")
-        quantise_z(1, 2)
-        quantise_z(1, 3)
-        quantise_wb(0, 2, after="z_in11")
-        quantise_wb(1, 2, after="w1_c11")
-        z_s[0, 1] = keep("z_s01", [P, BANK], U8, after="wb_raw0")
-        quantise_z(0, 2)
-        quantise_z(0, 3)
+        z_s[0, 1] = keep("z_s01", [P, BANK], U8, after="prior7b")[:]
+        quantise_z(0, 1)
+        round_wb(0, 2, after="z_in10")
+        round_wb(1, 2, after="z_in01", copy=nc.vector.tensor_copy)
+        for b in range(2):
+            quantise_wb(b, 2, rest[:, BANK + WB_PIECE * b : BANK + WB_PIECE * (b + 1)])
 
         contention(0)
-        for unit in range(UNITS):
-            if unit + 1 < UNITS:
-                contention(unit + 1)
-            finish(unit)
+        contention(1)
+        for a in range(0, UNITS, 2):
+            last = a + 2 == UNITS
+            if not last:
+                contention(a + 2)
+            damp(a, last)
+            if not last:
+                contention(a + 3)
+                first_product(a)
+                first_product(a + 1)
+                second_product(a, nc.vector)
+                second_product(a + 1, nc.gpsimd if a // 2 in ON_GPSIMD else nc.vector)
+        one_product(UNITS - 2, 1)
+        one_product(UNITS - 1, 2)

@@ -29,9 +29,9 @@ UNITS = (N // P) * (T2 // BANK)
 PAGES = 3
 HALF = T2 // 2
 WORK_TAGS = ("w1_raw00", "w1_raw10", "w1_raw01", "w1_raw11", "tab_w0", "tab_w1")
-RES_TAGS = ["prior%d" % s for s in (0, 1, 2, 3, 4, 6, 5)] + ["h%d" % s for s in (0, 1, 4, 5, 7, 6)]
-LOAD_BANKS = (0, 1, 3, 6)
-SPEND_BANKS = (2, 7, 4, 5)
+RES_TAGS = ["prior%d" % s for s in (0, 1, 2, 3, 4, 6, 7, 5)] + ["h%d" % s for s in (0, 1, 4, 5, 6)]
+LOAD_BANKS = (1, 3, 0, 6, 4, 5, 0, 6, 4, 5, 0, 6)
+SPEND_BANKS = (2, 7, 1, 3)
 UNIT_PLACES = [(hf, nt) for nts in (range(4), range(4, 6)) for hf in range(2) for nt in nts]
 ON_GPSIMD = ()
 
@@ -59,8 +59,7 @@ def tile_list_listing_budget_pacer_kernel(
         wa_w = [keep("wa_w%d" % b, [P, 2 * N // 4], I32) for b in range(2)]
         wgs_sb = keep("wgs_sb", [P, S], F32)
         pages = [keep("page%d" % e, [P, T2], F32) for e in range(PAGES)]
-        prior_sb = [keep("prior%d" % s, [P, T2], F32) for s in range(LAST_SLICE)]
-        prior_sb.append([keep("prior7" + hf, [P, HALF], F32) for hf in "ab"])
+        prior_sb = [keep("prior%d" % s, [P, T2], F32) for s in range(H // P)]
         wb_raw = {}
 
         nc.vector.memset(tab_s[:], 0)
@@ -85,11 +84,7 @@ def tile_list_listing_budget_pacer_kernel(
         def load_prior(s):
             b, i = divmod(s, PACK)
             part = prior[KP * b : KP * (b + 1), :].rearrange("(p i) m -> p i m", i=PACK)
-            if s < LAST_SLICE:
-                nc.sync.dma_start(prior_sb[s][:], part[:, i, :])
-            else:
-                for hf in range(2):
-                    nc.sync.dma_start(prior_sb[s][hf][:], part[:, i, HALF * hf : HALF * (hf + 1)])
+            nc.sync.dma_start(prior_sb[s][:], part[:, i, :])
 
         def load_wb(b, piece):
             wb_raw[b, piece] = keep("wb_raw%d%d" % (b, piece), [P, PACK, WB_PIECE], F32)
@@ -110,12 +105,13 @@ def tile_list_listing_budget_pacer_kernel(
         load_prior(2)
         load_prior(3)
         load_wb(0, 0)
-        load_wb(0, 1)
         load_wb(1, 0)
         load_prior(4)
         load_prior(5)
+        load_wb(0, 1)
         load_wb(1, 1)
         load_prior(6)
+        load_prior(7)
         for quad in range(4):
             nc.sync.dma_start(
                 wa_s[32 * quad : 32 * quad + 4, :, :],
@@ -123,7 +119,6 @@ def tile_list_listing_budget_pacer_kernel(
             )
         for b in range(2):
             nc.sync.dma_start(wa_w[b][:], wa_words[b].bitcast(I32))
-        load_prior(LAST_SLICE)
         load_wb(0, 2)
         load_wb(1, 2)
 
@@ -239,11 +234,11 @@ def tile_list_listing_budget_pacer_kernel(
                     )
             return back
 
-        def fetch_words(b, quarter, back, after=None):
+        def fetch_words(b, quarter, back, copy, after=None):
             hf, part = divmod(quarter, 2)
             if part == 0:
                 z_in[b, hf] = keep("z_in%d%d" % (b, hf), [P, PACK * HALF], BF16, after=after)
-            nc.scalar.copy(
+            copy(
                 z_in[b, hf][:].bitcast(F32)[:, BANK * part : BANK * (part + 1)].rearrange("p (m u) -> p m u", u=2),
                 back[:].rearrange("p (u m) -> p m u", u=2),
             )
@@ -251,13 +246,19 @@ def tile_list_listing_budget_pacer_kernel(
         def quantise_z(b, hf):
             nc.vector.quantize_mx(z_c[b, hf][:].bitcast(FP8X4), z_s[b, hf], z_in[b, hf][:])
 
+        def quantise_z_quarter(b, quarter):
+            hf, part = divmod(quarter, 2)
+            cols = slice(QUARTER * part, QUARTER * (part + 1))
+            source = z_in[b, hf][:, PACK * QUARTER * part : PACK * QUARTER * (part + 1)]
+            nc.vector.quantize_mx(z_c[b, hf][:, cols].bitcast(FP8X4), z_s[b, hf][:, cols], source)
+
         work, loads, spends = {}, {}, {}
 
         def load_pass(unit, b):
             hf, nt = UNIT_PLACES[unit]
             piece, part = divmod(nt, WB_PIECE // P)
             if b == 0:
-                loads[unit] = bank(LOAD_BANKS[unit % 4])
+                loads[unit] = bank(LOAD_BANKS[unit])
             nc.tensor.matmul_mx(
                 loads[unit][:],
                 lhsT=wb_c[b][:, P * nt : P * (nt + 1)].bitcast(FP8X4),
@@ -363,16 +364,16 @@ def tile_list_listing_budget_pacer_kernel(
             fetch_h(s, whole)
         banks = add_pair(2, (2, 3, 4, 5))
         add_turned(pages[2], range(8), pair_regions(banks, 0))
-        for piece in range(2):
-            round_wb(0, piece)
+        for b in range(2):
+            round_wb(b, 0)
         place(3, whole)
-        new_z_t(1, "z_t01", "wb_raw01")
+        new_z_t(1, "z_t01", "wb_raw10")
         close_pair(2, banks)
         for s, number in ((6, 2), (7, 3)):
             make_h(s, number, whole, (1, 0))
             fetch_h(s, whole)
         for quarter, number in enumerate((6, 7, 0, 1)):
-            fetch_words(0, quarter, turn_words(quarter, bank(number), (0, 1)))
+            fetch_words(0, quarter, turn_words(quarter, bank(number), (0, 1)), nc.scalar.copy)
 
         place(4, whole)
         banks = add_pair(4, (4, 5, 2, 7))
@@ -380,60 +381,46 @@ def tile_list_listing_budget_pacer_kernel(
         place(5, whole)
         new_z_t(0, "z_t10")
         close_pair(4, banks)
-        round_wb(1, 0, after="prior5")
-        backs = {}
+        round_wb(0, 1, after="prior5")
+        round_wb(1, 1, after="wb_raw01")
+        backs = [turn_words(quarter, bank(number), (0,)) for quarter, number in enumerate((4, 5, 2, 7))]
+        banks = add_pair(6, (0, 1, 3, 6))
         place(6, whole)
-
-        def slice_alone(hf, number, back_numbers):
-            blocks = range(4 * hf, 4 * hf + 4)
-            alone = bank(number)
-            add_turned(prior_sb[6], blocks, lambda block: (alone, block % 4), first=True)
-            add_turned(pages[6 % PAGES], blocks, lambda block: (alone, block % 4), last=True)
-            nc.scalar.copy(z_t[1, hf].rearrange("m (x e) -> m x e", e=2)[:, :, 0], alone[:])
-            for part in range(2):
-                backs[2 * hf + part] = turn_words(2 * hf + part, bank(back_numbers[part]), (0, 1))
-
-        early = keep("early_s", [P, 2 * BANK], U8, after="h6")
+        add_turned(pages[6 % PAGES], range(8), pair_regions(banks, 0))
+        place(7, whole)
+        early = keep("early_s", [P, 2 * BANK], U8, after="h7")
         z_s[0, 0] = early[:, 0:BANK]
         quantise_z(0, 0)
-        slice_alone(0, 2, (0, 1))
-        slice_alone(1, 7, (4, 5))
-        fetch_words(1, 0, backs[0])
-        fetch_words(1, 1, backs[1])
-        round_wb(1, 1, after="wb_raw01")
-        fetch_words(1, 2, backs[2], after="wb_raw11")
-        fetch_words(1, 3, backs[3])
         quantise_wb(0, 0, early[:, BANK : BANK + WB_PIECE])
         quantise_wb(1, 0, early[:, BANK + WB_PIECE : 2 * BANK])
-        spend_pass(0, 0)
-        spend_pass(1, 0)
+        new_z_t(1, "z_t11", "wb_raw11")
+        for quarter in range(4):
+            add_turned(pages[7 % PAGES], (2 * quarter, 2 * quarter + 1), pair_regions(banks, 1), last=True)
+        round_pair(1, 0, banks[0], nc.scalar.copy)
+        round_pair(1, 1, banks[1], nc.vector.tensor_copy)
+        round_pair(1, 2, banks[2], nc.scalar.copy)
+        for quarter in range(3):
+            turn_words(quarter, backs[quarter], (1,))
+        fetch_words(1, 0, backs[0], nc.scalar.copy)
+        fetch_words(1, 1, backs[1], nc.vector.tensor_copy)
+        round_pair(1, 3, banks[3], nc.scalar.copy)
+        turn_words(3, backs[3], (1,))
+        fetch_words(1, 2, backs[2], nc.scalar.copy)
+        fetch_words(1, 3, backs[3], nc.scalar.copy)
         load_pass(0, 0)
         load_pass(1, 0)
-        spend_pass(2, 0)
-        spend_pass(3, 0)
-        place(7, whole)
-
-        def add_last(hf):
-            nc.vector.tensor_tensor(
-                z_in[1, hf][:].rearrange("p (m i) -> p m i", i=PACK)[:, :, PACK - 1],
-                pages[LAST_SLICE % PAGES][:, HALF * hf : HALF * (hf + 1)],
-                prior_sb[LAST_SLICE][hf][:],
-                ADD,
-            )
-
         z_s[1, 0] = keep("z_s10", [P, BANK], U8)[:]
         z_s[1, 1] = keep("z_s11", [P, BANK], U8)[:]
-        add_last(0)
-        quantise_z(1, 0)
-        rest = keep("late_s", [P, 2 * BANK], U8, after="prior7a")
+        quantise_z_quarter(1, 0)
+        quantise_z_quarter(1, 1)
+        rest = keep("late_s", [P, 3 * BANK], U8, after="z_in10")
         quantise_wb(0, 1, rest[:, 0:WB_PIECE])
         quantise_wb(1, 1, rest[:, WB_PIECE : 2 * WB_PIECE])
-        add_last(1)
-        quantise_z(1, 1)
-        z_s[0, 1] = keep("z_s01", [P, BANK], U8, after="prior7b")[:]
+        z_s[0, 1] = rest[:, 2 * BANK : 3 * BANK]
         quantise_z(0, 1)
-        round_wb(0, 2, after="z_in10")
-        round_wb(1, 2, after="z_in01", copy=nc.vector.tensor_copy)
+        quantise_z(1, 1)
+        for b in range(2):
+            round_wb(b, 2, after="z_in%d1" % b, copy=nc.vector.tensor_copy)
         for b in range(2):
             quantise_wb(b, 2, rest[:, BANK + WB_PIECE * b : BANK + WB_PIECE * (b + 1)])
 

@@ -29,11 +29,11 @@ UNITS = (N // P) * (T2 // BANK)
 PAGES = 3
 HALF = T2 // 2
 WORK_TAGS = ("w1_raw00", "w1_raw10", "w1_raw01", "w1_raw11", "tab_w0", "tab_w1")
-RES_TAGS = ["prior%d" % s for s in (0, 1, 2, 3, 4, 6, 7, 5)] + ["h%d" % s for s in (0, 1, 4, 5, 6)]
-LOAD_BANKS = (1, 3, 0, 6, 4, 5, 0, 6, 4, 5, 0, 6)
-SPEND_BANKS = (2, 7, 1, 3)
+RES_TAGS = ["prior%d" % s for s in (0, 1, 2, 3, 6, 7, 4, 5)] + ["h%d" % s for s in (0, 1, 4, 5, 6)]
+LOAD_BANKS = (3, 6, 0, 1, 4, 5, 0, 1, 4, 5, 0, 1)
+SPEND_BANKS = (2, 7, 3, 6)
 UNIT_PLACES = [(hf, nt) for nts in (range(4), range(4, 6)) for hf in range(2) for nt in nts]
-ON_GPSIMD = ()
+SQUARED_ON_SCALAR = 2
 
 
 def tile_list_listing_budget_pacer_kernel(
@@ -111,6 +111,7 @@ def tile_list_listing_budget_pacer_kernel(
         load_wb(0, 1)
         load_wb(1, 1)
         load_prior(6)
+        load_wb(0, 2)
         load_prior(7)
         for quad in range(4):
             nc.sync.dma_start(
@@ -119,7 +120,6 @@ def tile_list_listing_budget_pacer_kernel(
             )
         for b in range(2):
             nc.sync.dma_start(wa_w[b][:], wa_words[b].bitcast(I32))
-        load_wb(0, 2)
         load_wb(1, 2)
 
         w1_c, w1_s = {}, {}
@@ -252,7 +252,7 @@ def tile_list_listing_budget_pacer_kernel(
             source = z_in[b, hf][:, PACK * QUARTER * part : PACK * QUARTER * (part + 1)]
             nc.vector.quantize_mx(z_c[b, hf][:, cols].bitcast(FP8X4), z_s[b, hf][:, cols], source)
 
-        work, loads, spends = {}, {}, {}
+        work, loads, spends, squared = {}, {}, {}, set()
 
         def load_pass(unit, b):
             hf, nt = UNIT_PLACES[unit]
@@ -284,6 +284,9 @@ def tile_list_listing_budget_pacer_kernel(
             )
 
         def contention(unit):
+            if unit in squared:
+                return
+            squared.add(unit)
             for b in range(2):
                 if b == 1 or unit not in loads:
                     load_pass(unit, b)
@@ -294,13 +297,12 @@ def tile_list_listing_budget_pacer_kernel(
         def scratch(unit, row):
             return work[unit // 2][:, row, BANK * (unit % 2) : BANK * (unit % 2 + 1)]
 
-        def damp(unit, apart):
-            if apart:
-                for one in (unit, unit + 1):
-                    nc.scalar.activation(scratch(one, 1), scratch(one, 0), ACT.Abs_reciprocal_sqrt, bias=ones[:])
+        def damp(group):
+            if len(group) == 1:
+                square, root = scratch(group[0], 0), scratch(group[0], 1)
             else:
-                both = work[unit // 2]
-                nc.scalar.activation(both[:, 1, :], both[:, 0, :], ACT.Abs_reciprocal_sqrt, bias=ones[:])
+                square, root = work[group[0] // 2][:, 0, :], work[group[0] // 2][:, 1, :]
+            nc.scalar.activation(root, square, ACT.Abs_reciprocal_sqrt, bias=ones[:])
 
         def first_product(unit):
             for b in range(2):
@@ -382,31 +384,29 @@ def tile_list_listing_budget_pacer_kernel(
         new_z_t(0, "z_t10")
         close_pair(4, banks)
         round_wb(0, 1, after="prior5")
-        round_wb(1, 1, after="wb_raw01")
+        round_wb(1, 1, after="prior4")
+        round_wb(0, 2, after="w1_c01")
         backs = [turn_words(quarter, bank(number), (0,)) for quarter, number in enumerate((4, 5, 2, 7))]
         banks = add_pair(6, (0, 1, 3, 6))
         place(6, whole)
         add_turned(pages[6 % PAGES], range(8), pair_regions(banks, 0))
         place(7, whole)
-        early = keep("early_s", [P, 2 * BANK], U8, after="h7")
-        z_s[0, 0] = early[:, 0:BANK]
+        z_s[0, 0] = keep("z_s00", [P, BANK], U8, after="h7")[:]
         quantise_z(0, 0)
-        quantise_wb(0, 0, early[:, BANK : BANK + WB_PIECE])
-        quantise_wb(1, 0, early[:, BANK + WB_PIECE : 2 * BANK])
-        new_z_t(1, "z_t11", "wb_raw11")
+        new_z_t(1, "z_t11")
         for quarter in range(4):
             add_turned(pages[7 % PAGES], (2 * quarter, 2 * quarter + 1), pair_regions(banks, 1), last=True)
-        round_pair(1, 0, banks[0], nc.scalar.copy)
-        round_pair(1, 1, banks[1], nc.vector.tensor_copy)
-        round_pair(1, 2, banks[2], nc.scalar.copy)
-        for quarter in range(3):
+        round_pair(1, 0, banks[0], nc.vector.tensor_copy)
+        for quarter in range(1, 4):
+            round_pair(1, quarter, banks[quarter], nc.scalar.copy)
+        first = keep("first_s", [P, BANK], U8, after="page1")
+        quantise_wb(0, 0, first[:, 0:WB_PIECE])
+        quantise_wb(1, 0, first[:, WB_PIECE:BANK])
+        for quarter in range(4):
             turn_words(quarter, backs[quarter], (1,))
-        fetch_words(1, 0, backs[0], nc.scalar.copy)
-        fetch_words(1, 1, backs[1], nc.vector.tensor_copy)
-        round_pair(1, 3, banks[3], nc.scalar.copy)
-        turn_words(3, backs[3], (1,))
-        fetch_words(1, 2, backs[2], nc.scalar.copy)
-        fetch_words(1, 3, backs[3], nc.scalar.copy)
+        fetch_words(1, 0, backs[0], nc.vector.tensor_copy)
+        for quarter in range(1, 4):
+            fetch_words(1, quarter, backs[quarter], nc.scalar.copy)
         load_pass(0, 0)
         load_pass(1, 0)
         z_s[1, 0] = keep("z_s10", [P, BANK], U8)[:]
@@ -419,23 +419,26 @@ def tile_list_listing_budget_pacer_kernel(
         z_s[0, 1] = rest[:, 2 * BANK : 3 * BANK]
         quantise_z(0, 1)
         quantise_z(1, 1)
-        for b in range(2):
-            round_wb(b, 2, after="z_in%d1" % b, copy=nc.vector.tensor_copy)
+        round_wb(1, 2, after="z_in01", copy=nc.vector.tensor_copy)
         for b in range(2):
             quantise_wb(b, 2, rest[:, BANK + WB_PIECE * b : BANK + WB_PIECE * (b + 1)])
 
+        groups = [(0,), (1,)] + [(a, a + 1) for a in range(2, UNITS - 2, 2)] + [(UNITS - 2,), (UNITS - 1,)]
         contention(0)
-        contention(1)
-        for a in range(0, UNITS, 2):
-            last = a + 2 == UNITS
-            if not last:
-                contention(a + 2)
-            damp(a, last)
-            if not last:
-                contention(a + 3)
-                first_product(a)
-                first_product(a + 1)
-                second_product(a, nc.vector)
-                second_product(a + 1, nc.gpsimd if a // 2 in ON_GPSIMD else nc.vector)
-        one_product(UNITS - 2, 1)
+        for group in groups:
+            if group[-1] + 1 < UNITS:
+                contention(group[-1] + 1)
+            damp(group)
+            if len(group) == 2 and group[-1] + 2 < UNITS - 1 or group == (1,):
+                contention(group[-1] + 2)
+            if group[0] < UNITS - SQUARED_ON_SCALAR:
+                for unit in group:
+                    first_product(unit)
+                if group[0] < UNITS - 2:
+                    for unit in group:
+                        second_product(unit, nc.vector)
+        if SQUARED_ON_SCALAR == 2:
+            one_product(UNITS - 2, 1)
+        else:
+            second_product(UNITS - 2, nc.vector)
         one_product(UNITS - 1, 2)

@@ -15,7 +15,6 @@ U8 = mybir.dt.uint8
 FP8X4 = mybir.dt.float8_e4m3fn_x4
 FP4X4 = mybir.dt.float4_e2m1fn_x4
 MULT = mybir.AluOpType.mult
-ADD = mybir.AluOpType.add
 ACT = mybir.ActivationFunctionType
 
 P = 128
@@ -24,7 +23,6 @@ KP = P * PACK
 BANK = 512
 QUARTER = T2 // 4
 WB_PIECE = 256
-LAST_SLICE = H // P - 1
 UNITS = (N // P) * (T2 // BANK)
 PAGES = 3
 HALF = T2 // 2
@@ -33,7 +31,6 @@ RES_TAGS = ["prior%d" % s for s in (0, 1, 2, 3, 6, 7, 4, 5)] + ["h%d" % s for s 
 LOAD_BANKS = (3, 6, 0, 1, 4, 5, 0, 1, 4, 5, 0, 1)
 SPEND_BANKS = (2, 7, 3, 6)
 UNIT_PLACES = [(hf, nt) for nts in (range(4), range(4, 6)) for hf in range(2) for nt in nts]
-SQUARED_ON_SCALAR = 2
 
 
 def tile_list_listing_budget_pacer_kernel(
@@ -69,7 +66,7 @@ def tile_list_listing_budget_pacer_kernel(
                 tab_s[32 * quad : 32 * quad + 8, :], tab_scales[:, 4 * quad : 4 * quad + 4, :].bitcast(I32)
             )
         for page in pages:
-            nc.gpsimd.memset(page[:], 0.0)
+            nc.vector.memset(page[:], 0.0)
         make_identity(nc, ident[:])
         ones = keep("ones", [P, 1], F32)
         nc.scalar.activation(ones[:], pages[0][:, 0:1], ACT.Abs_reciprocal_sqrt, bias=1.0)
@@ -96,9 +93,10 @@ def tile_list_listing_budget_pacer_kernel(
         load_w1(1, 0)
         for a in range(2):
             nc.sync.dma_start(tab_w[a][:], tab_words[a].rearrange("p t i -> p (t i)").bitcast(I32))
-        nc.sync.dma_start(wgs_sb[:], wgs)
+        nc.sync.dma_start(wgs_sb[:, 0 : S // 2], wgs[:, 0 : S // 2])
         nc.sync.dma_start(idx2[:], offs2)
         load_w1(0, 1)
+        nc.sync.dma_start(wgs_sb[:, S // 2 : S], wgs[:, S // 2 : S])
         load_w1(1, 1)
         load_prior(0)
         load_prior(1)
@@ -111,7 +109,6 @@ def tile_list_listing_budget_pacer_kernel(
         load_wb(0, 1)
         load_wb(1, 1)
         load_prior(6)
-        load_wb(0, 2)
         load_prior(7)
         for quad in range(4):
             nc.sync.dma_start(
@@ -120,13 +117,14 @@ def tile_list_listing_budget_pacer_kernel(
             )
         for b in range(2):
             nc.sync.dma_start(wa_w[b][:], wa_words[b].bitcast(I32))
+        load_wb(0, 2)
         load_wb(1, 2)
 
         w1_c, w1_s = {}, {}
 
-        def quantise_w1(a, b, after=None, scales_after=None):
+        def quantise_w1(a, b, after=None, scales_after=None, copy=nc.scalar.copy):
             stage = keep("w1_stage%d%d" % (a, b), [P, PACK * KP], BF16, after=after)
-            nc.scalar.copy(
+            copy(
                 stage[:].rearrange("p (i c j) -> p c j i", i=PACK, j=PACK),
                 w1_raw[a, b][:].rearrange("p j (c i) -> p c j i", i=PACK),
             )
@@ -234,10 +232,10 @@ def tile_list_listing_budget_pacer_kernel(
                     )
             return back
 
-        def fetch_words(b, quarter, back, copy, after=None):
+        def fetch_words(b, quarter, back, copy):
             hf, part = divmod(quarter, 2)
             if part == 0:
-                z_in[b, hf] = keep("z_in%d%d" % (b, hf), [P, PACK * HALF], BF16, after=after)
+                z_in[b, hf] = keep("z_in%d%d" % (b, hf), [P, PACK * HALF], BF16)
             copy(
                 z_in[b, hf][:].bitcast(F32)[:, BANK * part : BANK * (part + 1)].rearrange("p (m u) -> p m u", u=2),
                 back[:].rearrange("p (u m) -> p m u", u=2),
@@ -306,14 +304,13 @@ def tile_list_listing_budget_pacer_kernel(
 
         def first_product(unit):
             for b in range(2):
-                if b == 1 or unit not in spends:
-                    spend_pass(unit, b)
+                spend_pass(unit, b)
             nc.vector.tensor_tensor(scratch(unit, 0), spends[unit][:], scratch(unit, 1), MULT)
 
-        def second_product(unit, engine):
+        def second_product(unit):
             hf, nt = UNIT_PLACES[unit]
             res = keep("res%d" % unit, [P, BANK], F32, after=RES_TAGS[unit])
-            engine.tensor_tensor(res[:], scratch(unit, 0), scratch(unit, 1), MULT)
+            nc.vector.tensor_tensor(res[:], scratch(unit, 0), scratch(unit, 1), MULT)
             nc.sync.dma_start(out[P * nt : P * (nt + 1), BANK * hf : BANK * (hf + 1)], res[:])
 
         def one_product(unit, pieces):
@@ -333,7 +330,7 @@ def tile_list_listing_budget_pacer_kernel(
 
         v_s = keep("v_s", [P, S], U8)
         nc.vector.tensor_copy(v_s[:], tab_s[:].bitcast(U8).indirect(idx[:]))
-        quantise_w1(0, 0)
+        quantise_w1(0, 0, copy=nc.vector.tensor_copy)
         v_w[0] = keep("v_w0", [P, S], U32, after="w1_stage00")
         nc.vector.tensor_copy(v_w[0][:], tab_w[0][:].bitcast(U32).indirect(idx[:]))
         quantise_w1(1, 0, scales_after="tab_w0")
@@ -341,19 +338,18 @@ def tile_list_listing_budget_pacer_kernel(
         for half in halves:
             offsets = idx[:, half.start // 16 : half.stop // 16]
             nc.vector.tensor_copy(v_w[1][:, half], tab_w[1][:].bitcast(U32).indirect(offsets))
-        for half, number in zip(halves, (0, 2)):
-            make_h(0, number, half, (0, 1))
-            fetch_h(0, half)
-            place(0, half)
-        for s, number in ((1, 1), (2, 6), (3, 7)):
+        for n, half in enumerate(halves):
+            for s in range(2):
+                make_h(s, 2 * n + s, half, (0, 1))
+                fetch_h(s, half)
+                place(s, half)
+        for s, number in ((2, 6), (3, 7)):
             make_h(s, number, whole, (1, 0))
-        fetch_h(1, whole)
 
         banks = [bank(number) for number in (2, 3, 4, 5)]
-        add_turned(pages[0], range(8), pair_regions(banks, 0), first=True)
-        add_turned(prior_sb[0], range(8), pair_regions(banks, 0))
+        add_turned(prior_sb[0], range(8), pair_regions(banks, 0), first=True)
+        add_turned(pages[0], range(8), pair_regions(banks, 0))
         add_turned(prior_sb[1], range(8), pair_regions(banks, 1))
-        place(1, whole)
         quantise_w1(0, 1)
         quantise_w1(1, 1, after="w1_c10")
         fetch_h(2, whole, after="w1_raw11")
@@ -385,7 +381,6 @@ def tile_list_listing_budget_pacer_kernel(
         close_pair(4, banks)
         round_wb(0, 1, after="prior5")
         round_wb(1, 1, after="prior4")
-        round_wb(0, 2, after="w1_c01")
         backs = [turn_words(quarter, bank(number), (0,)) for quarter, number in enumerate((4, 5, 2, 7))]
         banks = add_pair(6, (0, 1, 3, 6))
         place(6, whole)
@@ -419,7 +414,8 @@ def tile_list_listing_budget_pacer_kernel(
         z_s[0, 1] = rest[:, 2 * BANK : 3 * BANK]
         quantise_z(0, 1)
         quantise_z(1, 1)
-        round_wb(1, 2, after="z_in01", copy=nc.vector.tensor_copy)
+        for b in range(2):
+            round_wb(b, 2, after="z_in%d1" % b, copy=nc.vector.tensor_copy)
         for b in range(2):
             quantise_wb(b, 2, rest[:, BANK + WB_PIECE * b : BANK + WB_PIECE * (b + 1)])
 
@@ -431,14 +427,10 @@ def tile_list_listing_budget_pacer_kernel(
             damp(group)
             if len(group) == 2 and group[-1] + 2 < UNITS - 1 or group == (1,):
                 contention(group[-1] + 2)
-            if group[0] < UNITS - SQUARED_ON_SCALAR:
+            if group[0] < UNITS - 2:
                 for unit in group:
                     first_product(unit)
-                if group[0] < UNITS - 2:
-                    for unit in group:
-                        second_product(unit, nc.vector)
-        if SQUARED_ON_SCALAR == 2:
-            one_product(UNITS - 2, 1)
-        else:
-            second_product(UNITS - 2, nc.vector)
+                for unit in group:
+                    second_product(unit)
+        one_product(UNITS - 2, 1)
         one_product(UNITS - 1, 2)

@@ -61,10 +61,6 @@ def tile_list_listing_budget_pacer_kernel(
 
         nc.vector.memset(tab_s[:], 0)
         nc.vector.memset(wa_s[:], 0)
-        for quad in range(4):
-            nc.gpsimd.dma_start(
-                tab_s[32 * quad : 32 * quad + 8, :], tab_scales[:, 4 * quad : 4 * quad + 4, :].bitcast(I32)
-            )
         for page in pages:
             nc.vector.memset(page[:], 0.0)
         make_identity(nc, ident[:])
@@ -89,6 +85,10 @@ def tile_list_listing_budget_pacer_kernel(
             nc.sync.dma_start(wb_raw[b, piece][:], part.rearrange("(p j) c -> p j c", j=PACK))
 
         load_w1(0, 0)
+        for quad in range(4):
+            nc.sync.dma_start(
+                tab_s[32 * quad : 32 * quad + 8, :], tab_scales[:, 4 * quad : 4 * quad + 4, :].bitcast(I32)
+            )
         nc.sync.dma_start(idx[:], offs)
         load_w1(1, 0)
         for a in range(2):

@@ -26,10 +26,11 @@ WB_PIECE = 256
 UNITS = (N // P) * (T2 // BANK)
 PAGES = 3
 HALF = T2 // 2
-WORK_TAGS = ("w1_raw00", "w1_raw10", "w1_raw01", "w1_raw11", "tab_w0", "tab_w1")
-RES_TAGS = ["prior%d" % s for s in (0, 1, 2, 3, 6, 7, 4, 5)] + ["h%d" % s for s in (0, 1, 4, 5, 6)]
-LOAD_BANKS = (3, 6, 0, 1, 4, 5, 0, 1, 4, 5, 0, 1)
-SPEND_BANKS = (2, 7, 3, 6)
+WORK_TAGS = ("w1_raw00", "w1_raw10", "w1_raw01", "wb_raw00", "tab_w0", "tab_w1")
+RES_TAGS = ["prior%d" % s for s in (0, 1, 2, 3, 6, 7, 4, 5)] + ["h0", "h1", "h2", "wb_raw01", "wb_raw11"]
+SET_X, SET_Y = (2, 3, 4, 5), (0, 1, 6, 7)
+LOAD_BANKS = (4, 5, 2, 3, 0, 1, 2, 3, 0, 1, 2, 3)
+SPEND_BANKS = (6, 7, 4, 5)
 UNIT_PLACES = [(hf, nt) for nts in (range(4), range(4, 6)) for hf in range(2) for nt in nts]
 
 
@@ -39,6 +40,7 @@ def tile_list_listing_budget_pacer_kernel(
     nc = tc.nc
     with ExitStack() as ctx:
         held = ctx.enter_context(tc.tile_pool(name="held", bufs=1))
+        shared = ctx.enter_context(tc.tile_pool(name="shared", bufs=1))
         psum = ctx.enter_context(tc.psum_pool(name="psum", bufs=1))
 
         def keep(name, shape, dtype, after=None):
@@ -70,7 +72,10 @@ def tile_list_listing_budget_pacer_kernel(
         w1_raw = {}
 
         def load_w1(a, b):
-            w1_raw[a, b] = keep("w1_raw%d%d" % (a, b), [P, PACK, KP], F32)
+            if (a, b) == (1, 1):
+                w1_raw[a, b] = shared.tile([P, PACK, KP], F32, name="w1_last", offset=0)
+            else:
+                w1_raw[a, b] = keep("w1_raw%d%d" % (a, b), [P, PACK, KP], F32)
             part = w1[KP * a : KP * (a + 1), KP * b : KP * (b + 1)]
             nc.sync.dma_start(w1_raw[a, b][:], part.rearrange("(p j) c -> p j c", j=PACK))
 
@@ -80,7 +85,10 @@ def tile_list_listing_budget_pacer_kernel(
             nc.sync.dma_start(prior_sb[s][:], part[:, i, :])
 
         def load_wb(b, piece):
-            wb_raw[b, piece] = keep("wb_raw%d%d" % (b, piece), [P, PACK, WB_PIECE], F32)
+            if (b, piece) == (1, 0):
+                wb_raw[b, piece] = shared.tile([P, PACK, WB_PIECE], F32, name="wb_raw10", offset=14 * 1024)
+            else:
+                wb_raw[b, piece] = keep("wb_raw%d%d" % (b, piece), [P, PACK, WB_PIECE], F32)
             part = wb[KP * b : KP * (b + 1), WB_PIECE * piece : WB_PIECE * (piece + 1)]
             nc.sync.dma_start(wb_raw[b, piece][:], part.rearrange("(p j) c -> p j c", j=PACK))
 
@@ -93,23 +101,21 @@ def tile_list_listing_budget_pacer_kernel(
         load_w1(1, 0)
         for a in range(2):
             nc.sync.dma_start(tab_w[a][:], tab_words[a].rearrange("p t i -> p (t i)").bitcast(I32))
-        nc.sync.dma_start(wgs_sb[:, 0 : S // 2], wgs[:, 0 : S // 2])
+        nc.sync.dma_start(wgs_sb[:], wgs)
         nc.sync.dma_start(idx2[:], offs2)
         load_w1(0, 1)
-        nc.sync.dma_start(wgs_sb[:, S // 2 : S], wgs[:, S // 2 : S])
-        load_w1(1, 1)
         load_prior(0)
+        load_w1(1, 1)
         load_prior(1)
         load_prior(2)
         load_prior(3)
         load_wb(0, 0)
         load_wb(1, 0)
         load_prior(4)
-        load_prior(5)
+        load_prior(6)
         load_wb(0, 1)
         load_wb(1, 1)
-        load_prior(6)
-        load_prior(7)
+        load_prior(5)
         for quad in range(4):
             nc.sync.dma_start(
                 wa_s[32 * quad : 32 * quad + 4, :, :],
@@ -119,6 +125,7 @@ def tile_list_listing_budget_pacer_kernel(
             nc.sync.dma_start(wa_w[b][:], wa_words[b].bitcast(I32))
         load_wb(0, 2)
         load_wb(1, 2)
+        load_prior(7)
 
         w1_c, w1_s = {}, {}
 
@@ -167,9 +174,9 @@ def tile_list_listing_budget_pacer_kernel(
                     stop=(a == passes[1]),
                 )
 
-        def fetch_h(s, entries, after=None):
+        def fetch_h(s, entries, after=None, tile=None):
             if entries.start == 0:
-                h_sb[s] = keep("h%d" % s, [P, S], F32, after=after)
+                h_sb[s] = keep("h%d" % s, [P, S], F32, after=after)[:] if tile is None else tile
             nc.scalar.copy(h_sb[s][:, entries], h_ps[s, entries.start][:, entries])
 
         def place(s, entries):
@@ -178,8 +185,8 @@ def tile_list_listing_budget_pacer_kernel(
 
         z_t = {}
 
-        def new_z_t(pair, name, after=None):
-            both = keep(name, [P, 4 * BANK], BF16, after=after)
+        def new_z_t(pair, name, after=None, tile=None):
+            both = keep(name, [P, 4 * BANK], BF16, after=after) if tile is None else tile
             for hf in range(2):
                 z_t[pair, hf] = both[:, 2 * BANK * hf : 2 * BANK * (hf + 1)]
 
@@ -346,47 +353,51 @@ def tile_list_listing_budget_pacer_kernel(
         for s, number in ((2, 6), (3, 7)):
             make_h(s, number, whole, (1, 0))
 
-        banks = [bank(number) for number in (2, 3, 4, 5)]
+        fetch_h(2, whole)
+        place(2, whole)
+
+        banks = [bank(number) for number in SET_X]
         add_turned(prior_sb[0], range(8), pair_regions(banks, 0), first=True)
         add_turned(pages[0], range(8), pair_regions(banks, 0))
         add_turned(prior_sb[1], range(8), pair_regions(banks, 1))
         quantise_w1(0, 1)
-        quantise_w1(1, 1, after="w1_c10")
-        fetch_h(2, whole, after="w1_raw11")
-        fetch_h(3, whole, after="w1_c10")
-        new_z_t(0, "z_t00")
+        quantise_w1(1, 1)
+        fetch_h(3, whole, tile=shared.tile([P, S], F32, name="h3", offset=0)[:])
+        place(3, whole)
+        new_z_t(0, "z_t00", tile=shared.tile([P, 4 * BANK], BF16, name="z_t00", offset=4 * T2))
         close_pair(0, banks)
-        place(2, whole)
-        for s, number in ((4, 0), (5, 1)):
-            make_h(s, number, whole, (1, 0))
-            fetch_h(s, whole)
-        banks = add_pair(2, (2, 3, 4, 5))
+        banks = [bank(number) for number in SET_Y]
+        add_turned(prior_sb[2], range(8), pair_regions(banks, 0), first=True)
         add_turned(pages[2], range(8), pair_regions(banks, 0))
         for b in range(2):
             round_wb(b, 0)
-        place(3, whole)
-        new_z_t(1, "z_t01", "wb_raw10")
-        close_pair(2, banks)
-        for s, number in ((6, 2), (7, 3)):
+        h_late = shared.tile([P, PACK, S], F32, name="h_late", offset=8 * 1024)
+        for s, number in zip(range(4, 8), SET_X):
             make_h(s, number, whole, (1, 0))
-            fetch_h(s, whole)
-        for quarter, number in enumerate((6, 7, 0, 1)):
-            fetch_words(0, quarter, turn_words(quarter, bank(number), (0, 1)), nc.scalar.copy)
-
+            fetch_h(s, whole, tile=h_late[:, s - 4, :])
+        add_turned(prior_sb[3], range(8), pair_regions(banks, 1))
         place(4, whole)
-        banks = add_pair(4, (4, 5, 2, 7))
-        add_turned(pages[4 % PAGES], range(8), pair_regions(banks, 0))
+        new_z_t(1, "z_t01", tile=shared.tile([P, 4 * BANK], BF16, name="z_t01", offset=16 * 1024))
+        close_pair(2, banks)
         place(5, whole)
+        backs = [turn_words(quarter, bank(number), (0,)) for quarter, number in enumerate(SET_X)]
+        for quarter in range(4):
+            fetch_words(0, quarter, turn_words(quarter, backs[quarter], (1,)), nc.scalar.copy)
+
+        banks = add_pair(4, SET_Y)
+        add_turned(pages[4 % PAGES], range(8), pair_regions(banks, 0))
+        round_wb(0, 1)
         new_z_t(0, "z_t10")
         close_pair(4, banks)
-        round_wb(0, 1, after="prior5")
-        round_wb(1, 1, after="prior4")
-        backs = [turn_words(quarter, bank(number), (0,)) for quarter, number in enumerate((4, 5, 2, 7))]
-        banks = add_pair(6, (0, 1, 3, 6))
+        round_wb(1, 1)
         place(6, whole)
-        add_turned(pages[6 % PAGES], range(8), pair_regions(banks, 0))
         place(7, whole)
-        z_s[0, 0] = keep("z_s00", [P, BANK], U8, after="h7")[:]
+        backs = [turn_words(quarter, bank(number), (0,)) for quarter, number in enumerate(SET_Y)]
+        banks = add_pair(6, SET_X)
+        add_turned(pages[6 % PAGES], range(8), pair_regions(banks, 0))
+        for b in range(2):
+            round_wb(b, 2)
+        z_s[0, 0] = shared.tile([P, BANK], U8, name="z_s00", offset=8 * 1024, align_bytes=64)[:]
         quantise_z(0, 0)
         new_z_t(1, "z_t11")
         for quarter in range(4):
@@ -414,8 +425,6 @@ def tile_list_listing_budget_pacer_kernel(
         z_s[0, 1] = rest[:, 2 * BANK : 3 * BANK]
         quantise_z(0, 1)
         quantise_z(1, 1)
-        for b in range(2):
-            round_wb(b, 2, after="z_in%d1" % b, copy=nc.vector.tensor_copy)
         for b in range(2):
             quantise_wb(b, 2, rest[:, BANK + WB_PIECE * b : BANK + WB_PIECE * (b + 1)])
 

@@ -29,8 +29,10 @@ HALF = T2 // 2
 WORK_TAGS = ("w1_raw00", "w1_raw10", "w1_raw01", "wb_raw00", "tab_w0", "tab_w1")
 RES_TAGS = ["prior%d" % s for s in (0, 1, 2, 3, 6, 7, 4, 5)] + ["h0", "h1", "h2", "wb_raw01", "wb_raw11"]
 SET_X, SET_Y = (2, 3, 4, 5), (0, 1, 6, 7)
-LOAD_BANKS = (4, 5, 2, 3, 0, 1, 2, 3, 0, 1, 2, 3)
-SPEND_BANKS = (6, 7, 4, 5)
+SQUARED_ON_VECTOR = range(5, UNITS, 2)
+ON_GPSIMD = range(8)
+LOAD_BANKS = (4, 5, 2, 3) * 3
+SPEND_BANKS = (0, 1, 6, 7) * 3
 UNIT_PLACES = [(hf, nt) for nts in (range(4), range(4, 6)) for hf in range(2) for nt in nts]
 
 
@@ -139,22 +141,20 @@ def tile_list_listing_budget_pacer_kernel(
             w1_s[a, b] = keep("w1_s%d%d" % (a, b), [P, KP], U8, after=scales_after)
             nc.vector.quantize_mx(w1_c[a, b][:].bitcast(FP8X4), w1_s[a, b][:], stage[:])
 
-        wb_c = [keep("wb_c%d" % b, [P, N], U32) for b in range(2)]
-        wb_s, wb_stage = {}, {}
+        wb_c = [keep("wb_c%d" % piece, [P, 2 * WB_PIECE], U32) for piece in range(N // WB_PIECE)]
+        wb_stage = [keep("wb_stage%d" % piece, [P, 2, PACK * WB_PIECE], BF16) for piece in range(N // WB_PIECE)]
+        wb_s = {}
 
-        def round_wb(b, piece, after=None, copy=nc.scalar.copy):
-            wb_stage[b, piece] = keep("wb_stage%d%d" % (b, piece), [P, PACK * WB_PIECE], BF16, after=after)
-            copy(
-                wb_stage[b, piece][:].rearrange("p (c n j) -> p c j n", n=4, j=PACK),
+        def round_wb(b, piece):
+            nc.scalar.copy(
+                wb_stage[piece][:, b, :].rearrange("p (c n j) -> p c j n", n=4, j=PACK),
                 wb_raw[b, piece][:].rearrange("p j (c n) -> p c j n", n=4),
             )
 
-        def quantise_wb(b, piece, scales):
-            wb_s[b, piece] = scales
+        def quantise_wb(piece, scales):
+            wb_s[piece] = scales
             nc.vector.quantize_mx(
-                wb_c[b][:, WB_PIECE * piece : WB_PIECE * (piece + 1)].bitcast(FP8X4),
-                scales,
-                wb_stage[b, piece][:],
+                wb_c[piece][:].bitcast(FP8X4), scales, wb_stage[piece][:].rearrange("p b c -> p (b c)")
             )
 
         v_w, h_ps, h_sb = {}, {}, {}
@@ -251,86 +251,77 @@ def tile_list_listing_budget_pacer_kernel(
         def quantise_z(b, hf):
             nc.vector.quantize_mx(z_c[b, hf][:].bitcast(FP8X4), z_s[b, hf], z_in[b, hf][:])
 
-        def quantise_z_quarter(b, quarter):
-            hf, part = divmod(quarter, 2)
-            cols = slice(QUARTER * part, QUARTER * (part + 1))
-            source = z_in[b, hf][:, PACK * QUARTER * part : PACK * QUARTER * (part + 1)]
-            nc.vector.quantize_mx(z_c[b, hf][:, cols].bitcast(FP8X4), z_s[b, hf][:, cols], source)
-
-        work, loads, spends, squared = {}, {}, {}, set()
+        work, loads, spends = {}, {}, {}
 
         def load_pass(unit, b):
             hf, nt = UNIT_PLACES[unit]
             piece, part = divmod(nt, WB_PIECE // P)
-            if b == 0:
+            cols = slice(WB_PIECE * b + P * part, WB_PIECE * b + P * (part + 1))
+            first = unit not in loads
+            if first:
                 loads[unit] = bank(LOAD_BANKS[unit])
             nc.tensor.matmul_mx(
                 loads[unit][:],
-                lhsT=wb_c[b][:, P * nt : P * (nt + 1)].bitcast(FP8X4),
-                lhsT_scale=wb_s[b, piece][:, P * part : P * (part + 1)],
+                lhsT=wb_c[piece][:, cols].bitcast(FP8X4),
+                lhsT_scale=wb_s[piece][:, cols],
                 rhs=z_c[b, hf][:].bitcast(FP8X4),
                 rhs_scale=z_s[b, hf],
-                start=(b == 0),
-                stop=(b == 1),
+                start=first,
+                stop=not first,
             )
 
         def spend_pass(unit, b):
             hf, nt = UNIT_PLACES[unit]
-            if b == 0:
-                spends[unit] = bank(SPEND_BANKS[unit % 4])
+            if b == 1:
+                spends[unit] = bank(SPEND_BANKS[unit])
             nc.tensor.matmul_mx(
                 spends[unit][:],
                 lhsT=wa_w[b][:].bitcast(U8)[:, 2 * P * nt : 2 * P * (nt + 1)].bitcast(FP4X4),
                 lhsT_scale=wa_s[:, b, :].bitcast(U8)[:, P * nt : P * (nt + 1)],
                 rhs=z_c[b, hf][:].bitcast(FP8X4),
                 rhs_scale=z_s[b, hf],
-                start=(b == 0),
-                stop=(b == 1),
+                start=(b == 1),
+                stop=(b == 0),
             )
 
-        def contention(unit):
-            if unit in squared:
-                return
-            squared.add(unit)
-            for b in range(2):
-                if b == 1 or unit not in loads:
-                    load_pass(unit, b)
-            if unit % 2 == 0:
-                work[unit // 2] = keep("work%d" % unit, [P, 2, 2 * BANK], F32, after=WORK_TAGS[unit // 2])
-            nc.scalar.activation(scratch(unit, 0), loads[unit][:], ACT.Square)
-
         def scratch(unit, row):
+            if unit // 2 not in work:
+                work[unit // 2] = keep("work%d" % unit, [P, 2, 2 * BANK], F32, after=WORK_TAGS[unit // 2])
             return work[unit // 2][:, row, BANK * (unit % 2) : BANK * (unit % 2 + 1)]
 
-        def damp(group):
-            if len(group) == 1:
-                square, root = scratch(group[0], 0), scratch(group[0], 1)
+        def contention(unit):
+            for b in (1,) if unit in loads else (1, 0):
+                load_pass(unit, b)
+            if unit in SQUARED_ON_VECTOR:
+                nc.vector.tensor_copy(scratch(unit, 1), loads[unit][:])
+                nc.vector.tensor_tensor(scratch(unit, 0), loads[unit][:], scratch(unit, 1), MULT)
             else:
-                square, root = work[group[0] // 2][:, 0, :], work[group[0] // 2][:, 1, :]
-            nc.scalar.activation(root, square, ACT.Abs_reciprocal_sqrt, bias=ones[:])
+                nc.scalar.activation(scratch(unit, 0), loads[unit][:], ACT.Square)
+
+        def damp(unit):
+            nc.scalar.activation(scratch(unit, 1), scratch(unit, 0), ACT.Abs_reciprocal_sqrt, bias=ones[:])
+
+        def store(unit, res, cols):
+            hf, nt = UNIT_PLACES[unit]
+            nc.sync.dma_start(out[P * nt : P * (nt + 1), BANK * hf : BANK * (hf + 1)][:, cols], res)
 
         def first_product(unit):
-            for b in range(2):
+            for b in (1, 0):
                 spend_pass(unit, b)
             nc.vector.tensor_tensor(scratch(unit, 0), spends[unit][:], scratch(unit, 1), MULT)
 
-        def second_product(unit):
-            hf, nt = UNIT_PLACES[unit]
-            res = keep("res%d" % unit, [P, BANK], F32, after=RES_TAGS[unit])
-            nc.vector.tensor_tensor(res[:], scratch(unit, 0), scratch(unit, 1), MULT)
-            nc.sync.dma_start(out[P * nt : P * (nt + 1), BANK * hf : BANK * (hf + 1)], res[:])
+        def second_product(unit, engine, res, cols=slice(0, BANK)):
+            engine.tensor_tensor(res[:, cols], scratch(unit, 0)[:, cols], scratch(unit, 1)[:, cols], MULT)
+            store(unit, res[:, cols], cols)
 
-        def one_product(unit, pieces):
-            hf, nt = UNIT_PLACES[unit]
-            for b in range(2):
+        def one_product(unit, res, pieces):
+            for b in (1, 0):
                 spend_pass(unit, b)
             for piece in range(pieces):
-                width = BANK // pieces
-                cols = slice(width * piece, width * (piece + 1))
-                res = keep("res%d_%d" % (unit, piece), [P, width], F32, after=RES_TAGS[unit + piece])
+                cols = slice(BANK // pieces * piece, BANK // pieces * (piece + 1))
                 nc.scalar.activation(scratch(unit, 0)[:, cols], scratch(unit, 1)[:, cols], ACT.Square)
-                nc.vector.tensor_tensor(res[:], spends[unit][:, cols], scratch(unit, 0)[:, cols], MULT)
-                nc.sync.dma_start(out[P * nt : P * (nt + 1), BANK * hf : BANK * (hf + 1)][:, cols], res[:])
+                nc.vector.tensor_tensor(res[:, cols], spends[unit][:, cols], scratch(unit, 0)[:, cols], MULT)
+                store(unit, res[:, cols], cols)
 
         whole = slice(0, S)
         halves = (slice(0, S // 2), slice(S // 2, S))
@@ -399,47 +390,42 @@ def tile_list_listing_budget_pacer_kernel(
             round_wb(b, 2)
         z_s[0, 0] = shared.tile([P, BANK], U8, name="z_s00", offset=8 * 1024, align_bytes=64)[:]
         quantise_z(0, 0)
-        new_z_t(1, "z_t11")
+        for hf in range(2):
+            z_t[1, hf] = keep("z_t11%d" % hf, [P, 2 * BANK], BF16)[:]
         for quarter in range(4):
             add_turned(pages[7 % PAGES], (2 * quarter, 2 * quarter + 1), pair_regions(banks, 1), last=True)
         round_pair(1, 0, banks[0], nc.vector.tensor_copy)
         for quarter in range(1, 4):
             round_pair(1, quarter, banks[quarter], nc.scalar.copy)
         first = keep("first_s", [P, BANK], U8, after="page1")
-        quantise_wb(0, 0, first[:, 0:WB_PIECE])
-        quantise_wb(1, 0, first[:, WB_PIECE:BANK])
+        quantise_wb(0, first[:])
         for quarter in range(4):
             turn_words(quarter, backs[quarter], (1,))
         fetch_words(1, 0, backs[0], nc.vector.tensor_copy)
+        z_s[0, 1] = keep("z_s01", [P, BANK], U8, after="z_t110")[:]
+        quantise_z(0, 1)
         for quarter in range(1, 4):
             fetch_words(1, quarter, backs[quarter], nc.scalar.copy)
         load_pass(0, 0)
         load_pass(1, 0)
         z_s[1, 0] = keep("z_s10", [P, BANK], U8)[:]
         z_s[1, 1] = keep("z_s11", [P, BANK], U8)[:]
-        quantise_z_quarter(1, 0)
-        quantise_z_quarter(1, 1)
-        rest = keep("late_s", [P, 3 * BANK], U8, after="z_in10")
-        quantise_wb(0, 1, rest[:, 0:WB_PIECE])
-        quantise_wb(1, 1, rest[:, WB_PIECE : 2 * WB_PIECE])
-        z_s[0, 1] = rest[:, 2 * BANK : 3 * BANK]
-        quantise_z(0, 1)
+        quantise_z(1, 0)
+        rest = keep("late_s", [P, 2 * BANK], U8, after="z_in10")
+        quantise_wb(1, rest[:, 0:BANK])
         quantise_z(1, 1)
-        for b in range(2):
-            quantise_wb(b, 2, rest[:, BANK + WB_PIECE * b : BANK + WB_PIECE * (b + 1)])
+        quantise_wb(2, rest[:, BANK : 2 * BANK])
 
-        groups = [(0,), (1,)] + [(a, a + 1) for a in range(2, UNITS - 2, 2)] + [(UNITS - 2,), (UNITS - 1,)]
-        contention(0)
-        for group in groups:
-            if group[-1] + 1 < UNITS:
-                contention(group[-1] + 1)
-            damp(group)
-            if len(group) == 2 and group[-1] + 2 < UNITS - 1 or group == (1,):
-                contention(group[-1] + 2)
-            if group[0] < UNITS - 2:
-                for unit in group:
-                    first_product(unit)
-                for unit in group:
-                    second_product(unit)
-        one_product(UNITS - 2, 1)
-        one_product(UNITS - 1, 2)
+        started = set()
+        for unit in range(UNITS):
+            for other in range(min(UNITS, unit + 1 + 2)):
+                if other not in started and (other <= unit + 1 or other in SQUARED_ON_VECTOR):
+                    started.add(other)
+                    contention(other)
+            damp(unit)
+            res = keep("res%d" % unit, [P, BANK], F32, after=RES_TAGS[unit])[:]
+            if unit in ON_GPSIMD:
+                first_product(unit)
+                second_product(unit, nc.gpsimd, res)
+            else:
+                one_product(unit, res, 2 if unit == UNITS - 1 else 1)

@@ -29,8 +29,8 @@ HALF = T2 // 2
 WORK_TAGS = ("w1_raw00", "w1_raw10", "w1_raw01", "wb_raw00", "tab_w0", "tab_w1")
 RES_TAGS = ["prior%d" % s for s in (0, 1, 2, 3, 6, 7, 4, 5)] + ["h0", "h1", "h2", "wb_raw01", "wb_raw11"]
 SET_X, SET_Y = (2, 3, 4, 5), (0, 1, 6, 7)
-SQUARED_ON_VECTOR = range(5, UNITS, 2)
-ON_GPSIMD = range(8)
+SQUARED_ON_VECTOR = range(4, UNITS, 2)
+ON_GPSIMD = (0, 1, 2, 3, 4, 5, 6, 8)
 LOAD_BANKS = (4, 5, 2, 3) * 3
 SPEND_BANKS = (0, 1, 6, 7) * 3
 UNIT_PLACES = [(hf, nt) for nts in (range(4), range(4, 6)) for hf in range(2) for nt in nts]
@@ -251,7 +251,7 @@ def tile_list_listing_budget_pacer_kernel(
         def quantise_z(b, hf):
             nc.vector.quantize_mx(z_c[b, hf][:].bitcast(FP8X4), z_s[b, hf], z_in[b, hf][:])
 
-        work, loads, spends = {}, {}, {}
+        work, loads, spends, made = {}, {}, {}, set()
 
         def load_pass(unit, b):
             hf, nt = UNIT_PLACES[unit]
@@ -289,9 +289,14 @@ def tile_list_listing_budget_pacer_kernel(
                 work[unit // 2] = keep("work%d" % unit, [P, 2, 2 * BANK], F32, after=WORK_TAGS[unit // 2])
             return work[unit // 2][:, row, BANK * (unit % 2) : BANK * (unit % 2 + 1)]
 
+        def make_load(unit):
+            if unit not in made:
+                made.add(unit)
+                for b in (1,) if unit in loads else (1, 0):
+                    load_pass(unit, b)
+
         def contention(unit):
-            for b in (1,) if unit in loads else (1, 0):
-                load_pass(unit, b)
+            make_load(unit)
             if unit in SQUARED_ON_VECTOR:
                 nc.vector.tensor_copy(scratch(unit, 1), loads[unit][:])
                 nc.vector.tensor_tensor(scratch(unit, 0), loads[unit][:], scratch(unit, 1), MULT)
@@ -418,6 +423,8 @@ def tile_list_listing_budget_pacer_kernel(
 
         started = set()
         for unit in range(UNITS):
+            for other in range(min(UNITS, unit + 3 + 1)):
+                make_load(other)
             for other in range(min(UNITS, unit + 1 + 2)):
                 if other not in started and (other <= unit + 1 or other in SQUARED_ON_VECTOR):
                     started.add(other)

@@ -31,8 +31,8 @@ RES_TAGS = ["prior%d" % s for s in (0, 1, 2, 3, 6, 7, 4, 5)] + ["h0", "h1", "h2"
 SET_X, SET_Y = (2, 3, 4, 5), (0, 1, 6, 7)
 SQUARED_ON_VECTOR = range(4, UNITS, 2)
 ON_GPSIMD = (0, 1, 2, 3, 4, 5, 6, 8)
-LOAD_BANKS = (4, 5, 2, 3) * 3
-SPEND_BANKS = (0, 1, 6, 7) * 3
+LOAD_BANKS = (4, 0, 2, 3) * 3
+SPEND_BANKS = (1, 5, 6, 7) * 3
 UNIT_PLACES = [(hf, nt) for nts in (range(4), range(4, 6)) for hf in range(2) for nt in nts]
 
 
@@ -131,15 +131,18 @@ def tile_list_listing_budget_pacer_kernel(
 
         w1_c, w1_s = {}, {}
 
-        def quantise_w1(a, b, after=None, scales_after=None, copy=nc.scalar.copy):
-            stage = keep("w1_stage%d%d" % (a, b), [P, PACK * KP], BF16, after=after)
-            copy(
-                stage[:].rearrange("p (i c j) -> p c j i", i=PACK, j=PACK),
-                w1_raw[a, b][:].rearrange("p j (c i) -> p c j i", i=PACK),
-            )
-            w1_c[a, b] = keep("w1_c%d%d" % (a, b), [P, KP], U32)
-            w1_s[a, b] = keep("w1_s%d%d" % (a, b), [P, KP], U8, after=scales_after)
-            nc.vector.quantize_mx(w1_c[a, b][:].bitcast(FP8X4), w1_s[a, b][:], stage[:])
+        def quantise_w1(passes, b, scales_after=None, copy=nc.scalar.copy):
+            name = "%d%d" % (passes[0], b)
+            stage = keep("w1_stage" + name, [P, len(passes) * PACK * KP], BF16)
+            codes = keep("w1_c" + name, [P, len(passes) * KP], U32)
+            scales = keep("w1_s" + name, [P, len(passes) * KP], U8, after=scales_after)
+            for n, a in enumerate(passes):
+                copy(
+                    stage[:, PACK * KP * n : PACK * KP * (n + 1)].rearrange("p (i c j) -> p c j i", i=PACK, j=PACK),
+                    w1_raw[a, b][:].rearrange("p j (c i) -> p c j i", i=PACK),
+                )
+                w1_c[a, b], w1_s[a, b] = codes[:, KP * n : KP * (n + 1)], scales[:, KP * n : KP * (n + 1)]
+            nc.vector.quantize_mx(codes[:].bitcast(FP8X4), scales[:], stage[:])
 
         wb_c = [keep("wb_c%d" % piece, [P, 2 * WB_PIECE], U32) for piece in range(N // WB_PIECE)]
         wb_stage = [keep("wb_stage%d" % piece, [P, 2, PACK * WB_PIECE], BF16) for piece in range(N // WB_PIECE)]
@@ -187,8 +190,8 @@ def tile_list_listing_budget_pacer_kernel(
 
         def new_z_t(pair, name, after=None, tile=None):
             both = keep(name, [P, 4 * BANK], BF16, after=after) if tile is None else tile
-            for hf in range(2):
-                z_t[pair, hf] = both[:, 2 * BANK * hf : 2 * BANK * (hf + 1)]
+            for quarter in range(4):
+                z_t[pair, quarter] = both[:, BANK * quarter : BANK * (quarter + 1)]
 
         def add_turned(src, blocks, regions, first=False, last=False):
             seen = [regions(block)[0] for block in blocks]
@@ -207,9 +210,8 @@ def tile_list_listing_budget_pacer_kernel(
             return lambda block: (banks[block // 2], 2 * (block % 2) + e)
 
         def round_pair(pair, quarter, sums, copy):
-            hf, part = divmod(quarter, 2)
             copy(
-                z_t[pair, hf][:, BANK * part : BANK * (part + 1)].rearrange("m (l p e) -> m l p e", l=2, e=2),
+                z_t[pair, quarter].rearrange("m (l p e) -> m l p e", l=2, e=2),
                 sums[:].rearrange("m (l e p) -> m l p e", l=2, e=2),
             )
 
@@ -228,13 +230,12 @@ def tile_list_listing_budget_pacer_kernel(
         z_s, z_in = {}, {}
 
         def turn_words(quarter, back, pairs):
-            hf, part = divmod(quarter, 2)
             for pair in pairs:
-                words = z_t[pair, hf].bitcast(F32)
+                words = z_t[pair, quarter].bitcast(F32)
                 for l in range(2):
                     nc.tensor.transpose(
                         back[:, P * (2 * pair + l) : P * (2 * pair + l + 1)],
-                        words[:, P * (2 * part + l) : P * (2 * part + l + 1)],
+                        words[:, P * l : P * (l + 1)],
                         ident[:],
                     )
             return back
@@ -333,19 +334,19 @@ def tile_list_listing_budget_pacer_kernel(
 
         v_s = keep("v_s", [P, S], U8)
         nc.vector.tensor_copy(v_s[:], tab_s[:].bitcast(U8).indirect(idx[:]))
-        quantise_w1(0, 0, copy=nc.vector.tensor_copy)
+        quantise_w1((0,), 0, copy=nc.vector.tensor_copy)
         v_w[0] = keep("v_w0", [P, S], U32, after="w1_stage00")
         nc.vector.tensor_copy(v_w[0][:], tab_w[0][:].bitcast(U32).indirect(idx[:]))
-        quantise_w1(1, 0, scales_after="tab_w0")
-        v_w[1] = keep("v_w1", [P, S], U32, after="w1_stage10")
+        quantise_w1((1,), 0, scales_after="tab_w0")
+        v_w[1] = keep("v_w1", [P, S], U32)
         for half in halves:
             offsets = idx[:, half.start // 16 : half.stop // 16]
             nc.vector.tensor_copy(v_w[1][:, half], tab_w[1][:].bitcast(U32).indirect(offsets))
-        for n, half in enumerate(halves):
-            for s in range(2):
-                make_h(s, 2 * n + s, half, (0, 1))
-                fetch_h(s, half)
-                place(s, half)
+        pieces = [(1, slice(0, P)), (0, halves[0]), (1, slice(P, 2 * P)), (0, halves[1]), (1, halves[1])]
+        for number, (s, entries) in enumerate(pieces):
+            make_h(s, number, entries, (0, 1))
+            fetch_h(s, entries)
+            place(s, entries)
         for s, number in ((2, 6), (3, 7)):
             make_h(s, number, whole, (1, 0))
 
@@ -356,8 +357,7 @@ def tile_list_listing_budget_pacer_kernel(
         add_turned(prior_sb[0], range(8), pair_regions(banks, 0), first=True)
         add_turned(pages[0], range(8), pair_regions(banks, 0))
         add_turned(prior_sb[1], range(8), pair_regions(banks, 1))
-        quantise_w1(0, 1)
-        quantise_w1(1, 1)
+        quantise_w1((0, 1), 1)
         fetch_h(3, whole, tile=shared.tile([P, S], F32, name="h3", offset=0)[:])
         place(3, whole)
         new_z_t(0, "z_t00", tile=shared.tile([P, 4 * BANK], BF16, name="z_t00", offset=4 * T2))
@@ -395,20 +395,22 @@ def tile_list_listing_budget_pacer_kernel(
             round_wb(b, 2)
         z_s[0, 0] = shared.tile([P, BANK], U8, name="z_s00", offset=8 * 1024, align_bytes=64)[:]
         quantise_z(0, 0)
-        for hf in range(2):
-            z_t[1, hf] = keep("z_t11%d" % hf, [P, 2 * BANK], BF16)[:]
+        first_half = keep("z_t110", [P, 2 * BANK], BF16)
+        z_t[1, 0], z_t[1, 1] = first_half[:, 0:BANK], first_half[:, BANK : 2 * BANK]
+        z_t[1, 2] = keep("z_t112", [P, BANK], BF16)[:]
         for quarter in range(4):
             add_turned(pages[7 % PAGES], (2 * quarter, 2 * quarter + 1), pair_regions(banks, 1), last=True)
         round_pair(1, 0, banks[0], nc.vector.tensor_copy)
-        for quarter in range(1, 4):
+        for quarter in (1, 2):
             round_pair(1, quarter, banks[quarter], nc.scalar.copy)
         first = keep("first_s", [P, BANK], U8, after="page1")
         quantise_wb(0, first[:])
-        for quarter in range(4):
+        for quarter in range(3):
             turn_words(quarter, backs[quarter], (1,))
         fetch_words(1, 0, backs[0], nc.vector.tensor_copy)
-        z_s[0, 1] = keep("z_s01", [P, BANK], U8, after="z_t110")[:]
-        quantise_z(0, 1)
+        z_t[1, 3] = keep("z_last", [P, BANK], BF16, after="z_t110")[:]
+        round_pair(1, 3, banks[3], nc.vector.tensor_copy)
+        turn_words(3, backs[3], (1,))
         for quarter in range(1, 4):
             fetch_words(1, quarter, backs[quarter], nc.scalar.copy)
         load_pass(0, 0)
@@ -416,8 +418,10 @@ def tile_list_listing_budget_pacer_kernel(
         z_s[1, 0] = keep("z_s10", [P, BANK], U8)[:]
         z_s[1, 1] = keep("z_s11", [P, BANK], U8)[:]
         quantise_z(1, 0)
-        rest = keep("late_s", [P, 2 * BANK], U8, after="z_in10")
+        rest = keep("late_s", [P, 3 * BANK], U8, after="z_in10")
         quantise_wb(1, rest[:, 0:BANK])
+        z_s[0, 1] = rest[:, 2 * BANK : 3 * BANK]
+        quantise_z(0, 1)
         quantise_z(1, 1)
         quantise_wb(2, rest[:, BANK : 2 * BANK])
 

@@ -15,6 +15,7 @@ U8 = mybir.dt.uint8
 FP8X4 = mybir.dt.float8_e4m3fn_x4
 FP4X4 = mybir.dt.float4_e2m1fn_x4
 MULT = mybir.AluOpType.mult
+ADD = mybir.AluOpType.add
 ACT = mybir.ActivationFunctionType
 
 P = 128
@@ -24,16 +25,16 @@ BANK = 512
 QUARTER = T2 // 4
 WB_PIECE = 256
 UNITS = (N // P) * (T2 // BANK)
-PAGES = 3
+PAGES = 4
 HALF = T2 // 2
 WORK_TAGS = ("w1_raw00", "w1_raw10", "w1_raw01", "wb_raw00", "tab_w0", "tab_w1")
 RES_TAGS = ["prior%d" % s for s in (0, 1, 2, 3, 6, 7, 4, 5)] + ["h0", "h1", "h2", "wb_raw01", "wb_raw11"]
 SET_X, SET_Y = (2, 3, 4, 5), (0, 1, 6, 7)
-SQUARED_ON_VECTOR = range(4, UNITS, 2)
-ON_GPSIMD = (0, 1, 2, 3, 4, 5, 6, 8)
-LOAD_BANKS = (4, 0, 2, 3) * 3
-SPEND_BANKS = (1, 5, 6, 7) * 3
-UNIT_PLACES = [(hf, nt) for nts in (range(4), range(4, 6)) for hf in range(2) for nt in nts]
+SQUARED_ON_VECTOR = range(5, UNITS, 2)
+ON_GPSIMD = [unit for unit in range(UNITS - 2) if unit < 5 or unit % 2 == 0]
+LOAD_BANKS = (6, 7, 4, 5) * 3
+SPEND_BANKS = (0, 1, 3, 2) * 3
+UNIT_PLACES = [(hf, nt) for hf in range(2) for nt in range(N // P)]
 
 
 def tile_list_listing_budget_pacer_kernel(
@@ -114,10 +115,11 @@ def tile_list_listing_budget_pacer_kernel(
         load_wb(0, 0)
         load_wb(1, 0)
         load_prior(4)
-        load_prior(6)
+        load_prior(7)
         load_wb(0, 1)
         load_wb(1, 1)
         load_prior(5)
+        load_prior(6)
         for quad in range(4):
             nc.sync.dma_start(
                 wa_s[32 * quad : 32 * quad + 4, :, :],
@@ -127,7 +129,6 @@ def tile_list_listing_budget_pacer_kernel(
             nc.sync.dma_start(wa_w[b][:], wa_words[b].bitcast(I32))
         load_wb(0, 2)
         load_wb(1, 2)
-        load_prior(7)
 
         w1_c, w1_s = {}, {}
 
@@ -145,7 +146,7 @@ def tile_list_listing_budget_pacer_kernel(
             nc.vector.quantize_mx(codes[:].bitcast(FP8X4), scales[:], stage[:])
 
         wb_c = [keep("wb_c%d" % piece, [P, 2 * WB_PIECE], U32) for piece in range(N // WB_PIECE)]
-        wb_stage = [keep("wb_stage%d" % piece, [P, 2, PACK * WB_PIECE], BF16) for piece in range(N // WB_PIECE)]
+        wb_stage = [keep("wb_stage%d" % piece, [P, 2, PACK * WB_PIECE], BF16) for piece in range(2)]
         wb_s = {}
 
         def round_wb(b, piece):
@@ -243,7 +244,10 @@ def tile_list_listing_budget_pacer_kernel(
         def fetch_words(b, quarter, back, copy):
             hf, part = divmod(quarter, 2)
             if part == 0:
-                z_in[b, hf] = keep("z_in%d%d" % (b, hf), [P, PACK * HALF], BF16)
+                if (b, hf) == (1, 0):
+                    z_in[b, hf] = shared.tile([P, PACK * HALF], BF16, name="z_in10", offset=24 * 1024, align_bytes=64)
+                else:
+                    z_in[b, hf] = keep("z_in%d%d" % (b, hf), [P, PACK * HALF], BF16)
             copy(
                 z_in[b, hf][:].bitcast(F32)[:, BANK * part : BANK * (part + 1)].rearrange("p (m u) -> p m u", u=2),
                 back[:].rearrange("p (u m) -> p m u", u=2),
@@ -273,7 +277,8 @@ def tile_list_listing_budget_pacer_kernel(
 
         def spend_pass(unit, b):
             hf, nt = UNIT_PLACES[unit]
-            if b == 1:
+            first = unit not in spends
+            if first:
                 spends[unit] = bank(SPEND_BANKS[unit])
             nc.tensor.matmul_mx(
                 spends[unit][:],
@@ -281,8 +286,8 @@ def tile_list_listing_budget_pacer_kernel(
                 lhsT_scale=wa_s[:, b, :].bitcast(U8)[:, P * nt : P * (nt + 1)],
                 rhs=z_c[b, hf][:].bitcast(FP8X4),
                 rhs_scale=z_s[b, hf],
-                start=(b == 1),
-                stop=(b == 0),
+                start=first,
+                stop=not first,
             )
 
         def scratch(unit, row):
@@ -312,7 +317,7 @@ def tile_list_listing_budget_pacer_kernel(
             nc.sync.dma_start(out[P * nt : P * (nt + 1), BANK * hf : BANK * (hf + 1)][:, cols], res)
 
         def first_product(unit):
-            for b in (1, 0):
+            for b in (1,) if unit in spends else (1, 0):
                 spend_pass(unit, b)
             nc.vector.tensor_tensor(scratch(unit, 0), spends[unit][:], scratch(unit, 1), MULT)
 
@@ -321,7 +326,7 @@ def tile_list_listing_budget_pacer_kernel(
             store(unit, res[:, cols], cols)
 
         def one_product(unit, res, pieces):
-            for b in (1, 0):
+            for b in (1,) if unit in spends else (1, 0):
                 spend_pass(unit, b)
             for piece in range(pieces):
                 cols = slice(BANK // pieces * piece, BANK // pieces * (piece + 1))
@@ -373,7 +378,8 @@ def tile_list_listing_budget_pacer_kernel(
             fetch_h(s, whole, tile=h_late[:, s - 4, :])
         add_turned(prior_sb[3], range(8), pair_regions(banks, 1))
         place(4, whole)
-        new_z_t(1, "z_t01", tile=shared.tile([P, 4 * BANK], BF16, name="z_t01", offset=16 * 1024))
+        old_words = shared.tile([P, 4 * BANK], BF16, name="z_t01", offset=16 * 1024)
+        new_z_t(1, "z_t01", tile=old_words)
         close_pair(2, banks)
         place(5, whole)
         backs = [turn_words(quarter, bank(number), (0,)) for quarter, number in enumerate(SET_X)]
@@ -383,47 +389,57 @@ def tile_list_listing_budget_pacer_kernel(
         banks = add_pair(4, SET_Y)
         add_turned(pages[4 % PAGES], range(8), pair_regions(banks, 0))
         round_wb(0, 1)
-        new_z_t(0, "z_t10")
+        new_z_t(0, "z_t10", tile=shared.tile([P, 4 * BANK], BF16, name="z_t10", offset=20 * 1024))
         close_pair(4, banks)
         round_wb(1, 1)
         place(6, whole)
         place(7, whole)
+        sums = [bank(number) for number in SET_X[:2]]
+        add_turned(prior_sb[6], range(8), lambda block: (sums[block // 4], block % 4), first=True)
         backs = [turn_words(quarter, bank(number), (0,)) for quarter, number in enumerate(SET_Y)]
-        banks = add_pair(6, SET_X)
-        add_turned(pages[6 % PAGES], range(8), pair_regions(banks, 0))
+        for hf in range(2):
+            add_turned(pages[6 % PAGES], range(4 * hf, 4 * hf + 4), lambda block: (sums[hf], block % 4), last=True)
+        for hf in range(2):
+            words = old_words[:, 2 * BANK * hf : 2 * BANK * (hf + 1)].rearrange("m (c e) -> m c e", e=2)
+            nc.scalar.copy(words[:, :, 0], sums[hf][:])
+            for quarter in (2 * hf, 2 * hf + 1):
+                turn_words(quarter, backs[quarter], (1,))
+        for quarter in range(4):
+            fetch_words(1, quarter, backs[quarter], nc.scalar.copy)
+        wb_stage.append(shared.tile([P, 2, PACK * WB_PIECE], BF16, name="wb_stage2", offset=16 * 1024, align_bytes=64))
         for b in range(2):
             round_wb(b, 2)
-        z_s[0, 0] = shared.tile([P, BANK], U8, name="z_s00", offset=8 * 1024, align_bytes=64)[:]
+
+        def add_last(hf, tile):
+            cols = slice(HALF * hf, HALF * (hf + 1))
+            nc.vector.tensor_tensor(tile[:], pages[7 % PAGES][:, cols], prior_sb[7][:, cols], ADD)
+            return tile
+
+        def lay_last(hf, tile):
+            places = z_in[1, hf][:].rearrange("p (m i) -> p m i", i=PACK)[:, :, 3]
+            nc.vector.tensor_copy(places, tile[:])
+
+        z_s[0, 0] = shared.tile([P, BANK], U8, name="z_s00", offset=20 * 1024, align_bytes=64)[:]
         quantise_z(0, 0)
-        first_half = keep("z_t110", [P, 2 * BANK], BF16)
-        z_t[1, 0], z_t[1, 1] = first_half[:, 0:BANK], first_half[:, BANK : 2 * BANK]
-        z_t[1, 2] = keep("z_t112", [P, BANK], BF16)[:]
-        for quarter in range(4):
-            add_turned(pages[7 % PAGES], (2 * quarter, 2 * quarter + 1), pair_regions(banks, 1), last=True)
-        round_pair(1, 0, banks[0], nc.vector.tensor_copy)
-        for quarter in (1, 2):
-            round_pair(1, quarter, banks[quarter], nc.scalar.copy)
-        first = keep("first_s", [P, BANK], U8, after="page1")
+        last = add_last(0, shared.tile([P, HALF], BF16, name="last0", offset=21 * 1024))
+        first = shared.tile([P, BANK], U8, name="first_s", offset=22 * 1024, align_bytes=64)
         quantise_wb(0, first[:])
-        for quarter in range(3):
-            turn_words(quarter, backs[quarter], (1,))
-        fetch_words(1, 0, backs[0], nc.vector.tensor_copy)
-        z_t[1, 3] = keep("z_last", [P, BANK], BF16, after="z_t110")[:]
-        round_pair(1, 3, banks[3], nc.vector.tensor_copy)
-        turn_words(3, backs[3], (1,))
-        for quarter in range(1, 4):
-            fetch_words(1, quarter, backs[quarter], nc.scalar.copy)
-        load_pass(0, 0)
-        load_pass(1, 0)
+        lay_last(0, last)
+        for unit in range(3):
+            spend_pass(unit, 0)
+        for unit in range(2):
+            load_pass(unit, 0)
         z_s[1, 0] = keep("z_s10", [P, BANK], U8)[:]
         z_s[1, 1] = keep("z_s11", [P, BANK], U8)[:]
         quantise_z(1, 0)
-        rest = keep("late_s", [P, 3 * BANK], U8, after="z_in10")
+        last = add_last(1, shared.tile([P, HALF], BF16, name="last1", offset=24 * 1024))
+        rest = shared.tile([P, 3 * BANK], U8, name="late_s", offset=25 * 1024, align_bytes=64)
         quantise_wb(1, rest[:, 0:BANK])
-        z_s[0, 1] = rest[:, 2 * BANK : 3 * BANK]
-        quantise_z(0, 1)
-        quantise_z(1, 1)
+        lay_last(1, last)
         quantise_wb(2, rest[:, BANK : 2 * BANK])
+        z_s[0, 1] = rest[:, 2 * BANK : 3 * BANK]
+        quantise_z(1, 1)
+        quantise_z(0, 1)
 
         started = set()
         for unit in range(UNITS):

@@ -28,13 +28,13 @@ UNITS = (N // P) * (T2 // BANK)
 PAGES = 4
 HALF = T2 // 2
 WORK_TAGS = ("w1_raw00", "w1_raw10", "w1_raw01", "wb_raw00", "tab_w0", "tab_w1")
-RES_TAGS = ["prior%d" % s for s in (0, 1, 2, 3, 6, 7, 4, 5)] + ["h0", "h1", "h2", "wb_raw01", "wb_raw11"]
+RES_TAGS = ["prior%d" % s for s in (0, 1, 2, 3, 6, 7, 4, 5)] + ["h0", "h1", "h2", "wb_raw02", "wb_raw11"]
 SET_X, SET_Y = (2, 3, 4, 5), (0, 1, 6, 7)
 SQUARED_ON_VECTOR = range(5, UNITS, 2)
 ON_GPSIMD = [unit for unit in range(UNITS - 2) if unit < 5 or unit % 2 == 0]
 LOAD_BANKS = (6, 7, 4, 5) * 3
 SPEND_BANKS = (0, 1, 3, 2) * 3
-UNIT_PLACES = [(hf, nt) for hf in range(2) for nt in range(N // P)]
+UNIT_PLACES = [(hf, nt) for nts in (range(4), range(4, 6)) for hf in range(2) for nt in nts]
 
 
 def tile_list_listing_budget_pacer_kernel(
@@ -89,7 +89,7 @@ def tile_list_listing_budget_pacer_kernel(
 
         def load_wb(b, piece):
             if (b, piece) == (1, 0):
-                wb_raw[b, piece] = shared.tile([P, PACK, WB_PIECE], F32, name="wb_raw10", offset=14 * 1024)
+                wb_raw[b, piece] = shared.tile([P, PACK, WB_PIECE], F32, name="wb_raw10", offset=18 * 1024)
             else:
                 wb_raw[b, piece] = keep("wb_raw%d%d" % (b, piece), [P, PACK, WB_PIECE], F32)
             part = wb[KP * b : KP * (b + 1), WB_PIECE * piece : WB_PIECE * (piece + 1)]
@@ -107,17 +107,18 @@ def tile_list_listing_budget_pacer_kernel(
         nc.sync.dma_start(wgs_sb[:], wgs)
         nc.sync.dma_start(idx2[:], offs2)
         load_w1(0, 1)
-        load_prior(0)
         load_w1(1, 1)
+        load_prior(0)
+        load_wb(0, 0)
         load_prior(1)
         load_prior(2)
-        load_prior(3)
-        load_wb(0, 0)
         load_wb(1, 0)
-        load_prior(4)
-        load_prior(7)
         load_wb(0, 1)
+        load_prior(3)
+        load_prior(4)
         load_wb(1, 1)
+        load_prior(7)
+        load_wb(0, 2)
         load_prior(5)
         load_prior(6)
         for quad in range(4):
@@ -127,7 +128,6 @@ def tile_list_listing_budget_pacer_kernel(
             )
         for b in range(2):
             nc.sync.dma_start(wa_w[b][:], wa_words[b].bitcast(I32))
-        load_wb(0, 2)
         load_wb(1, 2)
 
         w1_c, w1_s = {}, {}
@@ -146,12 +146,13 @@ def tile_list_listing_budget_pacer_kernel(
             nc.vector.quantize_mx(codes[:].bitcast(FP8X4), scales[:], stage[:])
 
         wb_c = [keep("wb_c%d" % piece, [P, 2 * WB_PIECE], U32) for piece in range(N // WB_PIECE)]
-        wb_stage = [keep("wb_stage%d" % piece, [P, 2, PACK * WB_PIECE], BF16) for piece in range(2)]
+        wb_stage = [keep("wb_stage%d" % piece, [P, 2, PACK * WB_PIECE], BF16) for piece in range(3)]
         wb_s = {}
 
-        def round_wb(b, piece):
+        def round_wb(b, piece, stage=None):
+            stage = wb_stage[piece][:, b, :] if stage is None else stage
             nc.scalar.copy(
-                wb_stage[piece][:, b, :].rearrange("p (c n j) -> p c j n", n=4, j=PACK),
+                stage.rearrange("p (c n j) -> p c j n", n=4, j=PACK),
                 wb_raw[b, piece][:].rearrange("p j (c n) -> p c j n", n=4),
             )
 
@@ -222,8 +223,10 @@ def tile_list_listing_budget_pacer_kernel(
             add_turned(prior_sb[s + 1], range(8), pair_regions(banks, 1))
             return banks
 
-        def close_pair(s, banks):
+        def close_pair(s, banks, with_prior=False):
             for quarter in range(4):
+                if with_prior:
+                    add_turned(prior_sb[s + 1], (2 * quarter, 2 * quarter + 1), pair_regions(banks, 1))
                 add_turned(pages[(s + 1) % PAGES], (2 * quarter, 2 * quarter + 1), pair_regions(banks, 1), last=True)
                 round_pair(s % PACK // 2, quarter, banks[quarter], nc.scalar.copy)
 
@@ -245,7 +248,7 @@ def tile_list_listing_budget_pacer_kernel(
             hf, part = divmod(quarter, 2)
             if part == 0:
                 if (b, hf) == (1, 0):
-                    z_in[b, hf] = shared.tile([P, PACK * HALF], BF16, name="z_in10", offset=24 * 1024, align_bytes=64)
+                    z_in[b, hf] = shared.tile([P, PACK * HALF], BF16, name="z_in10", offset=28 * 1024, align_bytes=64)
                 else:
                     z_in[b, hf] = keep("z_in%d%d" % (b, hf), [P, PACK * HALF], BF16)
             copy(
@@ -361,24 +364,24 @@ def tile_list_listing_budget_pacer_kernel(
         banks = [bank(number) for number in SET_X]
         add_turned(prior_sb[0], range(8), pair_regions(banks, 0), first=True)
         add_turned(pages[0], range(8), pair_regions(banks, 0))
-        add_turned(prior_sb[1], range(8), pair_regions(banks, 1))
         quantise_w1((0, 1), 1)
         fetch_h(3, whole, tile=shared.tile([P, S], F32, name="h3", offset=0)[:])
         place(3, whole)
-        new_z_t(0, "z_t00", tile=shared.tile([P, 4 * BANK], BF16, name="z_t00", offset=4 * T2))
-        close_pair(0, banks)
+        round_wb(0, 0)
+        new_z_t(0, "z_t00", tile=shared.tile([P, 4 * BANK], BF16, name="z_t00", offset=4 * 1024))
+        close_pair(0, banks, with_prior=True)
         banks = [bank(number) for number in SET_Y]
         add_turned(prior_sb[2], range(8), pair_regions(banks, 0), first=True)
         add_turned(pages[2], range(8), pair_regions(banks, 0))
-        for b in range(2):
-            round_wb(b, 0)
-        h_late = shared.tile([P, PACK, S], F32, name="h_late", offset=8 * 1024)
+        round_wb(1, 0)
+        round_wb(0, 1)
+        h_late = shared.tile([P, PACK, S], F32, name="h_late", offset=12 * 1024)
         for s, number in zip(range(4, 8), SET_X):
             make_h(s, number, whole, (1, 0))
             fetch_h(s, whole, tile=h_late[:, s - 4, :])
         add_turned(prior_sb[3], range(8), pair_regions(banks, 1))
         place(4, whole)
-        old_words = shared.tile([P, 4 * BANK], BF16, name="z_t01", offset=16 * 1024)
+        old_words = shared.tile([P, 4 * BANK], BF16, name="z_t01", offset=20 * 1024)
         new_z_t(1, "z_t01", tile=old_words)
         close_pair(2, banks)
         place(5, whole)
@@ -388,10 +391,10 @@ def tile_list_listing_budget_pacer_kernel(
 
         banks = add_pair(4, SET_Y)
         add_turned(pages[4 % PAGES], range(8), pair_regions(banks, 0))
-        round_wb(0, 1)
-        new_z_t(0, "z_t10", tile=shared.tile([P, 4 * BANK], BF16, name="z_t10", offset=20 * 1024))
-        close_pair(4, banks)
         round_wb(1, 1)
+        new_z_t(0, "z_t10", tile=shared.tile([P, 4 * BANK], BF16, name="z_t10", offset=24 * 1024))
+        close_pair(4, banks)
+        round_wb(0, 2)
         place(6, whole)
         place(7, whole)
         sums = [bank(number) for number in SET_X[:2]]
@@ -404,27 +407,28 @@ def tile_list_listing_budget_pacer_kernel(
             nc.scalar.copy(words[:, :, 0], sums[hf][:])
             for quarter in (2 * hf, 2 * hf + 1):
                 turn_words(quarter, backs[quarter], (1,))
-        for quarter in range(4):
+        for quarter in range(3):
             fetch_words(1, quarter, backs[quarter], nc.scalar.copy)
-        wb_stage.append(shared.tile([P, 2, PACK * WB_PIECE], BF16, name="wb_stage2", offset=16 * 1024, align_bytes=64))
-        for b in range(2):
-            round_wb(b, 2)
 
         def add_last(hf, tile):
             cols = slice(HALF * hf, HALF * (hf + 1))
             nc.vector.tensor_tensor(tile[:], pages[7 % PAGES][:, cols], prior_sb[7][:, cols], ADD)
             return tile
 
-        def lay_last(hf, tile):
-            places = z_in[1, hf][:].rearrange("p (m i) -> p m i", i=PACK)[:, :, 3]
-            nc.vector.tensor_copy(places, tile[:])
+        def lay_last(hf, tile, cols=slice(0, HALF), copy=nc.vector.tensor_copy):
+            places = z_in[1, hf][:].rearrange("p (m i) -> p m i", i=PACK)[:, cols, 3]
+            copy(places, tile[:, cols])
 
-        z_s[0, 0] = shared.tile([P, BANK], U8, name="z_s00", offset=20 * 1024, align_bytes=64)[:]
+        z_s[0, 0] = shared.tile([P, BANK], U8, name="z_s00", offset=24 * 1024, align_bytes=64)[:]
         quantise_z(0, 0)
-        last = add_last(0, shared.tile([P, HALF], BF16, name="last0", offset=21 * 1024))
-        first = shared.tile([P, BANK], U8, name="first_s", offset=22 * 1024, align_bytes=64)
+        last = add_last(0, shared.tile([P, HALF], BF16, name="last0", offset=25 * 1024))
+        first = shared.tile([P, BANK], U8, name="first_s", offset=26 * 1024, align_bytes=64)
         quantise_wb(0, first[:])
-        lay_last(0, last)
+        lay_last(0, last, slice(0, QUARTER))
+        lay_last(0, last, slice(QUARTER, HALF), nc.scalar.copy)
+        fetch_words(1, 3, backs[3], nc.scalar.copy)
+        last_stage = shared.tile([P, PACK * WB_PIECE], BF16, name="last_stage", offset=20 * 1024, align_bytes=64)
+        round_wb(1, 2, last_stage[:])
         for unit in range(3):
             spend_pass(unit, 0)
         for unit in range(2):
@@ -432,14 +436,17 @@ def tile_list_listing_budget_pacer_kernel(
         z_s[1, 0] = keep("z_s10", [P, BANK], U8)[:]
         z_s[1, 1] = keep("z_s11", [P, BANK], U8)[:]
         quantise_z(1, 0)
-        last = add_last(1, shared.tile([P, HALF], BF16, name="last1", offset=24 * 1024))
-        rest = shared.tile([P, 3 * BANK], U8, name="late_s", offset=25 * 1024, align_bytes=64)
+        last = add_last(1, shared.tile([P, HALF], BF16, name="last1", offset=25 * 1024))
+        rest = shared.tile([P, 3 * BANK], U8, name="late_s", offset=29 * 1024, align_bytes=64)
         quantise_wb(1, rest[:, 0:BANK])
         lay_last(1, last)
-        quantise_wb(2, rest[:, BANK : 2 * BANK])
         z_s[0, 1] = rest[:, 2 * BANK : 3 * BANK]
-        quantise_z(1, 1)
         quantise_z(0, 1)
+        quantise_z(1, 1)
+        wb_s[2] = rest[:, BANK : 2 * BANK]
+        for b, stage in enumerate((wb_stage[2][:, 0, :], last_stage[:])):
+            cols = slice(WB_PIECE * b, WB_PIECE * (b + 1))
+            nc.vector.quantize_mx(wb_c[2][:, cols].bitcast(FP8X4), wb_s[2][:, cols], stage)
 
         started = set()
         for unit in range(UNITS):

@@ -27,13 +27,16 @@ WB_PIECE = 256
 UNITS = (N // P) * (T2 // BANK)
 PAGES = 4
 HALF = T2 // 2
+KIB = 1024
 WORK_TAGS = ("w1_raw00", "w1_raw10", "w1_raw01", "wb_raw00", "tab_w0", "tab_w1")
-RES_TAGS = ["prior%d" % s for s in (0, 1, 2, 3, 6, 7, 4, 5)] + ["h0", "h1", "h2", "wb_raw02", "wb_raw11"]
+RES_TAGS = ["prior%d" % s for s in (0, 1, 2, 3, 6, 7, 4, 5)] + ["h0", "h1", "h2", "wb_raw02"]
 SET_X, SET_Y = (2, 3, 4, 5), (0, 1, 6, 7)
-SQUARED_ON_VECTOR = range(5, UNITS, 2)
-ON_GPSIMD = [unit for unit in range(UNITS - 2) if unit < 5 or unit % 2 == 0]
-LOAD_BANKS = (6, 7, 4, 5) * 3
-SPEND_BANKS = (0, 1, 3, 2) * 3
+ALTERNATE_FROM = 5
+SQUARED_ON_VECTOR = range(ALTERNATE_FROM, UNITS, 2)
+ON_GPSIMD = [unit for unit in range(UNITS - 2) if unit not in SQUARED_ON_VECTOR]
+LOAD_AHEAD = 3
+LOAD_BANKS = (6, 7, 4, 5)
+SPEND_BANKS = (0, 1, 3, 2)
 UNIT_PLACES = [(hf, nt) for nts in (range(4), range(4, 6)) for hf in range(2) for nt in nts]
 
 
@@ -48,6 +51,9 @@ def tile_list_listing_budget_pacer_kernel(
 
         def keep(name, shape, dtype, after=None):
             return held.tile(shape, dtype, name=name, tag=after or name, align_bytes=64)
+
+        def lay_at(name, shape, dtype, offset):
+            return shared.tile(shape, dtype, name=name, offset=offset, align_bytes=64)
 
         def bank(number):
             return psum.tile([P, BANK], F32, name="bank%d" % number)
@@ -76,7 +82,7 @@ def tile_list_listing_budget_pacer_kernel(
 
         def load_w1(a, b):
             if (a, b) == (1, 1):
-                w1_raw[a, b] = shared.tile([P, PACK, KP], F32, name="w1_last", offset=0)
+                w1_raw[a, b] = lay_at("w1_last", [P, PACK, KP], F32, 0)
             else:
                 w1_raw[a, b] = keep("w1_raw%d%d" % (a, b), [P, PACK, KP], F32)
             part = w1[KP * a : KP * (a + 1), KP * b : KP * (b + 1)]
@@ -89,7 +95,7 @@ def tile_list_listing_budget_pacer_kernel(
 
         def load_wb(b, piece):
             if (b, piece) == (1, 0):
-                wb_raw[b, piece] = shared.tile([P, PACK, WB_PIECE], F32, name="wb_raw10", offset=18 * 1024)
+                wb_raw[b, piece] = lay_at("wb_raw10", [P, PACK, WB_PIECE], F32, 18 * KIB)
             else:
                 wb_raw[b, piece] = keep("wb_raw%d%d" % (b, piece), [P, PACK, WB_PIECE], F32)
             part = wb[KP * b : KP * (b + 1), WB_PIECE * piece : WB_PIECE * (piece + 1)]
@@ -146,11 +152,10 @@ def tile_list_listing_budget_pacer_kernel(
             nc.vector.quantize_mx(codes[:].bitcast(FP8X4), scales[:], stage[:])
 
         wb_c = [keep("wb_c%d" % piece, [P, 2 * WB_PIECE], U32) for piece in range(N // WB_PIECE)]
-        wb_stage = [keep("wb_stage%d" % piece, [P, 2, PACK * WB_PIECE], BF16) for piece in range(3)]
+        wb_stage = [keep("wb_stage%d" % piece, [P, 2, PACK * WB_PIECE], BF16) for piece in range(2)]
         wb_s = {}
 
-        def round_wb(b, piece, stage=None):
-            stage = wb_stage[piece][:, b, :] if stage is None else stage
+        def round_wb(b, piece, stage):
             nc.scalar.copy(
                 stage.rearrange("p (c n j) -> p c j n", n=4, j=PACK),
                 wb_raw[b, piece][:].rearrange("p j (c n) -> p c j n", n=4),
@@ -179,9 +184,9 @@ def tile_list_listing_budget_pacer_kernel(
                     stop=(a == passes[1]),
                 )
 
-        def fetch_h(s, entries, after=None, tile=None):
-            if entries.start == 0:
-                h_sb[s] = keep("h%d" % s, [P, S], F32, after=after)[:] if tile is None else tile
+        def fetch_h(s, entries):
+            if s not in h_sb:
+                h_sb[s] = keep("h%d" % s, [P, S], F32)[:]
             nc.scalar.copy(h_sb[s][:, entries], h_ps[s, entries.start][:, entries])
 
         def place(s, entries):
@@ -190,10 +195,11 @@ def tile_list_listing_budget_pacer_kernel(
 
         z_t = {}
 
-        def new_z_t(pair, name, after=None, tile=None):
-            both = keep(name, [P, 4 * BANK], BF16, after=after) if tile is None else tile
+        def new_words(pair, name, offset):
+            words = lay_at(name, [P, 4 * BANK], BF16, offset)
             for quarter in range(4):
-                z_t[pair, quarter] = both[:, BANK * quarter : BANK * (quarter + 1)]
+                z_t[pair, quarter] = words[:, BANK * quarter : BANK * (quarter + 1)]
+            return words
 
         def add_turned(src, blocks, regions, first=False, last=False):
             seen = [regions(block)[0] for block in blocks]
@@ -211,47 +217,36 @@ def tile_list_listing_budget_pacer_kernel(
         def pair_regions(banks, e):
             return lambda block: (banks[block // 2], 2 * (block % 2) + e)
 
-        def round_pair(pair, quarter, sums, copy):
-            copy(
-                z_t[pair, quarter].rearrange("m (l p e) -> m l p e", l=2, e=2),
-                sums[:].rearrange("m (l e p) -> m l p e", l=2, e=2),
-            )
-
-        def add_pair(s, numbers):
+        def open_pair(s, numbers):
             banks = [bank(number) for number in numbers]
             add_turned(prior_sb[s], range(8), pair_regions(banks, 0), first=True)
-            add_turned(prior_sb[s + 1], range(8), pair_regions(banks, 1))
             return banks
 
-        def close_pair(s, banks, with_prior=False):
+        def close_pair(s, banks, sources):
             for quarter in range(4):
-                if with_prior:
-                    add_turned(prior_sb[s + 1], (2 * quarter, 2 * quarter + 1), pair_regions(banks, 1))
-                add_turned(pages[(s + 1) % PAGES], (2 * quarter, 2 * quarter + 1), pair_regions(banks, 1), last=True)
-                round_pair(s % PACK // 2, quarter, banks[quarter], nc.scalar.copy)
+                for src in sources:
+                    add_turned(src, (2 * quarter, 2 * quarter + 1), pair_regions(banks, 1), last=src is sources[-1])
+                nc.scalar.copy(
+                    z_t[s % PACK // 2, quarter].rearrange("m (l p e) -> m l p e", l=2, e=2),
+                    banks[quarter][:].rearrange("m (l e p) -> m l p e", l=2, e=2),
+                )
 
         z_c = {(b, hf): keep("z_c%d%d" % (b, hf), [P, BANK], U32) for b in range(2) for hf in range(2)}
         z_s, z_in = {}, {}
 
-        def turn_words(quarter, back, pairs):
-            for pair in pairs:
-                words = z_t[pair, quarter].bitcast(F32)
-                for l in range(2):
-                    nc.tensor.transpose(
-                        back[:, P * (2 * pair + l) : P * (2 * pair + l + 1)],
-                        words[:, P * l : P * (l + 1)],
-                        ident[:],
-                    )
+        def turn_words(quarter, back, pair):
+            words = z_t[pair, quarter].bitcast(F32)
+            for l in range(2):
+                nc.tensor.transpose(
+                    back[:, P * (2 * pair + l) : P * (2 * pair + l + 1)], words[:, P * l : P * (l + 1)], ident[:]
+                )
             return back
 
-        def fetch_words(b, quarter, back, copy):
+        def fetch_words(b, quarter, back):
             hf, part = divmod(quarter, 2)
-            if part == 0:
-                if (b, hf) == (1, 0):
-                    z_in[b, hf] = shared.tile([P, PACK * HALF], BF16, name="z_in10", offset=28 * 1024, align_bytes=64)
-                else:
-                    z_in[b, hf] = keep("z_in%d%d" % (b, hf), [P, PACK * HALF], BF16)
-            copy(
+            if (b, hf) not in z_in:
+                z_in[b, hf] = keep("z_in%d%d" % (b, hf), [P, PACK * HALF], BF16)
+            nc.scalar.copy(
                 z_in[b, hf][:].bitcast(F32)[:, BANK * part : BANK * (part + 1)].rearrange("p (m u) -> p m u", u=2),
                 back[:].rearrange("p (u m) -> p m u", u=2),
             )
@@ -259,7 +254,7 @@ def tile_list_listing_budget_pacer_kernel(
         def quantise_z(b, hf):
             nc.vector.quantize_mx(z_c[b, hf][:].bitcast(FP8X4), z_s[b, hf], z_in[b, hf][:])
 
-        work, loads, spends, made = {}, {}, {}, set()
+        work, loads, spends = {}, {}, {}
 
         def load_pass(unit, b):
             hf, nt = UNIT_PLACES[unit]
@@ -267,7 +262,7 @@ def tile_list_listing_budget_pacer_kernel(
             cols = slice(WB_PIECE * b + P * part, WB_PIECE * b + P * (part + 1))
             first = unit not in loads
             if first:
-                loads[unit] = bank(LOAD_BANKS[unit])
+                loads[unit] = bank(LOAD_BANKS[unit % 4])
             nc.tensor.matmul_mx(
                 loads[unit][:],
                 lhsT=wb_c[piece][:, cols].bitcast(FP8X4),
@@ -282,7 +277,7 @@ def tile_list_listing_budget_pacer_kernel(
             hf, nt = UNIT_PLACES[unit]
             first = unit not in spends
             if first:
-                spends[unit] = bank(SPEND_BANKS[unit])
+                spends[unit] = bank(SPEND_BANKS[unit % 4])
             nc.tensor.matmul_mx(
                 spends[unit][:],
                 lhsT=wa_w[b][:].bitcast(U8)[:, 2 * P * nt : 2 * P * (nt + 1)].bitcast(FP4X4),
@@ -298,14 +293,11 @@ def tile_list_listing_budget_pacer_kernel(
                 work[unit // 2] = keep("work%d" % unit, [P, 2, 2 * BANK], F32, after=WORK_TAGS[unit // 2])
             return work[unit // 2][:, row, BANK * (unit % 2) : BANK * (unit % 2 + 1)]
 
-        def make_load(unit):
-            if unit not in made:
-                made.add(unit)
-                for b in (1,) if unit in loads else (1, 0):
-                    load_pass(unit, b)
+        def finish_sum(one_pass, started, unit):
+            for b in (1,) if unit in started else (1, 0):
+                one_pass(unit, b)
 
-        def contention(unit):
-            make_load(unit)
+        def square_load(unit):
             if unit in SQUARED_ON_VECTOR:
                 nc.vector.tensor_copy(scratch(unit, 1), loads[unit][:])
                 nc.vector.tensor_tensor(scratch(unit, 0), loads[unit][:], scratch(unit, 1), MULT)
@@ -315,27 +307,28 @@ def tile_list_listing_budget_pacer_kernel(
         def damp(unit):
             nc.scalar.activation(scratch(unit, 1), scratch(unit, 0), ACT.Abs_reciprocal_sqrt, bias=ones[:])
 
+        def result(unit):
+            return keep("res%d" % unit, [P, BANK], F32, after=RES_TAGS[unit])
+
         def store(unit, res, cols):
             hf, nt = UNIT_PLACES[unit]
-            nc.sync.dma_start(out[P * nt : P * (nt + 1), BANK * hf : BANK * (hf + 1)][:, cols], res)
+            nc.sync.dma_start(out[P * nt : P * (nt + 1), BANK * hf : BANK * (hf + 1)][:, cols], res[:, cols])
 
-        def first_product(unit):
-            for b in (1,) if unit in spends else (1, 0):
-                spend_pass(unit, b)
+        def two_products(unit, second):
+            finish_sum(spend_pass, spends, unit)
             nc.vector.tensor_tensor(scratch(unit, 0), spends[unit][:], scratch(unit, 1), MULT)
+            res = result(unit)
+            second.tensor_tensor(res[:], scratch(unit, 0), scratch(unit, 1), MULT)
+            store(unit, res, slice(0, BANK))
 
-        def second_product(unit, engine, res, cols=slice(0, BANK)):
-            engine.tensor_tensor(res[:, cols], scratch(unit, 0)[:, cols], scratch(unit, 1)[:, cols], MULT)
-            store(unit, res[:, cols], cols)
-
-        def one_product(unit, res, pieces):
-            for b in (1,) if unit in spends else (1, 0):
-                spend_pass(unit, b)
+        def one_product(unit, pieces):
+            res = result(unit)
+            finish_sum(spend_pass, spends, unit)
             for piece in range(pieces):
                 cols = slice(BANK // pieces * piece, BANK // pieces * (piece + 1))
                 nc.scalar.activation(scratch(unit, 0)[:, cols], scratch(unit, 1)[:, cols], ACT.Square)
                 nc.vector.tensor_tensor(res[:, cols], spends[unit][:, cols], scratch(unit, 0)[:, cols], MULT)
-                store(unit, res[:, cols], cols)
+                store(unit, res, cols)
 
         whole = slice(0, S)
         halves = (slice(0, S // 2), slice(S // 2, S))
@@ -357,78 +350,78 @@ def tile_list_listing_budget_pacer_kernel(
             place(s, entries)
         for s, number in ((2, 6), (3, 7)):
             make_h(s, number, whole, (1, 0))
-
         fetch_h(2, whole)
         place(2, whole)
 
-        banks = [bank(number) for number in SET_X]
-        add_turned(prior_sb[0], range(8), pair_regions(banks, 0), first=True)
+        banks = open_pair(0, SET_X)
         add_turned(pages[0], range(8), pair_regions(banks, 0))
         quantise_w1((0, 1), 1)
-        fetch_h(3, whole, tile=shared.tile([P, S], F32, name="h3", offset=0)[:])
+        h_sb[3] = lay_at("h3", [P, S], F32, 0)[:]
+        fetch_h(3, whole)
         place(3, whole)
-        round_wb(0, 0)
-        new_z_t(0, "z_t00", tile=shared.tile([P, 4 * BANK], BF16, name="z_t00", offset=4 * 1024))
-        close_pair(0, banks, with_prior=True)
-        banks = [bank(number) for number in SET_Y]
-        add_turned(prior_sb[2], range(8), pair_regions(banks, 0), first=True)
+        round_wb(0, 0, wb_stage[0][:, 0, :])
+        new_words(0, "words01", 4 * KIB)
+        close_pair(0, banks, (prior_sb[1], pages[1]))
+        banks = open_pair(2, SET_Y)
         add_turned(pages[2], range(8), pair_regions(banks, 0))
-        round_wb(1, 0)
-        round_wb(0, 1)
-        h_late = shared.tile([P, PACK, S], F32, name="h_late", offset=12 * 1024)
-        for s, number in zip(range(4, 8), SET_X):
+        round_wb(1, 0, wb_stage[0][:, 1, :])
+        round_wb(0, 1, wb_stage[1][:, 0, :])
+        h_late = lay_at("h_late", [P, PACK, S], F32, 12 * KIB)
+        for s, number in zip(range(PACK, 2 * PACK), SET_X):
             make_h(s, number, whole, (1, 0))
-            fetch_h(s, whole, tile=h_late[:, s - 4, :])
+            h_sb[s] = h_late[:, s - PACK, :]
+            fetch_h(s, whole)
         add_turned(prior_sb[3], range(8), pair_regions(banks, 1))
         place(4, whole)
-        old_words = shared.tile([P, 4 * BANK], BF16, name="z_t01", offset=20 * 1024)
-        new_z_t(1, "z_t01", tile=old_words)
-        close_pair(2, banks)
+        second_words = new_words(1, "words23", 20 * KIB)
+        close_pair(2, banks, (pages[3],))
         place(5, whole)
-        backs = [turn_words(quarter, bank(number), (0,)) for quarter, number in enumerate(SET_X)]
+        backs = [turn_words(quarter, bank(number), 0) for quarter, number in enumerate(SET_X)]
         for quarter in range(4):
-            fetch_words(0, quarter, turn_words(quarter, backs[quarter], (1,)), nc.scalar.copy)
+            fetch_words(0, quarter, turn_words(quarter, backs[quarter], 1))
 
-        banks = add_pair(4, SET_Y)
+        banks = open_pair(4, SET_Y)
+        add_turned(prior_sb[5], range(8), pair_regions(banks, 1))
         add_turned(pages[4 % PAGES], range(8), pair_regions(banks, 0))
-        round_wb(1, 1)
-        new_z_t(0, "z_t10", tile=shared.tile([P, 4 * BANK], BF16, name="z_t10", offset=24 * 1024))
-        close_pair(4, banks)
-        round_wb(0, 2)
+        round_wb(1, 1, wb_stage[1][:, 1, :])
+        new_words(0, "words45", 24 * KIB)
+        close_pair(4, banks, (pages[5 % PAGES],))
+        last_stages = [keep("wb_stage02", [P, PACK * WB_PIECE], BF16)]
+        round_wb(0, 2, last_stages[0][:])
         place(6, whole)
         place(7, whole)
         sums = [bank(number) for number in SET_X[:2]]
         add_turned(prior_sb[6], range(8), lambda block: (sums[block // 4], block % 4), first=True)
-        backs = [turn_words(quarter, bank(number), (0,)) for quarter, number in enumerate(SET_Y)]
+        backs = [turn_words(quarter, bank(number), 0) for quarter, number in enumerate(SET_Y)]
+        add_turned(pages[6 % PAGES], range(8), lambda block: (sums[block // 4], block % 4), last=True)
         for hf in range(2):
-            add_turned(pages[6 % PAGES], range(4 * hf, 4 * hf + 4), lambda block: (sums[hf], block % 4), last=True)
-        for hf in range(2):
-            words = old_words[:, 2 * BANK * hf : 2 * BANK * (hf + 1)].rearrange("m (c e) -> m c e", e=2)
+            words = second_words[:, 2 * BANK * hf : 2 * BANK * (hf + 1)].rearrange("m (c e) -> m c e", e=2)
             nc.scalar.copy(words[:, :, 0], sums[hf][:])
             for quarter in (2 * hf, 2 * hf + 1):
-                turn_words(quarter, backs[quarter], (1,))
+                turn_words(quarter, backs[quarter], 1)
+        z_in[1, 0] = lay_at("z_in10", [P, PACK * HALF], BF16, 28 * KIB)
         for quarter in range(3):
-            fetch_words(1, quarter, backs[quarter], nc.scalar.copy)
+            fetch_words(1, quarter, backs[quarter])
 
-        def add_last(hf, tile):
+        def add_last(hf, offset):
             cols = slice(HALF * hf, HALF * (hf + 1))
-            nc.vector.tensor_tensor(tile[:], pages[7 % PAGES][:, cols], prior_sb[7][:, cols], ADD)
-            return tile
+            sums = lay_at("last%d" % hf, [P, HALF], BF16, offset)
+            nc.vector.tensor_tensor(sums[:], pages[7 % PAGES][:, cols], prior_sb[7][:, cols], ADD)
+            return sums
 
-        def lay_last(hf, tile, cols=slice(0, HALF), copy=nc.vector.tensor_copy):
-            places = z_in[1, hf][:].rearrange("p (m i) -> p m i", i=PACK)[:, cols, 3]
-            copy(places, tile[:, cols])
+        def lay_last(hf, sums, cols, copy):
+            copy(z_in[1, hf][:].rearrange("p (m i) -> p m i", i=PACK)[:, cols, PACK - 1], sums[:, cols])
 
-        z_s[0, 0] = shared.tile([P, BANK], U8, name="z_s00", offset=24 * 1024, align_bytes=64)[:]
+        z_s[0, 0] = lay_at("z_s00", [P, BANK], U8, 24 * KIB)[:]
         quantise_z(0, 0)
-        last = add_last(0, shared.tile([P, HALF], BF16, name="last0", offset=25 * 1024))
-        first = shared.tile([P, BANK], U8, name="first_s", offset=26 * 1024, align_bytes=64)
-        quantise_wb(0, first[:])
-        lay_last(0, last, slice(0, QUARTER))
-        lay_last(0, last, slice(QUARTER, HALF), nc.scalar.copy)
-        fetch_words(1, 3, backs[3], nc.scalar.copy)
-        last_stage = shared.tile([P, PACK * WB_PIECE], BF16, name="last_stage", offset=20 * 1024, align_bytes=64)
-        round_wb(1, 2, last_stage[:])
+        first_half = add_last(0, 25 * KIB)
+        quantise_wb(0, lay_at("wb_s0", [P, BANK], U8, 26 * KIB)[:])
+        lay_last(0, first_half, slice(0, QUARTER), nc.vector.tensor_copy)
+        second_half = add_last(1, 22 * KIB)
+        lay_last(0, first_half, slice(QUARTER, HALF), nc.scalar.copy)
+        fetch_words(1, 3, backs[3])
+        last_stages.append(lay_at("wb_stage12", [P, PACK * WB_PIECE], BF16, 20 * KIB))
+        round_wb(1, 2, last_stages[1][:])
         for unit in range(3):
             spend_pass(unit, 0)
         for unit in range(2):
@@ -436,30 +429,30 @@ def tile_list_listing_budget_pacer_kernel(
         z_s[1, 0] = keep("z_s10", [P, BANK], U8)[:]
         z_s[1, 1] = keep("z_s11", [P, BANK], U8)[:]
         quantise_z(1, 0)
-        last = add_last(1, shared.tile([P, HALF], BF16, name="last1", offset=25 * 1024))
-        rest = shared.tile([P, 3 * BANK], U8, name="late_s", offset=29 * 1024, align_bytes=64)
-        quantise_wb(1, rest[:, 0:BANK])
-        lay_last(1, last)
-        z_s[0, 1] = rest[:, 2 * BANK : 3 * BANK]
+        quantise_wb(1, lay_at("wb_s1", [P, BANK], U8, 25 * KIB)[:])
+        late_s = lay_at("late_s", [P, 2 * BANK], U8, 29 * KIB)
+        lay_last(1, second_half, slice(0, HALF), nc.vector.tensor_copy)
+        z_s[0, 1], wb_s[2] = late_s[:, 0:BANK], late_s[:, BANK : 2 * BANK]
         quantise_z(0, 1)
         quantise_z(1, 1)
-        wb_s[2] = rest[:, BANK : 2 * BANK]
-        for b, stage in enumerate((wb_stage[2][:, 0, :], last_stage[:])):
+        for b, stage in enumerate(last_stages):
             cols = slice(WB_PIECE * b, WB_PIECE * (b + 1))
-            nc.vector.quantize_mx(wb_c[2][:, cols].bitcast(FP8X4), wb_s[2][:, cols], stage)
+            nc.vector.quantize_mx(wb_c[2][:, cols].bitcast(FP8X4), wb_s[2][:, cols], stage[:])
 
-        started = set()
+        summed, squared = set(), set()
         for unit in range(UNITS):
-            for other in range(min(UNITS, unit + 3 + 1)):
-                make_load(other)
-            for other in range(min(UNITS, unit + 1 + 2)):
-                if other not in started and (other <= unit + 1 or other in SQUARED_ON_VECTOR):
-                    started.add(other)
-                    contention(other)
+            for other in range(min(UNITS, unit + LOAD_AHEAD + 1)):
+                if other not in summed:
+                    summed.add(other)
+                    finish_sum(load_pass, loads, other)
+            for other in range(min(UNITS, unit + 3)):
+                if other not in squared and (other <= unit + 1 or other in SQUARED_ON_VECTOR):
+                    squared.add(other)
+                    square_load(other)
             damp(unit)
-            res = keep("res%d" % unit, [P, BANK], F32, after=RES_TAGS[unit])[:]
-            if unit in ON_GPSIMD:
-                first_product(unit)
-                second_product(unit, nc.gpsimd, res)
-            else:
-                one_product(unit, res, 2 if unit == UNITS - 1 else 1)
+            if unit not in SQUARED_ON_VECTOR:
+                two_products(unit, nc.gpsimd if unit in ON_GPSIMD else nc.vector)
+                if unit - 1 in SQUARED_ON_VECTOR and unit in ON_GPSIMD:
+                    one_product(unit - 1, 1)
+            elif unit + 1 not in ON_GPSIMD:
+                one_product(unit, 2 if unit == UNITS - 1 else 1)

@@ -101,13 +101,18 @@ def tile_list_listing_budget_pacer_kernel(
             part = wb[KP * b : KP * (b + 1), WB_PIECE * piece : WB_PIECE * (piece + 1)]
             nc.sync.dma_start(wb_raw[b, piece][:], part.rearrange("(p j) c -> p j c", j=PACK))
 
+        def load_scale_rows(row):
+            for a in range(2):
+                rows = tab_scales[a].bitcast(I32).rearrange("(q r) w -> r q w", r=4)
+                nc.sync.dma_start(tab_s[4 * a + row : P : 32, :], rows[row])
+
         load_w1(0, 0)
-        for quad in range(4):
-            nc.sync.dma_start(
-                tab_s[32 * quad : 32 * quad + 8, :], tab_scales[:, 4 * quad : 4 * quad + 4, :].bitcast(I32)
-            )
-        nc.sync.dma_start(idx[:], offs)
+        load_scale_rows(0)
+        load_scale_rows(1)
         load_w1(1, 0)
+        load_scale_rows(2)
+        load_scale_rows(3)
+        nc.sync.dma_start(idx[:], offs)
         for a in range(2):
             nc.sync.dma_start(tab_w[a][:], tab_words[a].rearrange("p t i -> p (t i)").bitcast(I32))
         nc.sync.dma_start(wgs_sb[:], wgs)
@@ -168,21 +173,24 @@ def tile_list_listing_budget_pacer_kernel(
             )
 
         v_w, h_ps, h_sb = {}, {}, {}
+        first, later = slice(0, P), slice(P, S)
 
         def make_h(s, number, entries, passes):
             b, i = divmod(s, PACK)
             cols = slice(P * i, P * (i + 1))
             h_ps[s, entries.start] = bank(number)
+            runs = (slice(P, 2 * P), slice(2 * P, S)) if entries == later else (entries,)
             for a in passes:
-                nc.tensor.matmul_mx(
-                    h_ps[s, entries.start][:, entries],
-                    lhsT=w1_c[a, b][:, cols].bitcast(FP8X4),
-                    lhsT_scale=w1_s[a, b][:, cols],
-                    rhs=v_w[a][:, entries].bitcast(FP8X4),
-                    rhs_scale=v_s[4 * a : P, entries],
-                    start=(a == passes[0]),
-                    stop=(a == passes[1]),
-                )
+                for run in runs:
+                    nc.tensor.matmul_mx(
+                        h_ps[s, entries.start][:, run],
+                        lhsT=w1_c[a, b][:, cols].bitcast(FP8X4),
+                        lhsT_scale=w1_s[a, b][:, cols],
+                        rhs=v_w[a][:, run].bitcast(FP8X4),
+                        rhs_scale=v_s[4 * a : P, run],
+                        start=(a == passes[0] and run is runs[0]),
+                        stop=(a == passes[1] and run is runs[-1]),
+                    )
 
         def fetch_h(s, entries):
             if s not in h_sb:
@@ -331,7 +339,6 @@ def tile_list_listing_budget_pacer_kernel(
                 store(unit, res, cols)
 
         whole = slice(0, S)
-        halves = (slice(0, S // 2), slice(S // 2, S))
 
         v_s = keep("v_s", [P, S], U8)
         nc.vector.tensor_copy(v_s[:], tab_s[:].bitcast(U8).indirect(idx[:]))
@@ -340,10 +347,10 @@ def tile_list_listing_budget_pacer_kernel(
         nc.vector.tensor_copy(v_w[0][:], tab_w[0][:].bitcast(U32).indirect(idx[:]))
         quantise_w1((1,), 0, scales_after="tab_w0")
         v_w[1] = keep("v_w1", [P, S], U32)
-        for half in halves:
-            offsets = idx[:, half.start // 16 : half.stop // 16]
-            nc.vector.tensor_copy(v_w[1][:, half], tab_w[1][:].bitcast(U32).indirect(offsets))
-        pieces = [(1, slice(0, P)), (0, halves[0]), (1, slice(P, 2 * P)), (0, halves[1]), (1, halves[1])]
+        for part in (first, later):
+            offsets = idx[:, part.start // 16 : part.stop // 16]
+            nc.vector.tensor_copy(v_w[1][:, part], tab_w[1][:].bitcast(U32).indirect(offsets))
+        pieces = [(0, first), (1, first), (0, later), (1, later)]
         for number, (s, entries) in enumerate(pieces):
             make_h(s, number, entries, (0, 1))
             fetch_h(s, entries)

@@ -23,11 +23,12 @@ PACK = 4
 KP = P * PACK
 BANK = 512
 QUARTER = T2 // 4
+HALF = T2 // 2
 WB_PIECE = 256
 UNITS = (N // P) * (T2 // BANK)
 PAGES = 4
-HALF = T2 // 2
 KIB = 1024
+WB_LAST_AT = 28 * KIB
 WORK_TAGS = ("w1_raw00", "w1_raw10", "w1_raw01", "wb_raw00", "tab_w0", "tab_w1")
 RES_TAGS = ["prior%d" % s for s in (0, 1, 2, 3, 6, 7, 4, 5)] + ["h0", "h1", "h2", "wb_raw02"]
 SET_X, SET_Y = (2, 3, 4, 5), (0, 1, 6, 7)
@@ -37,7 +38,9 @@ ON_GPSIMD = [unit for unit in range(UNITS - 2) if unit not in SQUARED_ON_VECTOR]
 LOAD_AHEAD = 3
 LOAD_BANKS = (6, 7, 4, 5)
 SPEND_BANKS = (0, 1, 3, 2)
-UNIT_PLACES = [(hf, nt) for nts in (range(4), range(4, 6)) for hf in range(2) for nt in nts]
+UNIT_PLACES = [[(nt, QUARTER * q, QUARTER) for nt in range(2)] for q in range(2)] + [
+    [(nt, HALF * hf, BANK)] for hf, nt in ((0, 2), (0, 3), (1, 0), (1, 1), (1, 2), (1, 3), (0, 4), (0, 5), (1, 4), (1, 5))
+]
 
 
 def tile_list_listing_budget_pacer_kernel(
@@ -96,6 +99,8 @@ def tile_list_listing_budget_pacer_kernel(
         def load_wb(b, piece):
             if (b, piece) == (1, 0):
                 wb_raw[b, piece] = lay_at("wb_raw10", [P, PACK, WB_PIECE], F32, 18 * KIB)
+            elif (b, piece) == (1, 2):
+                wb_raw[b, piece] = lay_at("wb_raw12", [P, PACK, WB_PIECE], F32, WB_LAST_AT)
             else:
                 wb_raw[b, piece] = keep("wb_raw%d%d" % (b, piece), [P, PACK, WB_PIECE], F32)
             part = wb[KP * b : KP * (b + 1), WB_PIECE * piece : WB_PIECE * (piece + 1)]
@@ -131,6 +136,7 @@ def tile_list_listing_budget_pacer_kernel(
         load_prior(7)
         load_wb(0, 2)
         load_prior(5)
+        load_wb(1, 2)
         load_prior(6)
         for quad in range(4):
             nc.sync.dma_start(
@@ -139,7 +145,6 @@ def tile_list_listing_budget_pacer_kernel(
             )
         for b in range(2):
             nc.sync.dma_start(wa_w[b][:], wa_words[b].bitcast(I32))
-        load_wb(1, 2)
 
         w1_c, w1_s = {}, {}
 
@@ -164,6 +169,12 @@ def tile_list_listing_budget_pacer_kernel(
             nc.scalar.copy(
                 stage.rearrange("p (c n j) -> p c j n", n=4, j=PACK),
                 wb_raw[b, piece][:].rearrange("p j (c n) -> p c j n", n=4),
+            )
+
+        def round_half(part, stage):
+            nc.scalar.copy(
+                stage.rearrange("p (c n j) -> p c j n", n=4, j=PACK),
+                wb_raw[1, 2][:, :, P * part : P * (part + 1)].rearrange("p j (c n) -> p c j n", n=4),
             )
 
         def quantise_wb(piece, scales):
@@ -265,41 +276,49 @@ def tile_list_listing_budget_pacer_kernel(
         work, loads, spends = {}, {}, {}
 
         def load_pass(unit, b):
-            hf, nt = UNIT_PLACES[unit]
-            piece, part = divmod(nt, WB_PIECE // P)
-            cols = slice(WB_PIECE * b + P * part, WB_PIECE * b + P * (part + 1))
             first = unit not in loads
             if first:
                 loads[unit] = bank(LOAD_BANKS[unit % 4])
-            nc.tensor.matmul_mx(
-                loads[unit][:],
-                lhsT=wb_c[piece][:, cols].bitcast(FP8X4),
-                lhsT_scale=wb_s[piece][:, cols],
-                rhs=z_c[b, hf][:].bitcast(FP8X4),
-                rhs_scale=z_s[b, hf],
-                start=first,
-                stop=not first,
-            )
+            for n, (nt, start, width) in enumerate(UNIT_PLACES[unit]):
+                piece, part = divmod(nt, WB_PIECE // P)
+                cols = slice(WB_PIECE * b + P * part, WB_PIECE * b + P * (part + 1))
+                hf, m = divmod(start, HALF)
+                nc.tensor.matmul_mx(
+                    loads[unit][:, width * n : width * (n + 1)],
+                    lhsT=wb_c[piece][:, cols].bitcast(FP8X4),
+                    lhsT_scale=wb_s[piece][:, cols],
+                    rhs=z_c[b, hf][:, m : m + width].bitcast(FP8X4),
+                    rhs_scale=z_s[b, hf][:, m : m + width],
+                    start=first and n == 0,
+                    stop=not first and width * (n + 1) == BANK,
+                )
 
         def spend_pass(unit, b):
-            hf, nt = UNIT_PLACES[unit]
             first = unit not in spends
             if first:
                 spends[unit] = bank(SPEND_BANKS[unit % 4])
-            nc.tensor.matmul_mx(
-                spends[unit][:],
-                lhsT=wa_w[b][:].bitcast(U8)[:, 2 * P * nt : 2 * P * (nt + 1)].bitcast(FP4X4),
-                lhsT_scale=wa_s[:, b, :].bitcast(U8)[:, P * nt : P * (nt + 1)],
-                rhs=z_c[b, hf][:].bitcast(FP8X4),
-                rhs_scale=z_s[b, hf],
-                start=first,
-                stop=not first,
-            )
+            for n, (nt, start, width) in enumerate(UNIT_PLACES[unit]):
+                hf, m = divmod(start, HALF)
+                nc.tensor.matmul_mx(
+                    spends[unit][:, width * n : width * (n + 1)],
+                    lhsT=wa_w[b][:].bitcast(U8)[:, 2 * P * nt : 2 * P * (nt + 1)].bitcast(FP4X4),
+                    lhsT_scale=wa_s[:, b, :].bitcast(U8)[:, P * nt : P * (nt + 1)],
+                    rhs=z_c[b, hf][:, m : m + width].bitcast(FP8X4),
+                    rhs_scale=z_s[b, hf][:, m : m + width],
+                    start=first and n == 0,
+                    stop=not first and width * (n + 1) == BANK,
+                )
 
         def scratch(unit, row):
             if unit // 2 not in work:
                 work[unit // 2] = keep("work%d" % unit, [P, 2, 2 * BANK], F32, after=WORK_TAGS[unit // 2])
             return work[unit // 2][:, row, BANK * (unit % 2) : BANK * (unit % 2 + 1)]
+
+        def squared_load(unit):
+            return scratch(0 if unit == 1 else unit, 0)
+
+        def product(unit):
+            return scratch(1 - unit if unit < 2 else unit, 0)
 
         def finish_sum(one_pass, started, unit):
             for b in (1,) if unit in started else (1, 0):
@@ -310,23 +329,27 @@ def tile_list_listing_budget_pacer_kernel(
                 nc.vector.tensor_copy(scratch(unit, 1), loads[unit][:])
                 nc.vector.tensor_tensor(scratch(unit, 0), loads[unit][:], scratch(unit, 1), MULT)
             else:
-                nc.scalar.activation(scratch(unit, 0), loads[unit][:], ACT.Square)
+                nc.scalar.activation(squared_load(unit), loads[unit][:], ACT.Square)
 
         def damp(unit):
-            nc.scalar.activation(scratch(unit, 1), scratch(unit, 0), ACT.Abs_reciprocal_sqrt, bias=ones[:])
+            nc.scalar.activation(scratch(unit, 1), squared_load(unit), ACT.Abs_reciprocal_sqrt, bias=ones[:])
 
         def result(unit):
             return keep("res%d" % unit, [P, BANK], F32, after=RES_TAGS[unit])
 
         def store(unit, res, cols):
-            hf, nt = UNIT_PLACES[unit]
-            nc.sync.dma_start(out[P * nt : P * (nt + 1), BANK * hf : BANK * (hf + 1)][:, cols], res[:, cols])
+            nt, start, width = UNIT_PLACES[unit][0]
+            if width == BANK:
+                nc.sync.dma_start(out[P * nt : P * (nt + 1), start : start + BANK][:, cols], res[:, cols])
+            else:
+                rows = out[P * nt : P * (nt + 2), start : start + width].rearrange("(t p) m -> p t m", p=P)
+                nc.sync.dma_start(rows, res[:].rearrange("p (t m) -> p t m", t=2))
 
         def two_products(unit, second):
             finish_sum(spend_pass, spends, unit)
-            nc.vector.tensor_tensor(scratch(unit, 0), spends[unit][:], scratch(unit, 1), MULT)
+            nc.vector.tensor_tensor(product(unit), spends[unit][:], scratch(unit, 1), MULT)
             res = result(unit)
-            second.tensor_tensor(res[:], scratch(unit, 0), scratch(unit, 1), MULT)
+            second.tensor_tensor(res[:], product(unit), scratch(unit, 1), MULT)
             store(unit, res, slice(0, BANK))
 
         def one_product(unit, pieces):
@@ -391,10 +414,11 @@ def tile_list_listing_budget_pacer_kernel(
         add_turned(prior_sb[5], range(8), pair_regions(banks, 1))
         add_turned(pages[4 % PAGES], range(8), pair_regions(banks, 0))
         round_wb(1, 1, wb_stage[1][:, 1, :])
+        last_stages = [keep("wb_stage2", [P, 3 * PACK * P], BF16)]
+        round_wb(0, 2, last_stages[0][:, 0 : PACK * WB_PIECE])
         new_words(0, "words45", 24 * KIB)
         close_pair(4, banks, (pages[5 % PAGES],))
-        last_stages = [keep("wb_stage02", [P, PACK * WB_PIECE], BF16)]
-        round_wb(0, 2, last_stages[0][:])
+        round_half(0, last_stages[0][:, PACK * WB_PIECE :])
         place(6, whole)
         place(7, whole)
         sums = [bank(number) for number in SET_X[:2]]
@@ -406,54 +430,61 @@ def tile_list_listing_budget_pacer_kernel(
             nc.scalar.copy(words[:, :, 0], sums[hf][:])
             for quarter in (2 * hf, 2 * hf + 1):
                 turn_words(quarter, backs[quarter], 1)
-        z_in[1, 0] = lay_at("z_in10", [P, PACK * HALF], BF16, 28 * KIB)
-        for quarter in range(3):
+        for quarter in range(2):
+            fetch_words(1, quarter, backs[quarter])
+        last_stages.append(lay_at("wb_stage12", [P, PACK * P], BF16, 20 * KIB))
+        round_half(1, last_stages[1][:])
+        for quarter in range(2, 4):
             fetch_words(1, quarter, backs[quarter])
 
-        def add_last(hf, offset):
-            cols = slice(HALF * hf, HALF * (hf + 1))
-            sums = lay_at("last%d" % hf, [P, HALF], BF16, offset)
+        def add_last(cols, name, offset):
+            sums = lay_at(name, [P, cols.stop - cols.start], BF16, offset)
             nc.vector.tensor_tensor(sums[:], pages[7 % PAGES][:, cols], prior_sb[7][:, cols], ADD)
             return sums
 
-        def lay_last(hf, sums, cols, copy):
-            copy(z_in[1, hf][:].rearrange("p (m i) -> p m i", i=PACK)[:, cols, PACK - 1], sums[:, cols])
+        def lay_last(cols, sums, copy):
+            hf, m = divmod(cols.start, HALF)
+            copy(z_in[1, hf][:].rearrange("p (m i) -> p m i", i=PACK)[:, m : m + sums.shape[1], PACK - 1], sums[:])
 
+        def quantise_quarter(quarter):
+            cols = slice(QUARTER * quarter, QUARTER * (quarter + 1))
+            values = z_in[1, 0][:, PACK * cols.start : PACK * cols.stop]
+            nc.vector.quantize_mx(z_c[1, 0][:, cols].bitcast(FP8X4), z_s[1, 0][:, cols], values)
+
+        quarters = [slice(QUARTER * quarter, QUARTER * (quarter + 1)) for quarter in range(2)]
         z_s[0, 0] = lay_at("z_s00", [P, BANK], U8, 24 * KIB)[:]
+        late = [lay_at("late%d" % n, [P, BANK], U8, WB_LAST_AT + BANK * n)[:] for n in range(5)]
+        z_s[1, 0], z_s[0, 1], z_s[1, 1], wb_s[2] = late[1:]
         quantise_z(0, 0)
-        first_half = add_last(0, 25 * KIB)
+        first_sums = add_last(quarters[0], "last0", 25 * KIB)
         quantise_wb(0, lay_at("wb_s0", [P, BANK], U8, 26 * KIB)[:])
-        lay_last(0, first_half, slice(0, QUARTER), nc.vector.tensor_copy)
-        second_half = add_last(1, 22 * KIB)
-        lay_last(0, first_half, slice(QUARTER, HALF), nc.scalar.copy)
-        fetch_words(1, 3, backs[3])
-        last_stages.append(lay_at("wb_stage12", [P, PACK * WB_PIECE], BF16, 20 * KIB))
-        round_wb(1, 2, last_stages[1][:])
-        for unit in range(3):
-            spend_pass(unit, 0)
-        for unit in range(2):
-            load_pass(unit, 0)
-        z_s[1, 0] = keep("z_s10", [P, BANK], U8)[:]
-        z_s[1, 1] = keep("z_s11", [P, BANK], U8)[:]
-        quantise_z(1, 0)
-        quantise_wb(1, lay_at("wb_s1", [P, BANK], U8, 25 * KIB)[:])
-        late_s = lay_at("late_s", [P, 2 * BANK], U8, 29 * KIB)
-        lay_last(1, second_half, slice(0, HALF), nc.vector.tensor_copy)
-        z_s[0, 1], wb_s[2] = late_s[:, 0:BANK], late_s[:, BANK : 2 * BANK]
+        lay_last(quarters[0], first_sums, nc.vector.tensor_copy)
+        second_sums = add_last(quarters[1], "last1", WB_LAST_AT + 5 * BANK)
+        quantise_quarter(0)
+        spend_pass(0, 0)
+        for b in range(2):
+            load_pass(0, b)
+        load_pass(1, 0)
+        spend_pass(1, 0)
+        spend_pass(2, 0)
+        lay_last(quarters[1], second_sums, nc.scalar.copy)
+        third_sums = add_last(slice(HALF, T2), "last2", WB_LAST_AT + 6 * BANK)
+        quantise_wb(1, late[0])
+        quantise_quarter(1)
+        lay_last(slice(HALF, T2), third_sums, nc.vector.tensor_copy)
         quantise_z(0, 1)
         quantise_z(1, 1)
-        for b, stage in enumerate(last_stages):
-            cols = slice(WB_PIECE * b, WB_PIECE * (b + 1))
+        for stage, cols in zip(last_stages, (slice(0, 3 * P), slice(3 * P, 4 * P))):
             nc.vector.quantize_mx(wb_c[2][:, cols].bitcast(FP8X4), wb_s[2][:, cols], stage[:])
 
-        summed, squared = set(), set()
+        summed, squared = {0}, set()
         for unit in range(UNITS):
             for other in range(min(UNITS, unit + LOAD_AHEAD + 1)):
                 if other not in summed:
                     summed.add(other)
                     finish_sum(load_pass, loads, other)
             for other in range(min(UNITS, unit + 3)):
-                if other not in squared and (other <= unit + 1 or other in SQUARED_ON_VECTOR):
+                if other not in squared and (other <= unit + min(unit, 1) or other in SQUARED_ON_VECTOR):
                     squared.add(other)
                     square_load(other)
             damp(unit)

@@ -136,7 +136,6 @@ def tile_list_listing_budget_pacer_kernel(
         load_prior(7)
         load_wb(0, 2)
         load_prior(5)
-        load_wb(1, 2)
         load_prior(6)
         for quad in range(4):
             nc.sync.dma_start(
@@ -145,6 +144,7 @@ def tile_list_listing_budget_pacer_kernel(
             )
         for b in range(2):
             nc.sync.dma_start(wa_w[b][:], wa_words[b].bitcast(I32))
+        load_wb(1, 2)
 
         w1_c, w1_s = {}, {}
 

from contextlib import ExitStack

import concourse.mybir as mybir
from concourse.masks import make_identity

K, T, S, H, T2, N = 1024, 2048, 512, 1024, 1024, 768
FLOPS = 2 * K * H * S + 2 * 2 * H * N * T2

F32 = mybir.dt.float32
BF16 = mybir.dt.bfloat16
I32 = mybir.dt.int32
U32 = mybir.dt.uint32
U16 = mybir.dt.uint16
U8 = mybir.dt.uint8
FP8X4 = mybir.dt.float8_e4m3fn_x4
FP4X4 = mybir.dt.float4_e2m1fn_x4
MULT = mybir.AluOpType.mult
ADD = mybir.AluOpType.add
ACT = mybir.ActivationFunctionType

P = 128
PACK = 4
KP = P * PACK
BANK = 512
QUARTER = T2 // 4
HALF = T2 // 2
WB_PIECE = 256
UNITS = (N // P) * (T2 // BANK)
PAGES = 4
KIB = 1024
WB_LAST_AT = 28 * KIB
WORK_TAGS = ("w1_raw00", "w1_raw10", "w1_raw01", "wb_raw00", "tab_w0", "tab_w1")
RES_TAGS = ["prior%d" % s for s in (0, 1, 2, 3, 6, 7, 4, 5)] + ["h0", "h1", "h2", "wb_raw02"]
SET_X, SET_Y = (2, 3, 4, 5), (0, 1, 6, 7)
ALTERNATE_FROM = 5
SQUARED_ON_VECTOR = range(ALTERNATE_FROM, UNITS, 2)
ON_GPSIMD = [unit for unit in range(UNITS - 2) if unit not in SQUARED_ON_VECTOR]
LOAD_AHEAD = 3
LOAD_BANKS = (6, 7, 4, 5)
SPEND_BANKS = (0, 1, 3, 2)
UNIT_PLACES = [[(nt, QUARTER * q, QUARTER) for nt in range(2)] for q in range(2)] + [
    [(nt, HALF * hf, BANK)] for hf, nt in ((0, 2), (0, 3), (1, 0), (1, 1), (1, 2), (1, 3), (0, 4), (0, 5), (1, 4), (1, 5))
]


def tile_list_listing_budget_pacer_kernel(
    tc, tab_words, tab_scales, offs, w1, wgs, offs2, prior, wa_words, wa_scales, wb, out
):
    nc = tc.nc
    with ExitStack() as ctx:
        held = ctx.enter_context(tc.tile_pool(name="held", bufs=1))
        shared = ctx.enter_context(tc.tile_pool(name="shared", bufs=1))
        psum = ctx.enter_context(tc.psum_pool(name="psum", bufs=1))

        def keep(name, shape, dtype, after=None):
            return held.tile(shape, dtype, name=name, tag=after or name, align_bytes=64)

        def lay_at(name, shape, dtype, offset):
            return shared.tile(shape, dtype, name=name, offset=offset, align_bytes=64)

        def bank(number):
            return psum.tile([P, BANK], F32, name="bank%d" % number)

        idx = held.tile([P, S // 16], U16, name="idx")
        idx2 = held.tile([P, S // 16], U16, name="idx2")
        ident = keep("ident", [P, P], F32)
        tab_w = [keep("tab_w%d" % a, [P, T], I32) for a in range(2)]
        tab_s = keep("tab_s", [P, T // 4], I32)
        wa_s = keep("wa_s", [P, 2, N // 4], I32)
        wa_w = [keep("wa_w%d" % b, [P, 2 * N // 4], I32) for b in range(2)]
        wgs_sb = keep("wgs_sb", [P, S], F32)
        pages = [keep("page%d" % e, [P, T2], F32) for e in range(PAGES)]
        prior_sb = [keep("prior%d" % s, [P, T2], F32) for s in range(H // P)]
        wb_raw = {}

        nc.vector.memset(tab_s[:], 0)
        nc.vector.memset(wa_s[:], 0)
        for page in pages:
            nc.vector.memset(page[:], 0.0)
        make_identity(nc, ident[:])
        ones = keep("ones", [P, 1], F32)
        nc.scalar.activation(ones[:], pages[0][:, 0:1], ACT.Abs_reciprocal_sqrt, bias=1.0)

        w1_raw = {}

        def load_w1(a, b):
            if (a, b) == (1, 1):
                w1_raw[a, b] = lay_at("w1_last", [P, PACK, KP], F32, 0)
            else:
                w1_raw[a, b] = keep("w1_raw%d%d" % (a, b), [P, PACK, KP], F32)
            part = w1[KP * a : KP * (a + 1), KP * b : KP * (b + 1)]
            nc.sync.dma_start(w1_raw[a, b][:], part.rearrange("(p j) c -> p j c", j=PACK))

        def load_prior(s):
            b, i = divmod(s, PACK)
            part = prior[KP * b : KP * (b + 1), :].rearrange("(p i) m -> p i m", i=PACK)
            nc.sync.dma_start(prior_sb[s][:], part[:, i, :])

        def load_wb(b, piece):
            if (b, piece) == (1, 0):
                wb_raw[b, piece] = lay_at("wb_raw10", [P, PACK, WB_PIECE], F32, 18 * KIB)
            elif (b, piece) == (1, 2):
                wb_raw[b, piece] = lay_at("wb_raw12", [P, PACK, WB_PIECE], F32, WB_LAST_AT)
            else:
                wb_raw[b, piece] = keep("wb_raw%d%d" % (b, piece), [P, PACK, WB_PIECE], F32)
            part = wb[KP * b : KP * (b + 1), WB_PIECE * piece : WB_PIECE * (piece + 1)]
            nc.sync.dma_start(wb_raw[b, piece][:], part.rearrange("(p j) c -> p j c", j=PACK))

        def load_scale_rows(row):
            for a in range(2):
                rows = tab_scales[a].bitcast(I32).rearrange("(q r) w -> r q w", r=4)
                nc.sync.dma_start(tab_s[4 * a + row : P : 32, :], rows[row])

        load_w1(0, 0)
        load_scale_rows(0)
        load_scale_rows(1)
        load_w1(1, 0)
        load_scale_rows(2)
        load_scale_rows(3)
        nc.sync.dma_start(idx[:], offs)
        for a in range(2):
            nc.sync.dma_start(tab_w[a][:], tab_words[a].rearrange("p t i -> p (t i)").bitcast(I32))
        nc.sync.dma_start(wgs_sb[:], wgs)
        nc.sync.dma_start(idx2[:], offs2)
        load_w1(0, 1)
        load_w1(1, 1)
        load_prior(0)
        load_wb(0, 0)
        load_prior(1)
        load_prior(2)
        load_wb(1, 0)
        load_wb(0, 1)
        load_prior(3)
        load_prior(4)
        load_wb(1, 1)
        load_prior(7)
        load_wb(0, 2)
        load_prior(5)
        load_prior(6)
        for quad in range(4):
            nc.sync.dma_start(
                wa_s[32 * quad : 32 * quad + 4, :, :],
                wa_scales[:, 4 * quad : 4 * quad + 4, :].bitcast(I32).rearrange("b r c -> r b c"),
            )
        for b in range(2):
            nc.sync.dma_start(wa_w[b][:], wa_words[b].bitcast(I32))
        load_wb(1, 2)

        w1_c, w1_s = {}, {}

        def quantise_w1(passes, b, scales_after=None, copy=nc.scalar.copy):
            name = "%d%d" % (passes[0], b)
            stage = keep("w1_stage" + name, [P, len(passes) * PACK * KP], BF16)
            codes = keep("w1_c" + name, [P, len(passes) * KP], U32)
            scales = keep("w1_s" + name, [P, len(passes) * KP], U8, after=scales_after)
            for n, a in enumerate(passes):
                copy(
                    stage[:, PACK * KP * n : PACK * KP * (n + 1)].rearrange("p (i c j) -> p c j i", i=PACK, j=PACK),
                    w1_raw[a, b][:].rearrange("p j (c i) -> p c j i", i=PACK),
                )
                w1_c[a, b], w1_s[a, b] = codes[:, KP * n : KP * (n + 1)], scales[:, KP * n : KP * (n + 1)]
            nc.vector.quantize_mx(codes[:].bitcast(FP8X4), scales[:], stage[:])

        wb_c = [keep("wb_c%d" % piece, [P, 2 * WB_PIECE], U32) for piece in range(N // WB_PIECE)]
        wb_stage = [keep("wb_stage%d" % piece, [P, 2, PACK * WB_PIECE], BF16) for piece in range(2)]
        wb_s = {}

        def round_wb(b, piece, stage):
            nc.scalar.copy(
                stage.rearrange("p (c n j) -> p c j n", n=4, j=PACK),
                wb_raw[b, piece][:].rearrange("p j (c n) -> p c j n", n=4),
            )

        def round_half(part, stage):
            nc.scalar.copy(
                stage.rearrange("p (c n j) -> p c j n", n=4, j=PACK),
                wb_raw[1, 2][:, :, P * part : P * (part + 1)].rearrange("p j (c n) -> p c j n", n=4),
            )

        def quantise_wb(piece, scales):
            wb_s[piece] = scales
            nc.vector.quantize_mx(
                wb_c[piece][:].bitcast(FP8X4), scales, wb_stage[piece][:].rearrange("p b c -> p (b c)")
            )

        v_w, h_ps, h_sb = {}, {}, {}
        first, later = slice(0, P), slice(P, S)

        def make_h(s, number, entries, passes):
            b, i = divmod(s, PACK)
            cols = slice(P * i, P * (i + 1))
            h_ps[s, entries.start] = bank(number)
            runs = (slice(P, 2 * P), slice(2 * P, S)) if entries == later else (entries,)
            for a in passes:
                for run in runs:
                    nc.tensor.matmul_mx(
                        h_ps[s, entries.start][:, run],
                        lhsT=w1_c[a, b][:, cols].bitcast(FP8X4),
                        lhsT_scale=w1_s[a, b][:, cols],
                        rhs=v_w[a][:, run].bitcast(FP8X4),
                        rhs_scale=v_s[4 * a : P, run],
                        start=(a == passes[0] and run is runs[0]),
                        stop=(a == passes[1] and run is runs[-1]),
                    )

        def fetch_h(s, entries):
            if s not in h_sb:
                h_sb[s] = keep("h%d" % s, [P, S], F32)[:]
            nc.scalar.copy(h_sb[s][:, entries], h_ps[s, entries.start][:, entries])

        def place(s, entries):
            offsets = idx2[:, entries.start // 16 : entries.stop // 16]
            nc.vector.tensor_tensor(pages[s % PAGES][:].indirect(offsets), h_sb[s][:, entries], wgs_sb[:, entries], MULT)

        z_t = {}

        def new_words(pair, name, offset):
            words = lay_at(name, [P, 4 * BANK], BF16, offset)
            for quarter in range(4):
                z_t[pair, quarter] = words[:, BANK * quarter : BANK * (quarter + 1)]
            return words

        def add_turned(src, blocks, regions, first=False, last=False):
            seen = [regions(block)[0] for block in blocks]
            for n, block in enumerate(blocks):
                sums, region = regions(block)
                nc.tensor.matmul(
                    sums[:, P * region : P * (region + 1)],
                    lhsT=src[:, P * block : P * (block + 1)],
                    rhs=ident[:],
                    is_transpose=True,
                    start=first and not any(sums is other for other in seen[:n]),
                    stop=last and not any(sums is other for other in seen[n + 1 :]),
                )

        def pair_regions(banks, e):
            return lambda block: (banks[block // 2], 2 * (block % 2) + e)

        def open_pair(s, numbers):
            banks = [bank(number) for number in numbers]
            add_turned(prior_sb[s], range(8), pair_regions(banks, 0), first=True)
            return banks

        def close_pair(s, banks, sources):
            for quarter in range(4):
                for src in sources:
                    add_turned(src, (2 * quarter, 2 * quarter + 1), pair_regions(banks, 1), last=src is sources[-1])
                nc.scalar.copy(
                    z_t[s % PACK // 2, quarter].rearrange("m (l p e) -> m l p e", l=2, e=2),
                    banks[quarter][:].rearrange("m (l e p) -> m l p e", l=2, e=2),
                )

        z_c = {(b, hf): keep("z_c%d%d" % (b, hf), [P, BANK], U32) for b in range(2) for hf in range(2)}
        z_s, z_in = {}, {}

        def turn_words(quarter, back, pair):
            words = z_t[pair, quarter].bitcast(F32)
            for l in range(2):
                nc.tensor.transpose(
                    back[:, P * (2 * pair + l) : P * (2 * pair + l + 1)], words[:, P * l : P * (l + 1)], ident[:]
                )
            return back

        def fetch_words(b, quarter, back):
            hf, part = divmod(quarter, 2)
            if (b, hf) not in z_in:
                z_in[b, hf] = keep("z_in%d%d" % (b, hf), [P, PACK * HALF], BF16)
            nc.scalar.copy(
                z_in[b, hf][:].bitcast(F32)[:, BANK * part : BANK * (part + 1)].rearrange("p (m u) -> p m u", u=2),
                back[:].rearrange("p (u m) -> p m u", u=2),
            )

        def quantise_z(b, hf):
            nc.vector.quantize_mx(z_c[b, hf][:].bitcast(FP8X4), z_s[b, hf], z_in[b, hf][:])

        work, loads, spends = {}, {}, {}

        def load_pass(unit, b):
            first = unit not in loads
            if first:
                loads[unit] = bank(LOAD_BANKS[unit % 4])
            for n, (nt, start, width) in enumerate(UNIT_PLACES[unit]):
                piece, part = divmod(nt, WB_PIECE // P)
                cols = slice(WB_PIECE * b + P * part, WB_PIECE * b + P * (part + 1))
                hf, m = divmod(start, HALF)
                nc.tensor.matmul_mx(
                    loads[unit][:, width * n : width * (n + 1)],
                    lhsT=wb_c[piece][:, cols].bitcast(FP8X4),
                    lhsT_scale=wb_s[piece][:, cols],
                    rhs=z_c[b, hf][:, m : m + width].bitcast(FP8X4),
                    rhs_scale=z_s[b, hf][:, m : m + width],
                    start=first and n == 0,
                    stop=not first and width * (n + 1) == BANK,
                )

        def spend_pass(unit, b):
            first = unit not in spends
            if first:
                spends[unit] = bank(SPEND_BANKS[unit % 4])
            for n, (nt, start, width) in enumerate(UNIT_PLACES[unit]):
                hf, m = divmod(start, HALF)
                nc.tensor.matmul_mx(
                    spends[unit][:, width * n : width * (n + 1)],
                    lhsT=wa_w[b][:].bitcast(U8)[:, 2 * P * nt : 2 * P * (nt + 1)].bitcast(FP4X4),
                    lhsT_scale=wa_s[:, b, :].bitcast(U8)[:, P * nt : P * (nt + 1)],
                    rhs=z_c[b, hf][:, m : m + width].bitcast(FP8X4),
                    rhs_scale=z_s[b, hf][:, m : m + width],
                    start=first and n == 0,
                    stop=not first and width * (n + 1) == BANK,
                )

        def scratch(unit, row):
            if unit // 2 not in work:
                work[unit // 2] = keep("work%d" % unit, [P, 2, 2 * BANK], F32, after=WORK_TAGS[unit // 2])
            return work[unit // 2][:, row, BANK * (unit % 2) : BANK * (unit % 2 + 1)]

        def squared_load(unit):
            return scratch(0 if unit == 1 else unit, 0)

        def product(unit):
            return scratch(1 - unit if unit < 2 else unit, 0)

        def finish_sum(one_pass, started, unit):
            for b in (1,) if unit in started else (1, 0):
                one_pass(unit, b)

        def square_load(unit):
            if unit in SQUARED_ON_VECTOR:
                nc.vector.tensor_copy(scratch(unit, 1), loads[unit][:])
                nc.vector.tensor_tensor(scratch(unit, 0), loads[unit][:], scratch(unit, 1), MULT)
            else:
                nc.scalar.activation(squared_load(unit), loads[unit][:], ACT.Square)

        def damp(unit):
            nc.scalar.activation(scratch(unit, 1), squared_load(unit), ACT.Abs_reciprocal_sqrt, bias=ones[:])

        def result(unit):
            return keep("res%d" % unit, [P, BANK], F32, after=RES_TAGS[unit])

        def store(unit, res, cols):
            nt, start, width = UNIT_PLACES[unit][0]
            if width == BANK:
                nc.sync.dma_start(out[P * nt : P * (nt + 1), start : start + BANK][:, cols], res[:, cols])
            else:
                rows = out[P * nt : P * (nt + 2), start : start + width].rearrange("(t p) m -> p t m", p=P)
                nc.sync.dma_start(rows, res[:].rearrange("p (t m) -> p t m", t=2))

        def two_products(unit, second):
            finish_sum(spend_pass, spends, unit)
            nc.vector.tensor_tensor(product(unit), spends[unit][:], scratch(unit, 1), MULT)
            res = result(unit)
            second.tensor_tensor(res[:], product(unit), scratch(unit, 1), MULT)
            store(unit, res, slice(0, BANK))

        def one_product(unit, pieces):
            res = result(unit)
            finish_sum(spend_pass, spends, unit)
            for piece in range(pieces):
                cols = slice(BANK // pieces * piece, BANK // pieces * (piece + 1))
                nc.scalar.activation(scratch(unit, 0)[:, cols], scratch(unit, 1)[:, cols], ACT.Square)
                nc.vector.tensor_tensor(res[:, cols], spends[unit][:, cols], scratch(unit, 0)[:, cols], MULT)
                store(unit, res, cols)

        whole = slice(0, S)

        v_s = keep("v_s", [P, S], U8)
        nc.vector.tensor_copy(v_s[:], tab_s[:].bitcast(U8).indirect(idx[:]))
        quantise_w1((0,), 0, copy=nc.vector.tensor_copy)
        v_w[0] = keep("v_w0", [P, S], U32, after="w1_stage00")
        nc.vector.tensor_copy(v_w[0][:], tab_w[0][:].bitcast(U32).indirect(idx[:]))
        quantise_w1((1,), 0, scales_after="tab_w0")
        v_w[1] = keep("v_w1", [P, S], U32)
        for part in (first, later):
            offsets = idx[:, part.start // 16 : part.stop // 16]
            nc.vector.tensor_copy(v_w[1][:, part], tab_w[1][:].bitcast(U32).indirect(offsets))
        pieces = [(0, first), (1, first), (0, later), (1, later)]
        for number, (s, entries) in enumerate(pieces):
            make_h(s, number, entries, (0, 1))
            fetch_h(s, entries)
            place(s, entries)
        for s, number in ((2, 6), (3, 7)):
            make_h(s, number, whole, (1, 0))
        fetch_h(2, whole)
        place(2, whole)

        banks = open_pair(0, SET_X)
        add_turned(pages[0], range(8), pair_regions(banks, 0))
        quantise_w1((0, 1), 1)
        h_sb[3] = lay_at("h3", [P, S], F32, 0)[:]
        fetch_h(3, whole)
        place(3, whole)
        round_wb(0, 0, wb_stage[0][:, 0, :])
        new_words(0, "words01", 4 * KIB)
        close_pair(0, banks, (prior_sb[1], pages[1]))
        banks = open_pair(2, SET_Y)
        add_turned(pages[2], range(8), pair_regions(banks, 0))
        round_wb(1, 0, wb_stage[0][:, 1, :])
        round_wb(0, 1, wb_stage[1][:, 0, :])
        h_late = lay_at("h_late", [P, PACK, S], F32, 12 * KIB)
        for s, number in zip(range(PACK, 2 * PACK), SET_X):
            make_h(s, number, whole, (1, 0))
            h_sb[s] = h_late[:, s - PACK, :]
            fetch_h(s, whole)
        add_turned(prior_sb[3], range(8), pair_regions(banks, 1))
        place(4, whole)
        second_words = new_words(1, "words23", 20 * KIB)
        close_pair(2, banks, (pages[3],))
        place(5, whole)
        backs = [turn_words(quarter, bank(number), 0) for quarter, number in enumerate(SET_X)]
        for quarter in range(4):
            fetch_words(0, quarter, turn_words(quarter, backs[quarter], 1))

        banks = open_pair(4, SET_Y)
        add_turned(prior_sb[5], range(8), pair_regions(banks, 1))
        add_turned(pages[4 % PAGES], range(8), pair_regions(banks, 0))
        round_wb(1, 1, wb_stage[1][:, 1, :])
        last_stages = [keep("wb_stage2", [P, 3 * PACK * P], BF16)]
        round_wb(0, 2, last_stages[0][:, 0 : PACK * WB_PIECE])
        new_words(0, "words45", 24 * KIB)
        close_pair(4, banks, (pages[5 % PAGES],))
        round_half(0, last_stages[0][:, PACK * WB_PIECE :])
        place(6, whole)
        place(7, whole)
        sums = [bank(number) for number in SET_X[:2]]
        add_turned(prior_sb[6], range(8), lambda block: (sums[block // 4], block % 4), first=True)
        backs = [turn_words(quarter, bank(number), 0) for quarter, number in enumerate(SET_Y)]
        add_turned(pages[6 % PAGES], range(8), lambda block: (sums[block // 4], block % 4), last=True)
        for hf in range(2):
            words = second_words[:, 2 * BANK * hf : 2 * BANK * (hf + 1)].rearrange("m (c e) -> m c e", e=2)
            nc.scalar.copy(words[:, :, 0], sums[hf][:])
            for quarter in (2 * hf, 2 * hf + 1):
                turn_words(quarter, backs[quarter], 1)
        for quarter in range(2):
            fetch_words(1, quarter, backs[quarter])
        last_stages.append(lay_at("wb_stage12", [P, PACK * P], BF16, 20 * KIB))
        round_half(1, last_stages[1][:])
        for quarter in range(2, 4):
            fetch_words(1, quarter, backs[quarter])

        def add_last(cols, name, offset):
            sums = lay_at(name, [P, cols.stop - cols.start], BF16, offset)
            nc.vector.tensor_tensor(sums[:], pages[7 % PAGES][:, cols], prior_sb[7][:, cols], ADD)
            return sums

        def lay_last(cols, sums, copy):
            hf, m = divmod(cols.start, HALF)
            copy(z_in[1, hf][:].rearrange("p (m i) -> p m i", i=PACK)[:, m : m + sums.shape[1], PACK - 1], sums[:])

        def quantise_quarter(quarter):
            cols = slice(QUARTER * quarter, QUARTER * (quarter + 1))
            values = z_in[1, 0][:, PACK * cols.start : PACK * cols.stop]
            nc.vector.quantize_mx(z_c[1, 0][:, cols].bitcast(FP8X4), z_s[1, 0][:, cols], values)

        quarters = [slice(QUARTER * quarter, QUARTER * (quarter + 1)) for quarter in range(2)]
        z_s[0, 0] = lay_at("z_s00", [P, BANK], U8, 24 * KIB)[:]
        late = [lay_at("late%d" % n, [P, BANK], U8, WB_LAST_AT + BANK * n)[:] for n in range(5)]
        z_s[1, 0], z_s[0, 1], z_s[1, 1], wb_s[2] = late[1:]
        quantise_z(0, 0)
        first_sums = add_last(quarters[0], "last0", 25 * KIB)
        quantise_wb(0, lay_at("wb_s0", [P, BANK], U8, 26 * KIB)[:])
        lay_last(quarters[0], first_sums, nc.vector.tensor_copy)
        second_sums = add_last(quarters[1], "last1", WB_LAST_AT + 5 * BANK)
        quantise_quarter(0)
        spend_pass(0, 0)
        for b in range(2):
            load_pass(0, b)
        load_pass(1, 0)
        spend_pass(1, 0)
        spend_pass(2, 0)
        lay_last(quarters[1], second_sums, nc.scalar.copy)
        third_sums = add_last(slice(HALF, T2), "last2", WB_LAST_AT + 6 * BANK)
        quantise_wb(1, late[0])
        quantise_quarter(1)
        lay_last(slice(HALF, T2), third_sums, nc.vector.tensor_copy)
        quantise_z(0, 1)
        quantise_z(1, 1)
        for stage, cols in zip(last_stages, (slice(0, 3 * P), slice(3 * P, 4 * P))):
            nc.vector.quantize_mx(wb_c[2][:, cols].bitcast(FP8X4), wb_s[2][:, cols], stage[:])

        summed, squared = {0}, set()
        for unit in range(UNITS):
            for other in range(min(UNITS, unit + LOAD_AHEAD + 1)):
                if other not in summed:
                    summed.add(other)
                    finish_sum(load_pass, loads, other)
            for other in range(min(UNITS, unit + 3)):
                if other not in squared and (other <= unit + min(unit, 1) or other in SQUARED_ON_VECTOR):
                    squared.add(other)
                    square_load(other)
            damp(unit)
            if unit not in SQUARED_ON_VECTOR:
                two_products(unit, nc.gpsimd if unit in ON_GPSIMD else nc.vector)
                if unit - 1 in SQUARED_ON_VECTOR and unit in ON_GPSIMD:
                    one_product(unit - 1, 1)
            elif unit + 1 not in ON_GPSIMD:
                one_product(unit, 2 if unit == UNITS - 1 else 1)
